import numpy as np, ml_dtypes
CORES = [36,164,52,180,100,228,116,244]
N = 8
BF = ml_dtypes.bfloat16
V, HP, Y, L, A, R, LM, C, RO, H = 3040, 8192, 512, 16, 4, 8, 20, 640, 3, 9
Q, TOP = L * A * R, 2 ** 20
def chain(rng, brk, gone, uneven):
    s = (N, 8, 16, V); i = np.arange(V)
    last = np.maximum.accumulate(np.where(rng.random(s) < brk, i, 0), axis=-1)
    off = np.exp2(19.8 * rng.random(s)).astype(np.int64) if uneven else rng.integers(1, TOP - V, s)
    away = rng.random(s) < gone
    p = np.where(away, 0, np.take_along_axis(off, last, -1) + i)
    one = rng.random(s) < 0.3; one[..., 0] = False; one[..., 1:] &= away[..., :-1] & ~away[..., 1:]
    return np.where(one, 1, p)
def place(p, order):
    inv = np.argsort(order, axis=-1)
    return np.stack([p[:, g][:, :, inv[g]] for g in range(8)], axis=1)
def names_of(rng, order, jump, power):
    i = np.arange(HP); last = np.maximum.accumulate(np.where(rng.random((N, 8, HP)) < jump, i, 0), axis=-1)
    first = (V * rng.random((N, 8, HP)) ** power).astype(np.int64)
    c = (np.take_along_axis(first, last, -1) + i - last) % V
    return np.take_along_axis(np.broadcast_to(order, (N, 8, V)), c, -1)
def parts(rng, uneven=False):
    order = np.argsort(rng.random((8, V)), axis=-1)
    brk = rng.choice(np.array([0.02, 0.1, 0.3]), (N, 8, 16, 1)); gone = rng.choice(np.array([0.05, 0.2, 0.35]), (N, 8, 16, 1))
    top = rng.integers(LM // 2, LM + 1, (N, 8, 1)); top[0] = LM
    d = {"wpos": place(chain(rng, brk, gone, uneven), order), "heap": names_of(rng, order, 0.25, 3 if uneven else 1),
         "gst": rng.integers(0, HP - LM + 1, (N, 8, Y)), "gln": ((top + 1) * rng.random((N, 8, Y))).astype(np.int64),
         "sens": rng.integers(0, Y, (N, 8, A * Y)), "rel": rng.integers(0, N * Y, (N, 8, R * Y)), "nxt": rng.integers(0, Y, (N, 8, Y)), "cur": rng.integers(0, Y, (N, 8, L))}
    return d, order
def pack(d):
    r = {"wpos": np.ascontiguousarray(d["wpos"].reshape(N, 128, V)).astype(np.int32)}
    for k in ("heap", "gst", "gln", "sens", "rel", "nxt", "cur"): r[k] = np.ascontiguousarray(d[k]).astype(np.int32)
    return r
def some(rng, ln, n, k):
    return rng.choice(np.flatnonzero(ln == n), k)
def plant(rng, d, g, w):
    m, n = w.shape
    p = rng.integers(1, TOP - n + 1, (N, 16, m, 1)) + np.arange(n)
    d["wpos"][:, g][:, :, w.reshape(-1)] = p.reshape(N, 16, m * n)
    s = rng.integers(0, HP - LM - m * n + 1, (N, 1)) + n * np.arange(m)
    d["heap"][np.arange(N)[:, None], g, s[:, :1] + np.arange(m * n)] = w.reshape(-1)
    return s
def ask_few(rng, d, g, w, heads):
    m, n = len(w), len(heads); s = plant(rng, d, g, w)
    t = rng.permutation(Y)[:2 * m + 1]; u = rng.permutation(Y)[:n + 1]
    for k, ln in ((t[:m], 3), (t[m:2 * m], 2)):
        d["gst"][:, g][:, k] = s; d["gln"][:, g][:, k] = ln
    d["gln"][:, g, t[2 * m]] = 0
    for a in range(N):
        o = ((a + 1) % N) * Y; se = d["sens"][a, g].reshape(Y, A); re_ = d["rel"][a, g].reshape(Y, R)
        se[heads] = u[n]; se[heads, rng.integers(0, A, n)] = u[:n]; re_[u[n]] = o + t[2 * m]
        for i in range(n): re_[u[i]] = o + t[(np.arange(R) + i) % m + m * (a & 1)]
        d["nxt"][a, g, u[:n]] = np.roll(heads, -1); d["cur"][a, g] = heads[(np.arange(L) + a) % n]
    return u[:n], t
def setup_inputs(rng):
    return pack(parts(rng)[0])
def setup_inputs_spread(rng):
    d, order = parts(rng, True)
    e = rng.choice(np.array([0.3, 1.0, 4.0]), (N, 8, 1))
    d["gln"] = ((LM + 1) * rng.random((N, 8, Y)) ** e).astype(np.int64)
    d["gst"] = ((HP - LM + 1) * rng.random((N, 8, Y)) ** 2).astype(np.int64)
    q = ((N * rng.random((N, 8, R * Y)) ** 2).astype(np.int64) + np.arange(N)[:, None, None]) % N
    d["rel"] = q * Y + (Y * rng.random((N, 8, R * Y)) ** 1.5).astype(np.int64)
    d["sens"] = (Y * rng.random((N, 8, A * Y)) ** 2).astype(np.int64); d["cur"] = (Y * rng.random((N, 8, L)) ** 2).astype(np.int64)
    d["nxt"] = (Y * rng.random((N, 8, Y)) ** 0.5).astype(np.int64)
    for k in ("sens", "cur", "nxt"): d[k] = np.minimum(d[k], Y - 1)
    d["gln"] = np.minimum(d["gln"], LM); d["gst"] = np.minimum(d["gst"], HP - LM)
    return pack(d)
def setup_inputs_ends(rng):
    d, order = parts(rng)
    for k, hi in (("heap", V - 1), ("gst", HP - LM), ("sens", Y - 1), ("rel", N * Y - 1), ("nxt", Y - 1), ("cur", Y - 1), ("wpos", TOP - 1)):
        m = rng.random(d[k].shape); d[k] = np.where(m < 0.38, 0, np.where(m < 0.76, hi, d[k]))
    d["gln"] = LM * rng.integers(0, 2, (N, 8, Y))
    for g in range(8):
        o = rng.permutation(np.arange(1, V - 1)); c0 = np.concatenate([np.array([0]), o[:LM - 1]]); c1 = np.concatenate([o[LM:2 * LM - 1], np.array([V - 1])])
        if g == 3: c0 = np.roll(c0, -1)
        d["heap"][:, g, :LM] = c0; d["heap"][:, g, HP - LM:] = c1
        w = d["wpos"][:, g]; w[:, :, c0] = 1 + np.arange(LM); w[:, :, c1] = TOP - LM + np.arange(LM)
        if g < 3: w[:, g::3, c1[LM // 2]] = 0
        if g == 4 or g == 5:
            n = H if g == 4 else H - 1
            w[:, n:, c0] = TOP - 1; w[:, n:, c1] = TOP - 1
        if g == 6: w[:, 3, 0] = 0
    d["gst"][:, :, 0] = 0; d["gst"][:, :, Y - 1] = HP - LM; d["gln"][:, :, Y - 1] = LM; d["gln"][:, ::2, 0] = LM; d["gln"][:, 1::2, 0] = 0
    n = C // (A * R * LM)
    d["cur"][:, 7] = 0; d["cur"][:, 7, L - n:] = Y - 1; d["sens"][:, 7, :A] = 0; d["sens"][:, 7, (Y - 1) * A:] = Y - 1
    d["rel"][:, 7, :R] = 0; d["rel"][:, 7, (Y - 1) * R:] = N * Y - 1; d["nxt"][:, 7, 0] = Y - 1; d["nxt"][:, 7, Y - 1] = rng.choice(np.array([0, Y - 1]), N)
    d["cur"][:, 6, 0] = Y - 1; d["sens"][:, 6, (Y - 1) * A:] = Y - 1; d["sens"][:, 6, (Y - 1) * A] = Y - 2
    d["rel"][:, 6, (Y - 2) * R:] = N * Y - 1; d["rel"][:, 6, (Y - 2) * R] = 0; d["nxt"][:, 6, Y - 1] = 0; d["nxt"][:, 6, Y - 2] = Y - 1
    return pack(d)
def setup_inputs_corners(rng):
    d, order = parts(rng)
    d["gln"] = np.array([0, 1, LM - 1, LM, LM, LM, LM, 2])[np.argsort(rng.random((N, 8, Y)), axis=-1) & 7]
    d["gst"][:, 3] = rng.choice(np.array([0, 1, HP - LM - 1, HP - LM]), (N, Y))
    m = C // LM
    for a in range(N):
        for g in range(8):
            got = []
            for o in range(N):
                ln = d["gln"][o, g]; case = (o + 3 * a + g) % 6
                want = ([(LM, m)], [(LM, m - 1), (LM - 1, 1)], [(LM, m), (1, 1)], [(LM, m + m // 2)], [(0, 2)], [(1, m)])[case]
                for n, k in want: got.append(o * Y + some(rng, ln, n, k))
            have = np.concatenate(got)[:Q]
            have = rng.permutation(np.concatenate([have, a * Y + some(rng, d["gln"][a, g], 0, Q - len(have))]))
            w = rng.permutation(Y)[:L]; s = rng.permutation(Y)[:L * A]
            d["cur"][a, g] = w; d["sens"][a, g].reshape(Y, A)[w] = s.reshape(L, A); d["rel"][a, g].reshape(Y, R)[s] = have.reshape(L * A, R)
            if g % 4 == 1: d["nxt"][a, g, s] = np.repeat(w, A)
            if g % 4 == 2: d["nxt"][a, g] = rng.choice(np.array([0, Y - 1]), Y)
    return pack(d)
def setup_inputs_crowd(rng):
    d, order = parts(rng)
    n = np.array([16, 15, H, H - 1, 16, H + 1, H, H - 1])[(np.arange(8)[None, :] + np.arange(N)[:, None]) & 7]
    turn = (np.arange(16)[None, None, :] + rng.integers(0, 16, (N, 8, 1))) & 15
    off = rng.integers(1, TOP - V, (N, 8, 16, 1)); i = np.arange(V)
    d["wpos"] = place(np.where((turn < n[:, :, None])[..., None], off + i, (off + 257 * i) & (TOP - 1)), order)
    d["cur"][:, ::2] = rng.integers(0, Y, (N, 4, 1)); d["cur"][:, 1::4, :L - 1] = rng.integers(0, Y, (N, 2, 1))
    few = rng.integers(0, Y, (N, 2, 3)); d["cur"][:, 3::4] = np.take_along_axis(few, rng.integers(0, 3, (N, 2, L)), -1)
    d["gln"][:, 4:] = np.minimum(d["gln"][:, 4:], 4)
    d["rel"][:, 2] = np.arange(N)[:, None] * Y + rng.integers(0, Y, (N, R * Y)); d["rel"][:, 6] = (N - 1) * Y + rng.integers(0, Y, (N, R * Y))
    return pack(d)
def setup_inputs_calm(rng):
    d, order = parts(rng); gs = [int(x) for x in rng.permutation(8)[:4]]; c = rng.permutation(np.arange(4, V - 4))
    g = gs[0]; h = rng.permutation(Y)[:2]
    u, t = ask_few(rng, d, g, c[None, :3], h)
    d["nxt"][:, g][:, u] = h; d["rel"][:, g, u[1] * R + R - 1] = ((np.arange(N) + 1) % N) * Y + t[2]
    d["cur"][:, g] = h[0]; d["cur"][1::2, g, L - 1] = h[1]
    ask_few(rng, d, gs[1], np.stack([c[3:7], np.arange(4), c[7:11]], axis=1), rng.permutation(4))
    ask_few(rng, d, gs[2], np.stack([c[11:15], V - 1 - np.arange(4), c[15:19]], axis=1), Y - 1 - rng.permutation(4))
    g = gs[3]; m = L * R; t = rng.permutation(Y)
    s = plant(rng, d, g, rng.permutation(V)[:2 * m].reshape(m, 2))
    d["gst"][:, g][:, t[:m]] = s; d["gln"][:, g] = 1; d["gln"][:, g][:, t[:m]] = 2
    for a in range(N):
        o = ((a + N - 1) % N) * Y; w = rng.permutation(Y)[:L]; u = rng.permutation(Y)[:L * A].reshape(L, A); v = rng.integers(0, A, L); v[L - 1] = A - 1
        d["sens"][a, g].reshape(Y, A)[w] = u; d["cur"][a, g] = w; d["nxt"][a, g, u] = w[:, None]
        rows = d["rel"][a, g].reshape(Y, R); rows[u] = o + t[rng.integers(m, Y, (L, A, R))]
        rows[u[np.arange(L), v]] = o + rng.permutation(t[:m]).reshape(L, R)
    return pack(d)
def check_inputs(d):
    bad = []
    for k, hi in (("wpos", 2 ** 20 - 1), ("heap", V - 1), ("gst", HP - LM), ("gln", LM), ("sens", Y - 1), ("rel", N * Y - 1), ("nxt", Y - 1), ("cur", Y - 1)):
        if np.min(d[k]) < 0 or np.max(d[k]) > hi: bad.append("range of " + k)
    return bad
def reference(wpos, heap, gst, gln, sens, rel, nxt, cur):
    P = np.array(wpos, dtype=np.int32).reshape(N, 8, 16, V); w = cur.astype(np.int64)
    yt = np.zeros((N, 8, RO, L, A), np.int64); yb = np.zeros((N, 8, RO, L, R), np.int64); yw = np.zeros((N, 8, RO, L), np.int64)
    gi = np.arange(8)[:, None]; e = np.arange(LM)[:, None]
    for rnd in range(RO):
        for a in range(N):
            s = np.take_along_axis(sens[a], (w[a][:, :, None] * A + np.arange(A)).reshape(8, L * A), 1).astype(np.int64)
            rq = np.take_along_axis(rel[a], (s[:, :, None] * R + np.arange(R)).reshape(8, Q), 1).astype(np.int64)
            q = rq // Y; t = rq - q * Y; ln = gln[q, gi, t].astype(np.int64); st = gst[q, gi, t].astype(np.int64)
            kept = np.zeros((8, Q), np.int64)
            for o in range(N):
                m = np.where(q == o, ln, 0); before = np.add.accumulate(m, axis=1) - m
                kept = kept + np.minimum(np.maximum(C - before, 0), m)
            word = heap[q[:, None, :], gi[:, :, None], st[:, None, :] + e]
            x = np.take_along_axis(P[a], word.reshape(8, 1, LM * Q), 2).reshape(8, 16, LM, Q)
            x = np.where((e < kept[:, None, :])[:, None], x, 0)
            more = np.zeros(x.shape, bool); more[:, :, 1:] = (x[:, :, 1:] == x[:, :, :-1] + 1) & (x[:, :, :-1] > 0)
            run = np.zeros((8, 16, Q), np.int64); score = np.zeros((8, 16, Q), np.int64)
            for i in range(LM):
                run = np.where(x[:, :, i] > 0, np.where(more[:, :, i], run, 0) + 1, 0)
                score = score + np.where(run > 0, 2 * run - 1, 0)
            tot = np.add.reduce(np.add.reduce(score, axis=1).reshape(8, L, A, R), axis=3)
            win = np.argmax(tot, axis=2)
            hot = np.add.reduce(more, axis=1, dtype=np.int64) >= H
            at = np.maximum.reduce(np.where(hot, e, -1), axis=1)
            b = np.where(at >= 0, np.take_along_axis(word, np.maximum(at, 0)[:, None, :], 1)[:, 0], -1).reshape(8, L, A, R)
            b = np.take_along_axis(b, win[:, :, None, None], 2)[:, :, 0]
            if rnd < RO - 1:
                for g in range(8):
                    c = b[g].reshape(-1); P[a, g][:, c[c >= 0]] = 0
            sw = np.take_along_axis(s.reshape(8, L, A), win[:, :, None], 2)[:, :, 0]
            w[a] = np.take_along_axis(nxt[a], sw, 1)
            yt[a, :, rnd] = tot; yb[a, :, rnd] = b; yw[a, :, rnd] = w[a]
    return {"yt": yt.reshape(N, 8, RO * L * A).astype(np.float32), "yb": yb.reshape(N, 8, RO * L * R).astype(np.float32), "yw": yw.reshape(N, 8, RO * L).astype(np.float32)}

@@ -1,0 +1,663 @@
+import numpy as np
+from concourse.bass import DstId, RemoteDMATransfer
+from concourse.mybir import AluOpType as A, AxisListType, ActivationFunctionType as F
+
+N, V, HP, C, RO = 8, 3040, 8192, 640, 3
+BIG = float(2 ** 60)
+SELF = N - 1
+GROUPS = [[0], [1, 2], [3, 4], [5, 6]]
+BATCH = [[0, 1, 2], [7], [3, 4, 5, 6]]
+ANSWERS = [[0], [7], [1, 2], [3, 4], [5, 6]]
+HEAP_ON_VECTOR = (2, 4, 6)
+SIGN_ON_VECTOR = ()
+EARLY = [1]
+GATE = 4
+T2_ON_SCALAR = 6
+ODD = 3072
+RING = 3
+f32, bf, i32, u16, f16 = "float32", "bfloat16", "int32", "uint16", "float16"
+SB = {
+    "wp": (V, i32), "B": (2 * ODD + 256, f32), "hb": (1536, bf), "HW": (2 * HP, bf), "sli": (280, f32), "R40": (280, f32),
+    "DQ": (512, f32), "DH": (256, f32), "acc": (8, f32), "S256": (128, f32), "nb": (8, f32),
+    "W0": (5632, bf), "W1": (5632, bf), "gi": (64, i32), "gf": (64, f32), "m1": (128, i32), "m2": (128, i32),
+    "m3": (256, f32), "msg": (64, u16), "Tc": (512, u16), "Ti": (512, i32), "Tj": (1024, i32), "Tl": (512, f16),
+    "off": (8, f32),
+    "Tb": (512, bf), "T1": (4096, bf), "T2": (4096, bf), "rn": (256, i32), "sn": (128, i32), "s2": (256, i32),
+    "nn": (32, i32), "n2": (64, i32), "cn": (4, i32), "c2": (8, i32), "RL": (512, f32), "SL": (512, f32),
+    "SN": (512, f32), "NW": (512, f32), "IO": (512, f32), "lr": (32, u16), "ls": (32, u16), "ln": (32, u16), "lc": (2, u16),
+    "l4": (4, u16), "li": (72, f32), "zz": (1024, bf),
+    "pc": (16, i32), "col": (32, f32), "it": (512, f32), "i2": (288, f32), "i3": (128, f32), "i4": (64, f32),
+    "BA": (144, bf), "B2": (144, bf), "Be": (144, bf), "Bk": (144, bf), "Bh": (144, bf), "Bf": (144, f16),
+    "Bq": (144, bf), "Bl": (144, bf),
+    "BK": (144, f32), "BP": (144, f16), "SG": (128, f32), "TRI": (128, f32), "UP": (128, f32), "S4": (128, f32),
+    "S4n": (128, f32), "PM0": (128, f32), "PM1": (128, f32), "OM": (512, bf), "R8": (512, bf), "R4": (128, f32),
+    "R16": (128, f32), "i16": (128, f32), "c641": (512, f16), "one": (640, bf),
+    "c16": (320, bf), "dump": (32, f32), "DG": (128, f32), "ID": (16, f32), "kc": (64, f32), "nix": (128, f32),
+    "d12": (16, f32), "neg": (256, f32),
+    "sl": (4, u16), "sq": (16, u16), "rq": (32, u16), "qo": (32, f32), "qp": (32, f32),
+    "t1": (256, f32), "t2": (128, f32), "u2": (128, f32), "u3": (128, f32),
+    "x1": (256, f32), "x2": (128, f32), "NWc": (64, f32), "SNo": (64, f32),
+    "G1": (512, bf), "G2": (512, bf), "sg0": (512, bf), "sg1": (512, bf), "z": (512, bf), "cum": (520, f16), "mm": (512, f16),
+    "Ff": (520, bf), "D": (512, bf), "o1": (32, f32), "o2": (32, f32), "pc1": (32, f32), "of": (32, u16),
+    "Y": (320, f32), "vi": (320, i32), "va": (320, i32), "E": (32, u16),
+    "RS": (3 * 320, u16), "RI": (3 * 320, u16), "PS": (3 * 320, u16), "PI": (3 * 320, u16),
+    "Hg": (5120, bf), "WF": (328, f32), "Ab": (RING * 648, f32),
+    "d": (RING * C, bf), "ct": (RING * C, bf), "r": (RING * C, bf), "cs": (648, f32), "g1": (512, f32), "sc": (520, f32),
+    "key": (64, f32), "mx": (48, f32), "oh": (64, f32), "y": (640, f32), "DB": (648, f32), "dd": (512, bf),
+    "en": (32, f32), "eu": (32, u16), "kl": (32, f32), "b1": (32, f32), "b2": (32, f32), "b3": (64, f32), "ow": (32, f32),
+    "bi": (24, i32), "bu": (16, u16), "Mk": (128, f32), "Wd": (128, f32), "K": (128, f32),
+    "k2": (256, f32), "own": (8, f32), "o256": (8, f32), "fi": (8, f32), "k3": (16, f32), "k4": (16, f32), "ku": (16, u16),
+    "YT": (192, f32), "YB": (384, f32), "YW": (48, f32),
+}
+HOME, SCRATCH = {}, {}
+for _k, (_n, _t) in SB.items():
+    _h = _k if _n > 600 else "all_" + _t
+    _at = SCRATCH[_h][1][1] if _h in SCRATCH else 0
+    HOME[_k] = (_h, _at)
+    SCRATCH[_h] = ("sbuf", [128, _at + (_n + 15) // 16 * 16], _t)
+SCRATCH["DT"] = ("dram", [N, 128, 64], u16)
+PSUM = ["Z0", "Z1", "PX0", "PX1", "PX2", "PH0", "PH1", "PM"]
+for _k in PSUM:
+    SCRATCH[_k] = ("psum", [128, 512], f32)
+    HOME[_k] = (_k, 0)
+SEMAPHORES = (["v", "s", "p", "g", "sent", "tab"] + ["d%d" % k for k in range(1, 45)]
+              + ["%s%d_%d" % (a, r, k) for a in "qa" for r in range(RO) for k in range(len(GROUPS))])
+CY, PE, GA, SC, FIX, HOP, DMA, REM, ISS, ROW, FIRST = 1.04e-3, 0.52e-3, 1.56, 3.8, 0.05, 0.06, 2.0, 2.5, 0.7, 0.05, 3.0
+SWEEPS, SEED = 1000, 5
+PLAN = []
+
+
+def rank_program(g, core, T, topo):
+    me = T.rank_of(core)
+    if me is None:
+        return
+    Q = {"v": g.vector, "s": g.scalar, "p": g.tensor, "g": g, "y": g.sync}
+    nodes, recs, nd, chain, last, gate = [], {}, [0], [None], {}, [None]
+
+    def a(name, lo=0, hi=None, st=1, ps=None):
+        return (name, lo, (SB[name][0] if name in SB else 512) if hi is None else hi, st, ps)
+
+    def ind(w, o):
+        return ("@", w, o)
+
+    def ap(x):
+        if not isinstance(x, tuple):
+            return x
+        if x[0] == "@":
+            return ap(x[1]).indirect(ap(x[2]))
+        ps = slice(0, 128) if x[4] is None else x[4]
+        h, at = HOME[x[0]]
+        return T[h][ps, at + x[1]:at + x[2]:x[3]] if x[3] > 1 else T[h][ps, at + x[1]:at + x[2]]
+
+    def width(x):
+        return 16 * width(x[2]) if x[0] == "@" else (x[2] - x[1] + x[3] - 1) // x[3]
+
+    def two(x):
+        return x[0] in SB and SB[x[0]][1] in (bf, u16, f16)
+
+    def add(q, fn, reads, writes, hold, late=0.0, sem=None, val=None, after=()):
+        use = []
+        for x in reads:
+            if isinstance(x, tuple):
+                use += [(x[1], 0), (x[2], 0)] if x[0] == "@" else [(x, 0)]
+        for x in writes:
+            if isinstance(x, tuple):
+                use += [(x[1], 1), (x[2], 0)] if x[0] == "@" else [(x, 1)]
+        deps, n = set(after), len(nodes)
+        for x, w in use:
+            for lo, hi, w0, q0, k in recs.get(x[0], []):
+                if (q0 != q or w or w0) if x[0] in PSUM else ((w or w0) and lo < x[2] and x[1] < hi):
+                    deps.add(k)
+        for x, w in use:
+            old = recs.get(x[0], [])
+            if w and x[0] in PSUM:
+                old = []
+            elif w and x[3] == 1 and x[4] is None:
+                old = [e for e in old if not (x[1] <= e[0] and e[1] <= x[2])]
+            recs[x[0]] = old + [(x[1], x[2], w, q, n)]
+        soft = set()
+        if chain[0]:
+            soft = {last[q, chain[0]]} - deps if (q, chain[0]) in last else set()
+            last[q, chain[0]] = n
+        if gate[0] is not None and q == "v":
+            soft = soft | ({gate[0]} - deps)
+        nodes.append({"q": q, "fn": fn, "deps": deps | soft, "soft": soft, "hold": hold, "late": late, "sem": sem or q, "val": val})
+        return n
+
+    def vec(fn, reads, o, per=1.0):
+        big = [x for x in reads if isinstance(x, tuple) and width(x) > 1] + [o]
+        if o[0] == "@":
+            per = SC
+        elif any(x[0] == "@" for x in big):
+            per = GA
+        elif all(two(x) for x in big):
+            per *= 0.5
+        add("v", fn, reads, [o], max(64, per * max(width(x) for x in big)) * CY + FIX)
+
+    def cp(o, i):
+        vec(lambda: g.vector.tensor_copy(ap(o), ap(i)), [i], o)
+
+    def tt(o, x, y, f):
+        vec(lambda: g.vector.tensor_tensor(ap(o), ap(x), ap(y), f), [x, y], o, 1.0 if x[0] in PSUM or y[0] in PSUM else 2.0)
+
+    def ts(o, x, s1, f1, s2=None, f2=None):
+        if f2 is None:
+            vec(lambda: g.vector.tensor_scalar(ap(o), ap(x), ap(s1), None, f1), [x, s1], o)
+        else:
+            vec(lambda: g.vector.tensor_scalar(ap(o), ap(x), ap(s1), ap(s2), f1, f2), [x, s1, s2], o)
+
+    def scan(o, d0, d1, init, f0, f1):
+        vec(lambda: g.vector.tensor_tensor_scan(ap(o), ap(d0), ap(d1), ap(init), f0, f1), [d0, d1, init], o)
+
+    def mset(o, c):
+        vec(lambda: g.vector.memset(ap(o), c), [], o)
+
+    def turn(o, i):
+        vec(lambda: g.vector.transpose(ap(o), ap(i)), [i], o)
+
+    def least(o, x):
+        vec(lambda: g.vector.tensor_reduce(ap(o), ap(x), AxisListType.X, A.min, apply_absolute_value=True), [x], o)
+
+    def act(o, i, f, bias=0.0, scale=1.0, total=None):
+        add("s", lambda: g.scalar.activation(ap(o), ap(i), f, bias=ap(bias), scale=ap(scale), accum_out=ap(total)),
+            [i, bias, scale], [o, total], max(64, width(o) * (GA if i[0] == "@" else 1.0)) * CY + FIX)
+
+    def iota(o, pat, base, ch):
+        kw = {} if SB[o[0]][1] == i32 else {"allow_small_or_imprecise_dtypes": True}
+        add("g", lambda: g.iota(ap(o), pat, base, ch, **kw), [], [o], 0.15 + 2 * width(o) * CY)
+
+    def mm(o, terms, start=True, stop=True):
+        def fn():
+            for k, t in enumerate(terms):
+                ins = g.tensor.matmul(ap(t[2] if len(t) > 2 else o), ap(t[0]), ap(t[1]), start and k == 0, stop and k == len(terms) - 1)
+            return ins
+        add("p", fn, [x for t in terms for x in t[:2]], [o], sum(max(64, width(t[1])) * (1 if two(t[0]) else 4) * PE for t in terms))
+
+    def dma(q, o, i, reads=(), writes=(), late=DMA):
+        nd[0] += 1
+        add(q, lambda: Q[q].dma_start(ap(o), ap(i)), [i] + list(reads), [o] + list(writes), 0.1, late, "d%d" % nd[0], 16)
+
+    def send(ds, sign, src, dst, sem, read, land, late):
+        trs, n = [], 0
+        for k, dl in enumerate(ds):
+            peer = T.cores[(me + sign * (dl + 1)) % N]
+            es = topo.engines(core, peer)
+            n = 1
+            while 2 * n * len(ds) <= len(es):
+                n *= 2
+            rid, pid = topo.addr(peer, core)
+            trs.append(RemoteDMATransfer(dst_ids=[DstId(rid=rid, pnc=pid)], dma_engine_mask=sum(1 << e for e in es[k * n:(k + 1) * n]),
+                                         remote_sem=T.sem[sem], src=src(dl), dst=dst(dl)))
+        k = add("g", lambda: g.remote_dma_fused(trs, local_sem=T.sem.sent), [read], [], ISS + (FIRST if sem == "tab" else 0.0), 0.0, "sent", n * len(ds))
+        add("r", None, [], [land], 0.0, late, sem, n * len(ds), [k])
+
+    def issue():
+        n = len(nodes)
+        rest = [0.0] * n
+        for k in range(n - 1, -1, -1):
+            rest[k] += nodes[k]["hold"] + nodes[k]["late"] + HOP
+            for j in nodes[k]["deps"]:
+                rest[j] = max(rest[j], rest[k])
+        users = [[] for k in range(n)]
+        for k in range(n):
+            for j in nodes[k]["deps"]:
+                users[j].append(k)
+
+        def place(turns, back):
+            at, used = [0.0] * n, {q: [] for q in Q}
+            for k in turns:
+                e = nodes[k]
+                if back:
+                    t = max([at[j] + nodes[j]["hold"] for j in users[k]] + [0.0]) + e["late"] + HOP
+                else:
+                    t = max([at[j] + nodes[j]["hold"] + nodes[j]["late"] + HOP for j in e["deps"]] + [0.0])
+                if e["q"] in used:
+                    spans = used[e["q"]]
+                    i = len(spans)
+                    while i and spans[i - 1][1] > t:
+                        i -= 1
+                    while i < len(spans) and spans[i][0] < t + e["hold"]:
+                        t = max(t, spans[i][1])
+                        i += 1
+                    spans.insert(i, (t, t + e["hold"]))
+                at[k] = t
+            return at, max(at[k] + nodes[k]["hold"] + (0.0 if back else nodes[k]["late"]) for k in range(n))
+
+        if not PLAN:
+            start, best = place(sorted(range(n), key=lambda k: (-rest[k], k)), False)
+            rng = np.random.default_rng(SEED)
+            for sweep in range(SWEEPS):
+                key = np.array(start) + rng.normal(0.0, (0.3, 1.0, 3.0)[sweep % 3], n) * (rng.random(n) < 0.3)
+                for k in range(n):
+                    for j in nodes[k]["deps"]:
+                        key[k] = max(key[k], key[j])
+                now, end = place(sorted(range(n), key=lambda k: (key[k], k)), False)
+                if sweep % 4 == 0:
+                    late = place(sorted(range(n), key=lambda k: (-now[k] - nodes[k]["hold"] - nodes[k]["late"], -k)), True)[0]
+                    now, end = place(sorted(range(n), key=lambda k: (-late[k] - nodes[k]["hold"], k)), False)
+                if end <= best:
+                    start, best = now, end
+            PLAN.append(start)
+        start = PLAN[0]
+        cnt, seen = {}, {q: {} for q in Q}
+        for k in sorted(range(n), key=lambda k: (start[k], k)):
+            e = nodes[k]
+            q, sem = e["q"], e["sem"]
+            if q != "r":
+                need = {}
+                for j in e["deps"] - e["soft"]:
+                    if not (q == "p" and nodes[j]["q"] == "p"):
+                        need[nodes[j]["sem"]] = max(need.get(nodes[j]["sem"], 0), nodes[j]["at"])
+                for s, val in need.items():
+                    if seen[q].get(s, 0) < val:
+                        Q[q].wait_ge(T.sem[s], val)
+                        seen[q][s] = val
+                ins = e["fn"]()
+                if sem != "sent":
+                    ins.then_inc(T.sem[sem], e["val"] or 1)
+            cnt[sem] = cnt.get(sem, 0) + (e["val"] or 1)
+            e["at"] = cnt[sem]
+        for s, val in cnt.items():
+            if max(seen[q].get(s, 0) for q in Q) < val:
+                g.sync.wait_ge(T.sem[s], val)
+
+    def band(name, i):
+        return a(name, 15 - i, 143 - i)
+
+    def pick(o, name, src, lo, hi, start=True, stop=True):
+        mm(o, [(band(name, i), a(src, lo + i, hi, 16)) for i in range(16)], start, stop)
+
+    def squeeze(o, name, lo, hi, f, st=1, sums=1):
+        mm(o, [(a("DQ" if f == 4 else "DH", 128 * d, 128 * d + 128), a(name, lo + st * d + k, hi, st * f))
+               for d in range(f) for k in range(sums)])
+
+    def colf(w, x, tmp):
+        ts(a(tmp, 0, w), x, 15, A.bitwise_and)
+        ts(a(tmp, w, 2 * w), x, 4, A.arith_shift_right)
+        ts(a(tmp, 0, w), a(tmp, 0, w), 32.0, A.mult)
+        tt(x, a(tmp, 0, w), a(tmp, w, 2 * w), A.add)
+
+    def col(k):
+        return a("col", k, k + 1)
+
+    def zero(name, n):
+        chain[0] = "zero"
+        for lo in range(0, n, 1024):
+            act(a(name, lo, lo + 1024), a("zz"), F.Copy)
+        chain[0] = None
+
+    row0 = slice(0, 128, 16)
+
+    dma("y", a("gi", 0, 32), T.gst[:])
+    dma("s", a("gi", 32, 64), T.gln[:])
+    for k in range(2):
+        dma("y", a("sn", 64 * k, 64 * k + 64), T.sens[k::2, :])
+        dma("s", a("rn", 128 * k, 128 * k + 128), T.rel[k::2, :])
+        dma("y", a("nn", 16 * k, 16 * k + 16), T.nxt[:, 256 * k:256 * k + 256])
+    dma("y", a("cn", 0, 1), T.cur[:])
+    dma("s", a("Tj", 0, 512), T.heap[:])
+    dma("y", a("wp", 0, 1536), T.wpos[:, 0:1536], late=6.0)
+    dma("s", a("wp", 1536, V), T.wpos[:, 1536:V], late=6.0)
+
+    iota(a("pc", 0, 1), [[1, 1]], 0, 1)
+    iota(a("i3"), [[16, 8], [0, 2], [2, 8]], 0, 0)
+    iota(a("i2", 0, 144), [[1, 144]], -15, 0)
+    iota(a("i2", 144, 288), [[1, 144]], -8, 0)
+    iota(a("li", 0, 32), [[8, 16], [128, 2]], 0, 0)
+    iota(a("li", 32, 64), [[4, 16], [64, 2]], 0, 0)
+    iota(a("li", 64, 68), [[4, 4]], 0, 0)
+    iota(a("i4"), [[0, 16], [1, 4]], 0, 0)
+    iota(a("it"), [[0, 64], [1, 8]], 0, 0)
+    iota(a("sli"), [[0, 7], [16, 40]], 0, 0)
+    iota(a("dump"), [[16, 32]], 5120, 0)
+    iota(a("nix"), [[1, 128]], 0, 0)
+    iota(a("i16"), [[0, 8], [1, 16]], 0, 0)
+    iota(a("R4"), [[0, 32], [1, 4]], 0, 0)
+    iota(a("SG"), [[16, 8], [0, 16]], 0, 0)
+    iota(a("IO"), [[1, 16], [16, 32]], 0, 0)
+    iota(a("d12"), [[16, 16]], 2 * ODD, 0)
+    mset(a("zz"), 0.0)
+    p0 = a("pc", 0, 1)
+    cp(col(0), p0)
+    ts(col(1), p0, -1.0, A.add)
+    ts(a("PM0"), a("i3"), col(0), A.is_equal)
+    ts(a("PM1"), a("i3"), col(1), A.is_equal)
+    for k, m in ((2, 112), (3, 15), (4, 8), (6, 7), (7, 119), (8, 3), (9, 12)):
+        ts(a("pc", k, k + 1), p0, m, A.bitwise_and)
+        ts(col(k), a("pc", k, k + 1), {4: 0.125, 9: 0.25}.get(k, 1.0), A.mult)
+    ts(col(5), col(4), -1.0, A.mult, 1.0, A.add)
+    chain[0] = "zero"
+    for lo in range(0, 5120, 640):
+        iota(a("W0", lo, lo + 640), [[0, 640]], 0, 0)
+    zero("HW", 2 * HP)
+
+    cp(a("gf"), a("gi"))
+    for k in range(4):
+        mm(a("PM", 32 * k, 32 * k + 32), [(a("PM%d" % (k & 1)), a("gf", 32 * (k >> 1), 32 * (k >> 1) + 32))])
+    cp(a("m1"), a("PM", 0, 128))
+    st, ln = a("m1", 0, 64), a("m1", 64, 128)
+    ts(a("m2", 0, 64), st, 127, A.bitwise_and)
+    ts(a("m2", 64, 128), st, 7, A.arith_shift_right)
+    ts(a("m3", 128, 192), ln, 1.0, A.min)
+    ts(a("m3", 192, 256), ln, col(5), A.mult, 2049.0, A.mult)
+    ts(a("m3", 64, 128), a("m2", 64, 128), 2048.0, A.add, col(4), A.mult)
+    ts(a("m3", 0, 64), a("m2", 0, 64), col(5), A.mult)
+    tt(a("m3", 0, 64), a("m3", 0, 64), a("m3", 64, 128), A.add)
+    tt(a("m3", 0, 64), a("m3", 0, 64), a("m3", 128, 192), A.mult)
+    tt(a("m3", 0, 64), a("m3", 0, 64), a("m3", 192, 256), A.add)
+    cp(a("msg"), a("m3", 0, 64))
+    own = ("DT", SELF, N, 1, None)
+    dma("y", T.DT[SELF], a("msg"), writes=[own])
+    send(list(range(SELF)), -1, lambda dl: T.DT[SELF], lambda dl: T.DT[dl], "tab", own, ("DT", 0, SELF, 1, None), REM + 1.0)
+    for dl in range(N):
+        dma("ys"[dl & 1], a("Tc", ps=slice(dl, 128, 8)), T.DT[dl], reads=[("DT", dl, dl + 1, 1, None)])
+        recs["Tc"], recs["Tc%d" % dl] = [], recs["Tc"]
+    recs["Tc"] = [e for dl in range(N) for e in recs["Tc%d" % dl]]
+
+    ts(a("lr"), a("li", 0, 32), col(6), A.add)
+    ts(a("ls"), a("li", 32, 64), col(8), A.add)
+    ts(a("l4"), a("li", 64, 68), col(9), A.add)
+    colf(128, a("sn"), "s2")
+    cp(a("g1"), ind(a("sn"), a("ls")))
+    turn(a("SL"), a("g1"))
+    ts(a("rn"), a("rn"), float(512 * (SELF - me)), A.add)
+    ts(a("rn"), a("rn"), 4095, A.bitwise_and)
+    cp(a("y", 0, 512), ind(a("rn"), a("lr")))
+    turn(a("RL"), a("y", 0, 512))
+    colf(1, a("cn", 0, 1), "c2")
+    cp(a("lc", 0, 1), a("cn", 0, 1))
+    act(a("kc"), a("i4"), F.Identity, bias=3.0, scale=-1.0)
+    ts(a("i4", 0, 4), a("i4", 0, 4), col(9), A.is_equal)
+    for d in range(4):
+        ts(a("DQ", 128 * d, 128 * d + 128), a("nix"), col(0), A.is_equal, a("i4", d, d + 1), A.mult)
+    for d in range(2):
+        ts(a("DH", 128 * d, 128 * d + 128), a("nix"), col(0), A.is_equal, col(5 - d), A.mult)
+    act(a("SNo", 0, 16), ind(a("SL"), a("lc", 0, 1)), F.Copy)
+    squeeze(a("PX1", 0, 4), "SNo", 0, 16, 4)
+    cp(a("sl"), a("PX1", 0, 4))
+    act(a("t1", 0, 64), ind(a("RL"), a("sl")), F.Copy)
+    squeeze(a("PX1", 32, 64), "t1", 0, 64, 2)
+    cp(a("rq"), a("PX1", 32, 64))
+
+    ts(col(10), col(5), 1024.0, A.mult)
+    ts(col(14), col(6), -float(C), A.mult, col(5), A.mult)
+    ts(col(15), col(5), -1.0, A.mult)
+    for name, w in (("Bf", col(5)), ("Bk", col(10)), ("BA", 1.0), ("B2", 2.0), ("Be", 0.5), ("Bh", col(4)), ("Bq", col(14)), ("Bl", col(15))):
+        ts(a(name), a("i2", 0, 144), col(2), A.is_equal, w, A.mult)
+    ts(a("BK"), a("i2", 144, 288), col(7), A.is_equal)
+    ts(a("BP"), a("i2", 144, 288), col(7), A.is_equal, col(5), A.mult)
+    ts(a("SG"), a("SG"), col(2), A.is_equal)
+    ts(a("TRI"), a("nix"), col(0), A.is_ge)
+    tt(a("TRI"), a("TRI"), a("SG"), A.mult)
+    tt(a("UP"), a("SG"), a("TRI"), A.subtract)
+    ts(a("dump"), a("dump"), col(3), A.add)
+    mset(a("c641"), -641.0)
+    mset(a("one"), 1.0)
+    mset(a("cum", 0, 1), -1.0)
+    mset(a("Ff", 0, 1), 0.0)
+    ts(a("R40"), a("sli"), 1.0, A.min)
+    ts(a("sli"), a("sli"), col(3), A.add)
+    ts(col(12), col(4), 1.0 - HP, A.mult, -1.0, A.add)
+    ts(col(13), col(4), 127.0, A.mult, 1.0, A.add)
+    ts(a("col", 16, 24), a("it", 0, 8), col(6), A.is_equal, col(12), A.mult)
+    act(a("off"), a("col", 16, 24), F.Copy, scale=-1024.0)
+    ts(a("col", 24, 32), a("it", 0, 8), col(6), A.is_equal, col(13), A.mult)
+    ts(a("Tj", 512, 1024), a("Tj", 0, 512), 4032, A.bitwise_and)
+    cp(a("hb", 0, 512), a("Tj", 512, 1024))
+    act(a("hb", 1024, 1536), a("hb", 0, 512), F.Identity, bias=float(ODD))
+    ts(a("Ti"), a("Tj", 0, 512), 63, A.bitwise_and)
+    ts(a("hb", 512, 1024), a("Ti"), 1.0, A.add)
+    for lo, (p, x) in zip((0, 0, HP, HP), ((0, 0), (1, 512), (0, 1024), (1, 512))):
+        dma("y", a("HW", lo, lo + HP, ps=slice(p, 128, 16)), a("hb", x, x + 512), late=3.0)
+        if p == 0:
+            keep = recs["HW"].pop()
+        else:
+            recs["HW"].append(keep)
+
+    mset(a("B", 0, 1), -5.0)
+    mset(a("B", V + 1, ODD + 1), -5.0)
+    for lo in range(0, V, 760):
+        ts(a("B", 1 + lo, 761 + lo), a("wp", lo, lo + 760), 4.0, A.mult, -5.0, A.add)
+        act(a("B", ODD + 1 + lo, ODD + 761 + lo), a("B", 1 + lo, 761 + lo), F.Identity, bias=-0.5)
+
+    cp(a("Ti"), a("Tc"))
+    ts(a("Tj", 0, 512), a("Ti"), 2047, A.bitwise_and)
+    cp(a("Tb"), a("Tj", 0, 512))
+    ts(a("Tl"), a("Tc"), 1.0 / 2048, A.mult, 1024.0, A.add)
+    chain[0] = "tables"
+    for q in range(N):
+        ts(a("T1", 512 * q, 512 * q + 512), a("Tl"), col(16 + q), A.mult, a("off", q, q + 1), A.add)
+        if q < T2_ON_SCALAR:
+            act(a("T2", 512 * q, 512 * q + 512), a("Tb"), F.Copy, scale=col(24 + q))
+        else:
+            ts(a("T2", 512 * q, 512 * q + 512), a("Tb"), col(24 + q), A.mult)
+    chain[0] = None
+
+    mset(a("Ab", 0, RING * 648, 648), 0.0)
+    mset(a("WF", 0, 1), 0.0)
+    colf(32, a("nn"), "n2")
+    for k in range(2):
+        cp(a("ln", k, 32, 2), a("nn", 16 * k, 16 * k + 16))
+    cp(a("SN"), ind(a("SL"), a("ln")))
+    act(a("NW"), ind(a("IO"), a("ln")), F.Copy)
+    ts(a("OM"), a("it"), col(3), A.is_equal)
+    ts(a("R8"), a("it"), 1.0, A.min)
+    ts(a("DG"), a("i16"), col(3), A.is_equal)
+    ts(a("ID"), a("i16", 0, 16), col(3), A.is_equal)
+    ts(a("R16"), a("i16"), 1.0, A.min)
+    ts(a("R4"), a("R4"), 1.0, A.min)
+    act(a("S4"), a("SG"), F.Copy, scale=4.0)
+    act(a("S4n"), a("SG"), F.Copy, scale=-4.0)
+    act(a("S256"), a("nix"), F.Copy, scale=1.0 / 4096)
+    act(a("i3"), a("nix"), F.Identity, bias=1.0, scale=1.0 / 256)
+    act(a("d12"), a("d12"), F.Identity, bias=col(3))
+    mset(a("neg"), -5.0)
+    mset(a("c16"), 8.0)
+    for dl in SIGN_ON_VECTOR:
+        ts(a("fi", 0, 1), col(3), float(dl), A.not_equal)
+        ts(a("c16"), a("c16"), a("fi", 0, 1), A.mult)
+    mset(a("cs", 0, 1), 0.0)
+    mset(a("DB", 0, 1), 0.0)
+    mset(a("sc", 0, 8), 0.0)
+
+    def forty(name, rd, ds):
+        return a(name, 320 * rd + 40 * ds[0], 320 * rd + 40 * (ds[-1] + 1))
+
+    def requests(rd):
+        W, sg = "W%d" % (rd & 1), "sg%d" % (rd & 1)
+        for k in range(len(EARLY)):
+            chain[0] = chain[0] if EARLY[k] else None
+        cp(a("G1"), ind(a("T1"), a("rq")))
+        chain[0] = None
+        act(a("G2"), ind(a("T2"), a("rq")), F.Copy)
+        act(a(sg), a("G1"), F.Sign)
+        scan(a("cum", 1, 513), a("G1"), a("c641"), -1.0, A.add, A.max)
+        act(a("z"), a("G1"), F.Relu, bias=1.0)
+        pick(a("PM", 0, 32), "Bk", sg, 0, 512, True, False)
+        pick(a("PH0", 0, 32), "Bq", sg, 0, 512)
+        tt(a("mm"), a("cum", 0, 512), a(sg), A.mult)
+        pick(a("PM", 0, 32), "Bf", "mm", 0, 512, False, True)
+        scan(a("Ff", 1, 513), a("z"), a("G2"), 0.0, A.mult, A.add)
+        act(a("qp"), a("PH0", 0, 32), F.Identity, bias=1023.0)
+        tt(a("D"), a("Ff", 1, 513), a("Ff", 0, 512), A.subtract)
+        tt(a("o2"), a("PM", 0, 32), a("qp"), A.add)
+        ts(a("o1"), a("PM", 0, 32), C - 1023.5, A.is_gt, 8192.0, A.mult)
+        tt(a("o1"), a("o1"), a("o2"), A.add)
+        tt(a("o2"), a("o1"), a("dump"), A.min)
+        cp(a("of"), a("o2"))
+        tt(ind(a(W), a("of")), a("D"), a("G1"), A.add)
+        for k, ds in enumerate(BATCH):
+            bank, lo, hi = "PX%d" % (k % 3), 40 * ds[0], 40 * (ds[-1] + 1)
+            pick(a(bank, 0, hi - lo), "BA", W, C * ds[0], C * (ds[-1] + 1))
+            scan(a("Y", lo, hi), a("R40", 0, hi - lo), a(bank, 0, hi - lo), 0.0, A.mult, A.add)
+            mm(a(bank, 256, 256 + hi - lo), [(a("TRI"), a("Y", lo, hi))]
+               + [(a("UP"), a("Y", x, x + 39), a(bank, 257 + x - lo, 296 + x - lo)) for x in range(lo, hi, 40)])
+            tt(a("vi", lo, hi), a(bank, 256, 256 + hi - lo), a("sli", 0, hi - lo), A.add)
+            ts(a("va", lo, hi), a("vi", lo, hi), 2 * HP - 1, A.bitwise_and)
+            cp(forty("RS", rd, ds), a("va", lo, hi))
+            for j, to in enumerate(GROUPS):
+                if to[0] in ds:
+                    send(to, 1, lambda dl: ap(forty("RS", rd, [dl])), lambda dl: ap(forty("RI", rd, [dl])), "q%d_%d" % (rd, j),
+                         forty("RS", rd, to), forty("RI", rd, to), REM + 16 * len(to) * ROW)
+
+    def ends(rd):
+        act(a("pc1"), a("PM", 0, 32), F.Identity, bias=1023.0)
+        act(a("qo"), a("qp"), F.Identity, bias=-1023.0)
+        mm(a("PM", 64, 96), [(a("BP", 8, 136), a("cum", 8, 513, 16)), (a("BP", 0, 128), a("cum", 16, 513, 16))])
+        pick(a("PM", 96, 128), "Bl", "G1", 0, 512)
+        ts(a("E"), a("PM", 64, 96), -1.0, A.mult, -1.0, A.add)
+        tt(a("b3", 0, 32), a("PM", 96, 128), a("pc1"), A.add)
+        ts(a("en"), a("b3", 0, 32), float(C), A.min)
+        cp(a("eu"), a("en"))
+        tt(a("kl"), a("pc1"), a("en"), A.subtract)
+        tt(a("en"), a("en"), a("qo"), A.add)
+
+    def ahead(rd):
+        act(a("NWc"), ind(a("NW"), a("sl")), F.Copy)
+        if rd + 1 < RO:
+            act(a("SNo"), ind(a("SN"), a("sl")), F.Copy)
+            squeeze(a("PX1", 0, 16), "SNo", 0, 64, 4)
+            cp(a("sq"), a("PX1", 0, 16))
+            act(a("t1"), ind(a("RL"), a("sq")), F.Copy)
+            for k in range(2):
+                mm(a("PX0", 64 * k, 64 * k + 64), [(a("DH", 128 * d, 128 * d + 128), a("t1", 2 * k + d, 256, 4)) for d in range(2)])
+
+    def answer(rd, ds):
+        for dl in ds:
+            src = ind(a("HW"), forty("RS" if dl == SELF else "RI", rd, [dl]))
+            if dl in HEAP_ON_VECTOR:
+                cp(a("Hg", C * dl, C * dl + C), src)
+            else:
+                act(a("Hg", C * dl, C * dl + C), src, F.Copy)
+        bank = a("PH%d" % ((ds[0] + 1) // 2 & 1), 0, 40 * len(ds))
+        pick(bank, "BA", "Hg", C * ds[0], C * (ds[-1] + 1))
+        if ds == [SELF]:
+            return cp(forty("PI", rd, ds), bank)
+        cp(forty("PS", rd, ds), bank)
+        send(ds, -1, lambda dl: ap(forty("PS", rd, [dl])), lambda dl: ap(forty("PI", rd, [dl])), "a%d_%d" % (rd, GROUPS.index(ds)),
+             forty("PS", rd, ds), forty("PI", rd, ds), REM + 16 * len(ds) * ROW)
+
+    def phrases(rd, dl, slot, first, last):
+        lo, x0 = C * slot, 648 * slot
+        hi, src = lo + C, ind(a("B", 0, ODD + V + 1), forty("PI", rd, [dl]))
+        act(a("Ab", x0 + 1, x0 + 641), src, F.Abs, bias=4.0)
+        tt(a("ct", lo, hi), src, a("Ab", x0, x0 + C), A.is_equal)
+        if dl in SIGN_ON_VECTOR:
+            ts(a("d", lo, hi), a("Ab", x0 + 1, x0 + 641), 2.0, A.is_gt, 2.0, A.mult)
+        else:
+            act(a("d", lo, hi), a("Ab", x0 + 1, x0 + 641), F.Sign, bias=-2.0)
+        scan(a("r", lo, hi), a("ct", lo, hi), a("ct", lo, hi), 0.0, A.mult, A.add)
+        for k in range(2):
+            x, y = lo + 320 * k, lo + 320 * k + 320
+            mm(a("Z%d" % k, 0, 320), [(band("BA", 8 + dl), a("ct", x, y)), (band("Be", dl), a("d", x, y))], first, False)
+        for k in range(2):
+            mm(a("Z%d" % k, 0, 320), [(band("B2", dl), a("r", lo + 320 * k, lo + 320 * k + 320))], False, last)
+
+    def winner(rd):
+        scan(a("cs", 1, 321), a("c16"), a("Z0", 0, 320), 0.0, A.add, A.add)
+        scan(a("cs", 321, 641), a("c16"), a("Z1", 0, 320), a("cs", 320, 321), A.add, A.add)
+        for k in range(2):
+            act(a("y", 320 * k, 320 * k + 320), a("Z%d" % k, 0, 320), F.Relu, bias=9216.0, scale=-1024.0)
+        tt(a("g1"), ind(a("cs", 0, 641), a("E")), a("OM"), A.mult)
+        scan(a("sc", 8, 520), a("R8"), a("g1"), 0.0, A.mult, A.add)
+        mm(a("PM", 128, 192), [(a("S4"), a("sc", 15, 520, 8)), (a("S4n"), a("sc", 7, 512, 8))])
+        tt(a("key"), a("PM", 128, 192), a("kc"), A.add)
+        tt(a("mx", 16, 48), a("key", 0, 64, 2), a("key", 1, 64, 2), A.max)
+        tt(a("mx", 0, 16), a("mx", 16, 48, 2), a("mx", 17, 48, 2), A.max)
+        tt(a("oh"), ind(a("mx", 0, 16), a("l4")), a("key"), A.is_equal)
+        if rd + 1 < RO:
+            for k in range(2):
+                tt(a("u2", 64 * k, 64 * k + 64), a("PX0", 64 * k, 64 * k + 64), a("oh"), A.mult)
+            scan(a("u3"), a("R4"), a("u2"), 0.0, A.mult, A.add)
+            for k in range(2):
+                cp(a("rq", k, 32, 2), a("u3", 64 * k + 3, 64 * k + 64, 4))
+
+    def results(rd):
+        shown(rd)
+        act(a("YT", 64 * rd, 64 * rd + 64), a("PM", 128, 192), F.Copy, scale=0.25)
+        tt(a("t2", 0, 64), a("NWc"), a("oh"), A.mult)
+        mm(a("PX1", 64, 80), [(a("SG"), a("t2", k, 64, 4)) for k in range(4)])
+        act(a("YW", 16 * rd, 16 * rd + 16), a("PX1", 64, 80), F.Copy, scale=1.0 / 16)
+        if rd + 1 < RO:
+            tt(a("t2", 64, 128), a("SNo"), a("oh"), A.mult)
+            squeeze(a("PX1", 96, 100), "t2", 64, 128, 4, 4, 4)
+            cp(a("sl"), a("PX1", 96, 100))
+
+    def distances(rd):
+        scan(a("DB", 1, 641), a("one"), a("y"), 0.0, A.add, A.min)
+        tt(a("dd"), ind(a("DB", 0, 641), a("eu")), a("sg%d" % (rd & 1)), A.mult)
+
+    def barrier_words(rd):
+        pick(a("Z0", 0, 32), "Bh", "dd", 0, 512)
+        squeeze(a("Z0", 64, 96), "oh", 0, 64, 2)
+        tt(a("b1"), a("Z0", 0, 32), a("kl"), A.is_gt)
+        tt(a("b2"), a("Z0", 0, 32), a("en"), A.add)
+        tt(a("b1"), a("b1"), a("Z0", 64, 96), A.mult)
+        tt(a("b2"), a("b2"), a("b1"), A.mult)
+        cp(a("WF", 1, 321), forty("PI", rd, [0, SELF]))
+        mm(a("Z1", 32, 40), [(a("BK", 8 - 8 * (k >> 1), 136 - 8 * (k >> 1)), a("b2", k, 32, 4)) for k in range(4)])
+        ts(a("bi", 0, 8), a("Z1", 32, 40), 15.0, A.add)
+        ts(a("bi", 8, 16), a("bi", 0, 8), 15, A.bitwise_and)
+        ts(a("bi", 16, 24), a("bi", 0, 8), 4, A.arith_shift_right)
+        cp(a("bu"), a("bi", 8, 24))
+        act(a("Mk"), ind(a("ID"), a("bu", 0, 8)), F.Copy)
+        tt(a("Wd"), ind(a("WF", 0, 321), a("bu", 8, 16)), a("Mk"), A.mult)
+        mm(a("Z1", 256, 384), [(a("SG"), a("S256"))] * (rd + 1 < RO) + [(a("SG"), a("Wd"))])
+        ts(a("x2"), a("Z1", 256, 384), ODD + 0.75, A.is_gt, -float(ODD), A.mult)
+        tt(a("K"), a("Z1", 256, 384), a("x2"), A.add)
+
+    def shown(rd):
+        if rd + 1 < RO:
+            tt(a("YB", 128 * rd, 128 * rd + 128), a("K"), a("i3"), A.subtract)
+        else:
+            act(a("YB", 128 * rd, 128 * rd + 128), a("K"), F.Identity, bias=-1.0)
+
+    def barriers():
+        tt(a("k2", 0, 128), a("K"), a("DG"), A.mult)
+        scan(a("k2", 128, 256), a("R16"), a("k2", 0, 128), 0.0, A.mult, A.add)
+        act(a("nb"), a("k2", 143, 256, 16), F.Identity, bias=64.0, scale=-256.0)
+        for c in range(8):
+            x = a("x1", 128 * (c & 1), 128 * (c & 1) + 16 * c + 16)
+            act(x, a("K", 0, 16 * c + 16), F.Abs, bias=a("nb", c, c + 1), scale=256.0)
+            act(x, x, F.Relu, bias=64.0 * 8192, scale=-8192.0, total=a("acc", c, c + 1))
+        act(a("own"), a("k2", 143, 256, 16), F.Identity, bias=float(ODD))
+        tt(a("k3", 0, 8), a("acc"), a("k2", 143, 256, 16), A.add)
+        tt(a("k3", 8, 16), a("acc"), a("own"), A.add)
+        tt(a("k4"), a("k3"), a("d12"), A.min)
+        cp(a("ku"), a("k4"))
+        cp(ind(a("B"), a("ku")), a("neg"))
+
+    slot = 0
+    for rd in range(RO):
+        if rd + 1 < RO:
+            for lo in range(0, 5120, 1024):
+                dma("y", a("W%d" % (~rd & 1), lo, lo + 1024), a("zz"), reads=[a("cs" if rd else "Tb")], late=4.0)
+        requests(rd)
+        if rd:
+            barrier_words(rd - 1)
+            barriers()
+        chain[0] = "answer"
+        for k, ds in enumerate(ANSWERS):
+            answer(rd, ds)
+            if k == GATE:
+                wait_for = last["v", "answer"]
+        chain[0], gate[0] = None, wait_for
+        if rd:
+            results(rd - 1)
+        ends(rd)
+        ahead(rd)
+        chain[0], gate[0] = "phrases", None
+        for dl in [SELF] + list(range(SELF)):
+            phrases(rd, dl, slot % RING, dl == SELF, dl == SELF - 1)
+            slot += 1
+        chain[0] = None
+        winner(rd)
+        chain[0] = "first%d" % rd
+        distances(rd)
+    chain[0] = None
+    barrier_words(RO - 1)
+    results(RO - 1)
+    dma("y", T.yb[:], a("YB", ps=row0))
+    dma("s", T.yt[:], a("YT", ps=row0))
+    dma("y", T.yw[:], a("YW", ps=row0))
+    issue()

@@ -5,14 +5,16 @@ from concourse.mybir import AluOpType as A, AxisListType, ActivationFunctionType
 N, V, HP, C, RO = 8, 3040, 8192, 640, 3
 BIG = float(2 ** 60)
 SELF = N - 1
-GROUPS = [[0], [1, 2], [3, 4], [5, 6]]
-BATCH = [[0, 1, 2], [7], [3, 4, 5, 6]]
-ANSWERS = [[0], [7], [1, 2], [3, 4], [5, 6]]
-HEAP_ON_VECTOR = (2, 4, 6)
-SIGN_ON_VECTOR = ()
+GROUPS = [[0, 1], [2, 3], [4, 5], [6]]
+BATCH = [[0, 1], [2, 3, 4, 5], [6, 7]]
+ANSWERS = [[0, 1], [7], [2, 3], [4, 5], [6]]
+HEAP_ON_VECTOR = (0, 2, 4)
+SIGN_ON_VECTOR = (4,)
 EARLY = [1]
-GATE = 4
-T2_ON_SCALAR = 6
+GATE = 3
+HUSH = 2
+REPEATS_ON_VECTOR = 0
+T2_ON_SCALAR = 16
 ODD = 3072
 RING = 3
 f32, bf, i32, u16, f16 = "float32", "bfloat16", "int32", "uint16", "float16"
@@ -21,10 +23,10 @@ SB = {
     "DQ": (512, f32), "DH": (256, f32), "acc": (8, f32), "S256": (128, f32), "nb": (8, f32),
     "W0": (5632, bf), "W1": (5632, bf), "gi": (64, i32), "gf": (64, f32), "m1": (128, i32), "m2": (128, i32),
     "m3": (256, f32), "msg": (64, u16), "Tc": (512, u16), "Ti": (512, i32), "Tj": (1024, i32), "Tl": (512, f16),
-    "off": (8, f32),
+    "off": (8, f32), "Ta": (512, bf), "qt": (64, u16),
     "Tb": (512, bf), "T1": (4096, bf), "T2": (4096, bf), "rn": (256, i32), "sn": (128, i32), "s2": (256, i32),
     "nn": (32, i32), "n2": (64, i32), "cn": (4, i32), "c2": (8, i32), "RL": (512, f32), "SL": (512, f32),
-    "SN": (512, f32), "NW": (512, f32), "IO": (512, f32), "lr": (32, u16), "ls": (32, u16), "ln": (32, u16), "lc": (2, u16),
+    "SN": (512, f32), "NW": (512, f32), "lr": (32, u16), "ls": (32, u16), "ln": (32, u16), "lc": (2, u16),
     "l4": (4, u16), "li": (72, f32), "zz": (1024, bf),
     "pc": (16, i32), "col": (32, f32), "it": (512, f32), "i2": (288, f32), "i3": (128, f32), "i4": (64, f32),
     "BA": (144, bf), "B2": (144, bf), "Be": (144, bf), "Bk": (144, bf), "Bh": (144, bf), "Bf": (144, f16),
@@ -36,7 +38,7 @@ SB = {
     "d12": (16, f32), "neg": (256, f32),
     "sl": (4, u16), "sq": (16, u16), "rq": (32, u16), "qo": (32, f32), "qp": (32, f32),
     "t1": (256, f32), "t2": (128, f32), "u2": (128, f32), "u3": (128, f32),
-    "x1": (256, f32), "x2": (128, f32), "NWc": (64, f32), "SNo": (64, f32),
+    "x1": (256, f32), "x2": (128, f32), "x3": (128, f32), "NWc": (64, f32), "SNo": (64, f32),
     "G1": (512, bf), "G2": (512, bf), "sg0": (512, bf), "sg1": (512, bf), "z": (512, bf), "cum": (520, f16), "mm": (512, f16),
     "Ff": (520, bf), "D": (512, bf), "o1": (32, f32), "o2": (32, f32), "pc1": (32, f32), "of": (32, u16),
     "Y": (320, f32), "vi": (320, i32), "va": (320, i32), "E": (32, u16),
@@ -61,9 +63,13 @@ for _k in PSUM:
     SCRATCH[_k] = ("psum", [128, 512], f32)
     HOME[_k] = (_k, 0)
 SEMAPHORES = (["v", "s", "p", "g", "sent", "tab"] + ["d%d" % k for k in range(1, 45)]
-              + ["%s%d_%d" % (a, r, k) for a in "qa" for r in range(RO) for k in range(len(GROUPS))])
-CY, PE, GA, SC, FIX, HOP, DMA, REM, ISS, ROW, FIRST = 1.04e-3, 0.52e-3, 1.56, 3.8, 0.05, 0.06, 2.0, 2.5, 0.7, 0.05, 3.0
-SWEEPS, SEED = 1000, 5
+              + ["%s%d_%d" % (a, r, k) for a in "qa" for r in range(RO) for k in range(SELF)])
+CASES = np.array([[0.9e-3, 0.5e-3, 1.56, 3.8, 0.05, 0.08, 2.7, 0.7, 0.05],
+                  [0.85e-3, 0.43e-3, 1.25, 2.5, 0.04, 0.12, 3.0, 0.9, 0.08],
+                  [1.15e-3, 0.7e-3, 1.85, 5.0, 0.05, 0.06, 2.5, 0.7, 0.05]])
+CY, PE, GA, SC, FIX, HOPS, REM, ISS, ROW = CASES.T
+HOP, DMA, FIRST = 0.08, 2.0, 3.0
+SWEEPS, STEPS, HEAT, SEED = 100, 20000, 0.01, 5
 PLAN = []
 
 
@@ -72,7 +78,7 @@ def rank_program(g, core, T, topo):
     if me is None:
         return
     Q = {"v": g.vector, "s": g.scalar, "p": g.tensor, "g": g, "y": g.sync}
-    nodes, recs, nd, chain, last, gate = [], {}, [0], [None], {}, [None]
+    nodes, recs, nd, chain, last, gate, hush = [], {}, [0], [None], {}, [None], [None]
 
     def a(name, lo=0, hi=None, st=1, ps=None):
         return (name, lo, (SB[name][0] if name in SB else 512) if hi is None else hi, st, ps)
@@ -119,9 +125,12 @@ def rank_program(g, core, T, topo):
         if chain[0]:
             soft = {last[q, chain[0]]} - deps if (q, chain[0]) in last else set()
             last[q, chain[0]] = n
+        if hush[0] is not None and q == "s":
+            soft = soft | ({hush[0]} - deps)
         if gate[0] is not None and q == "v":
             soft = soft | ({gate[0]} - deps)
-        nodes.append({"q": q, "fn": fn, "deps": deps | soft, "soft": soft, "hold": hold, "late": late, "sem": sem or q, "val": val})
+        nodes.append({"q": q, "fn": fn, "deps": deps | soft, "soft": soft, "holds": hold + 0 * HOPS, "lates": late + 0 * HOPS,
+                      "hold": float((hold + 0 * HOPS)[0]), "late": float((late + 0 * HOPS)[0]), "sem": sem or q, "val": val})
         return n
 
     def vec(fn, reads, o, per=1.0):
@@ -132,7 +141,7 @@ def rank_program(g, core, T, topo):
             per = GA
         elif all(two(x) for x in big):
             per *= 0.5
-        add("v", fn, reads, [o], max(64, per * max(width(x) for x in big)) * CY + FIX)
+        add("v", fn, reads, [o], np.maximum(64, per * max(width(x) for x in big)) * CY + FIX)
 
     def cp(o, i):
         vec(lambda: g.vector.tensor_copy(ap(o), ap(i)), [i], o)
@@ -160,7 +169,7 @@ def rank_program(g, core, T, topo):
 
     def act(o, i, f, bias=0.0, scale=1.0, total=None):
         add("s", lambda: g.scalar.activation(ap(o), ap(i), f, bias=ap(bias), scale=ap(scale), accum_out=ap(total)),
-            [i, bias, scale], [o, total], max(64, width(o) * (GA if i[0] == "@" else 1.0)) * CY + FIX)
+            [i, bias, scale], [o, total], np.maximum(64, width(o) * (GA if i[0] == "@" else 1.0)) * CY + FIX)
 
     def iota(o, pat, base, ch):
         kw = {} if SB[o[0]][1] == i32 else {"allow_small_or_imprecise_dtypes": True}
@@ -189,7 +198,7 @@ def rank_program(g, core, T, topo):
             trs.append(RemoteDMATransfer(dst_ids=[DstId(rid=rid, pnc=pid)], dma_engine_mask=sum(1 << e for e in es[k * n:(k + 1) * n]),
                                          remote_sem=T.sem[sem], src=src(dl), dst=dst(dl)))
         k = add("g", lambda: g.remote_dma_fused(trs, local_sem=T.sem.sent), [read], [], ISS + (FIRST if sem == "tab" else 0.0), 0.0, "sent", n * len(ds))
-        add("r", None, [], [land], 0.0, late, sem, n * len(ds), [k])
+        add("r", None, [], [land], late - REM, REM, sem, n * len(ds), [k])
 
     def issue():
         n = len(nodes)
@@ -204,7 +213,7 @@ def rank_program(g, core, T, topo):
                 users[j].append(k)
 
         def place(turns, back):
-            at, used = [0.0] * n, {q: [] for q in Q}
+            at, used = [0.0] * n, {q: [] for q in "vspgyr"}
             for k in turns:
                 e = nodes[k]
                 if back:
@@ -223,6 +232,65 @@ def rank_program(g, core, T, topo):
                 at[k] = t
             return at, max(at[k] + nodes[k]["hold"] + (0.0 if back else nodes[k]["late"]) for k in range(n))
 
+        def polish(turns, rng):
+            deps = [sorted(e["deps"] - e["soft"]) for e in nodes]
+            uses = [[] for k in range(n)]
+            for k in range(n):
+                for j in deps[k]:
+                    uses[j].append(k)
+            qs = [e["q"] for e in nodes]
+            cases = [([float(e["holds"][c]) for e in nodes], [float(e["lates"][c] + HOPS[c]) for e in nodes]) for c in range(len(HOPS))]
+
+            def run(turns):
+                total, pairs = 0.0, []
+                for hold, late in cases:
+                    done, why, free = [0.0] * n, [-1] * n, {}
+                    for k in turns:
+                        t, w = free.get(qs[k], (0.0, -1))
+                        for j in deps[k]:
+                            if done[j] > t:
+                                t, w = done[j], j
+                        why[k] = w
+                        free[qs[k]] = (t + hold[k], k)
+                        done[k] = t + hold[k] + late[k]
+                    k = max(range(n), key=lambda k: done[k])
+                    total += float(np.log(done[k]))
+                    while why[k] >= 0:
+                        if why[k] not in deps[k]:
+                            pairs.append((why[k], k))
+                        k = why[k]
+                return total, pairs
+
+            now, pairs = run(turns)
+            best, keep = now, turns
+            for step in range(STEPS):
+                x, y = pairs[int(rng.integers(len(pairs)))]
+                i, j = turns.index(x), turns.index(y)
+                mid = turns[i:j + 1]
+                if rng.random() < 0.5:
+                    move = {y}
+                    for k in reversed(mid):
+                        if k in move:
+                            move.update(deps[k])
+                    if x in move:
+                        continue
+                    mid = [k for k in mid if k in move] + [k for k in mid if k not in move]
+                else:
+                    move = {x}
+                    for k in mid:
+                        if k in move:
+                            move.update(uses[k])
+                    if y in move:
+                        continue
+                    mid = [k for k in mid if k not in move] + [k for k in mid if k in move]
+                other = turns[:i] + mid + turns[j + 1:]
+                total, found = run(other)
+                if total <= now + HEAT * (1.0 - step / STEPS) * rng.random():
+                    turns, now, pairs = other, total, found
+                    if now < best:
+                        best, keep = now, turns
+            return keep
+
         if not PLAN:
             start, best = place(sorted(range(n), key=lambda k: (-rest[k], k)), False)
             rng = np.random.default_rng(SEED)
@@ -237,10 +305,9 @@ def rank_program(g, core, T, topo):
                     now, end = place(sorted(range(n), key=lambda k: (-late[k] - nodes[k]["hold"], k)), False)
                 if end <= best:
                     start, best = now, end
-            PLAN.append(start)
-        start = PLAN[0]
+            PLAN.append(polish(sorted(range(n), key=lambda k: (start[k], k)), rng))
         cnt, seen = {}, {q: {} for q in Q}
-        for k in sorted(range(n), key=lambda k: (start[k], k)):
+        for k in PLAN[0]:
             e = nodes[k]
             q, sem = e["q"], e["sem"]
             if q != "r":
@@ -314,7 +381,7 @@ def rank_program(g, core, T, topo):
     iota(a("i16"), [[0, 8], [1, 16]], 0, 0)
     iota(a("R4"), [[0, 32], [1, 4]], 0, 0)
     iota(a("SG"), [[16, 8], [0, 16]], 0, 0)
-    iota(a("IO"), [[1, 16], [16, 32]], 0, 0)
+    iota(a("cs", 0, 512), [[1, 16], [16, 32]], 0, 0)
     iota(a("d12"), [[16, 16]], 2 * ODD, 0)
     mset(a("zz"), 0.0)
     p0 = a("pc", 0, 1)
@@ -399,9 +466,8 @@ def rank_program(g, core, T, topo):
     ts(a("sli"), a("sli"), col(3), A.add)
     ts(col(12), col(4), 1.0 - HP, A.mult, -1.0, A.add)
     ts(col(13), col(4), 127.0, A.mult, 1.0, A.add)
-    ts(a("col", 16, 24), a("it", 0, 8), col(6), A.is_equal, col(12), A.mult)
-    act(a("off"), a("col", 16, 24), F.Copy, scale=-1024.0)
-    ts(a("col", 24, 32), a("it", 0, 8), col(6), A.is_equal, col(13), A.mult)
+    act(col(11), col(12), F.Copy, scale=-1024.0)
+    ts(a("off"), a("it", 0, 8), col(6), A.is_equal)
     ts(a("Tj", 512, 1024), a("Tj", 0, 512), 4032, A.bitwise_and)
     cp(a("hb", 0, 512), a("Tj", 512, 1024))
     act(a("hb", 1024, 1536), a("hb", 0, 512), F.Identity, bias=float(ODD))
@@ -422,15 +488,23 @@ def rank_program(g, core, T, topo):
 
     cp(a("Ti"), a("Tc"))
     ts(a("Tj", 0, 512), a("Ti"), 2047, A.bitwise_and)
-    cp(a("Tb"), a("Tj", 0, 512))
+    ts(a("Tb"), a("Tj", 0, 512), col(13), A.mult)
     ts(a("Tl"), a("Tc"), 1.0 / 2048, A.mult, 1024.0, A.add)
+    ts(a("Ta"), a("Tl"), col(12), A.mult, col(11), A.add)
+    cp(a("n2", 0, 32), a("rq"))
+    ts(a("s2", 0, 32), a("n2", 0, 32), 9, A.arith_shift_right)
+    ts(a("s2", 32, 64), a("n2", 0, 32), 511, A.bitwise_and)
+    cp(a("qt"), a("s2", 0, 64))
+    act(a("dd"), ind(a("off"), a("qt", 0, 32)), F.Copy)
+    tt(a("G1"), ind(a("Ta"), a("qt", 32, 64)), a("dd"), A.mult)
+    tt(a("G2"), ind(a("Tb"), a("qt", 32, 64)), a("dd"), A.mult)
     chain[0] = "tables"
-    for q in range(N):
-        ts(a("T1", 512 * q, 512 * q + 512), a("Tl"), col(16 + q), A.mult, a("off", q, q + 1), A.add)
+    for q in range(2 * N):
+        o, x = a("T%d" % (1 + (q & 1)), 512 * (q >> 1), 512 * (q >> 1) + 512), a("Tb" if q & 1 else "Ta")
         if q < T2_ON_SCALAR:
-            act(a("T2", 512 * q, 512 * q + 512), a("Tb"), F.Copy, scale=col(24 + q))
+            act(o, x, F.Copy, scale=a("off", q >> 1, (q >> 1) + 1))
         else:
-            ts(a("T2", 512 * q, 512 * q + 512), a("Tb"), col(24 + q), A.mult)
+            ts(o, x, a("off", q >> 1, (q >> 1) + 1), A.mult)
     chain[0] = None
 
     mset(a("Ab", 0, RING * 648, 648), 0.0)
@@ -439,7 +513,7 @@ def rank_program(g, core, T, topo):
     for k in range(2):
         cp(a("ln", k, 32, 2), a("nn", 16 * k, 16 * k + 16))
     cp(a("SN"), ind(a("SL"), a("ln")))
-    act(a("NW"), ind(a("IO"), a("ln")), F.Copy)
+    act(a("NW"), ind(a("cs", 0, 512), a("ln")), F.Copy)
     ts(a("OM"), a("it"), col(3), A.is_equal)
     ts(a("R8"), a("it"), 1.0, A.min)
     ts(a("DG"), a("i16"), col(3), A.is_equal)
@@ -467,9 +541,10 @@ def rank_program(g, core, T, topo):
         W, sg = "W%d" % (rd & 1), "sg%d" % (rd & 1)
         for k in range(len(EARLY)):
             chain[0] = chain[0] if EARLY[k] else None
-        cp(a("G1"), ind(a("T1"), a("rq")))
-        chain[0] = None
-        act(a("G2"), ind(a("T2"), a("rq")), F.Copy)
+        if rd:
+            cp(a("G1"), ind(a("T1"), a("rq")))
+            chain[0] = None
+            act(a("G2"), ind(a("T2"), a("rq")), F.Copy)
         act(a(sg), a("G1"), F.Sign)
         scan(a("cum", 1, 513), a("G1"), a("c641"), -1.0, A.add, A.max)
         act(a("z"), a("G1"), F.Relu, bias=1.0)
@@ -529,12 +604,12 @@ def rank_program(g, core, T, topo):
                 cp(a("Hg", C * dl, C * dl + C), src)
             else:
                 act(a("Hg", C * dl, C * dl + C), src, F.Copy)
-        bank = a("PH%d" % ((ds[0] + 1) // 2 & 1), 0, 40 * len(ds))
+        bank = a("PH%d" % (ANSWERS.index(ds) & 1), 0, 40 * len(ds))
         pick(bank, "BA", "Hg", C * ds[0], C * (ds[-1] + 1))
         if ds == [SELF]:
             return cp(forty("PI", rd, ds), bank)
         cp(forty("PS", rd, ds), bank)
-        send(ds, -1, lambda dl: ap(forty("PS", rd, [dl])), lambda dl: ap(forty("PI", rd, [dl])), "a%d_%d" % (rd, GROUPS.index(ds)),
+        send(ds, -1, lambda dl: ap(forty("PS", rd, [dl])), lambda dl: ap(forty("PI", rd, [dl])), "a%d_%d" % (rd, ds[0]),
              forty("PS", rd, ds), forty("PI", rd, ds), REM + 16 * len(ds) * ROW)
 
     def phrases(rd, dl, slot, first, last):
@@ -617,10 +692,18 @@ def rank_program(g, core, T, topo):
         scan(a("k2", 128, 256), a("R16"), a("k2", 0, 128), 0.0, A.mult, A.add)
         act(a("nb"), a("k2", 143, 256, 16), F.Identity, bias=64.0, scale=-256.0)
         for c in range(8):
+            if c < REPEATS_ON_VECTOR:
+                x = a("x3", 64 * (c & 1), 64 * (c & 1) + 16 * c + 16)
+                ts(x, a("K", 0, 16 * c + 16), a("k2", 143 + 16 * c, 144 + 16 * c), A.subtract, 0.25, A.add)
+                least(a("fi", c, c + 1), x)
+                continue
             x = a("x1", 128 * (c & 1), 128 * (c & 1) + 16 * c + 16)
             act(x, a("K", 0, 16 * c + 16), F.Abs, bias=a("nb", c, c + 1), scale=256.0)
             act(x, x, F.Relu, bias=64.0 * 8192, scale=-8192.0, total=a("acc", c, c + 1))
+        if REPEATS_ON_VECTOR:
+            ts(a("acc", 0, REPEATS_ON_VECTOR), a("fi", 0, REPEATS_ON_VECTOR), 0.25, A.is_lt, 8192.0, A.mult)
         act(a("own"), a("k2", 143, 256, 16), F.Identity, bias=float(ODD))
+        last["repeats"] = len(nodes) - 2 - (REPEATS_ON_VECTOR > 0)
         tt(a("k3", 0, 8), a("acc"), a("k2", 143, 256, 16), A.add)
         tt(a("k3", 8, 16), a("acc"), a("own"), A.add)
         tt(a("k4"), a("k3"), a("d12"), A.min)
@@ -638,7 +721,9 @@ def rank_program(g, core, T, topo):
             barriers()
         chain[0] = "answer"
         for k, ds in enumerate(ANSWERS):
+            hush[0] = last["repeats"] if rd and k >= HUSH else None
             answer(rd, ds)
+            hush[0] = None
             if k == GATE:
                 wait_for = last["v", "answer"]
         chain[0], gate[0] = None, wait_for

@@ -1,3 +1,4 @@
+import math
 import numpy as np
 from concourse.bass import DstId, RemoteDMATransfer
 from concourse.mybir import AluOpType as A, AxisListType, ActivationFunctionType as F
@@ -9,7 +10,7 @@ GROUPS = [[0, 1], [2, 3], [4, 5], [6]]
 BATCH = [[0, 1], [2, 3, 4, 5], [6, 7]]
 ANSWERS = [[0, 1], [7], [2, 3], [4, 5], [6]]
 HEAP_ON_VECTOR = (0, 2, 4)
-SIGN_ON_VECTOR = (4,)
+ABSENT_ON_TENSOR = ()
 EARLY = [1]
 GATE = 3
 HUSH = 2
@@ -17,22 +18,24 @@ REPEATS_ON_VECTOR = 0
 T2_ON_SCALAR = 16
 ODD = 3072
 RING = 3
+BL = 672
 f32, bf, i32, u16, f16 = "float32", "bfloat16", "int32", "uint16", "float16"
 SB = {
-    "wp": (V, i32), "B": (2 * ODD + 256, f32), "hb": (1536, bf), "HW": (2 * HP, bf), "sli": (280, f32), "R40": (280, f32),
+    "wp": (V, i32), "B": (2 * ODD + 256, f32), "hb": (1024, bf), "HW": (2 * HP, bf), "sli": (252, f32), "R40": (252, f32),
     "DQ": (512, f32), "DH": (256, f32), "acc": (8, f32), "S256": (128, f32), "nb": (8, f32),
-    "W0": (5632, bf), "W1": (5632, bf), "gi": (64, i32), "gf": (64, f32), "m1": (128, i32), "m2": (128, i32),
-    "m3": (256, f32), "msg": (64, u16), "Tc": (512, u16), "Ti": (512, i32), "Tj": (1024, i32), "Tl": (512, f16),
+    "W0": (N * BL + 512, bf), "W1": (N * BL + 512, bf), "gi": (128, i32), "m2": (128, i32),
+    "msg": (64, u16), "Tc": (512, u16), "Ti": (512, i32), "Tj": (512, i32), "Tl": (512, f16),
     "off": (8, f32), "Ta": (512, bf), "qt": (64, u16),
     "Tb": (512, bf), "T1": (4096, bf), "T2": (4096, bf), "rn": (256, i32), "sn": (128, i32), "s2": (256, i32),
     "nn": (32, i32), "n2": (64, i32), "cn": (4, i32), "c2": (8, i32), "RL": (512, f32), "SL": (512, f32),
     "SN": (512, f32), "NW": (512, f32), "lr": (32, u16), "ls": (32, u16), "ln": (32, u16), "lc": (2, u16),
     "l4": (4, u16), "li": (72, f32), "zz": (1024, bf),
-    "pc": (16, i32), "col": (32, f32), "it": (512, f32), "i2": (288, f32), "i3": (128, f32), "i4": (64, f32),
-    "BA": (144, bf), "B2": (144, bf), "Be": (144, bf), "Bk": (144, bf), "Bh": (144, bf), "Bf": (144, f16),
+    "pc": (16, i32), "col": (32, f32), "it": (8, f32), "i3": (128, f32), "i4": (64, f32),
+    "BA": (144, bf), "B2": (144, bf), "Be": (144, bf), "Bg": (144, f16), "Bh": (144, bf), "Bf": (144, f16),
     "Bq": (144, bf), "Bl": (144, bf),
-    "BK": (144, f32), "BP": (144, f16), "SG": (128, f32), "TRI": (128, f32), "UP": (128, f32), "S4": (128, f32),
-    "S4n": (128, f32), "PM0": (128, f32), "PM1": (128, f32), "OM": (512, bf), "R8": (512, bf), "R4": (128, f32),
+    "BK": (144, f32), "BP": (144, f16), "SG": (128, f32), "TRI": (128, f32), "UP": (128, f32),
+    "PM0": (128, f32), "PM1": (128, f32), "R4": (128, f32), "Bn": (144, f32), "SO": (1024, f32),
+    "o4": (8, f32), "kq": (64, f32), "less": (128, f32), "Fs": (72, f32),
     "R16": (128, f32), "i16": (128, f32), "c641": (512, f16), "one": (640, bf),
     "c16": (320, bf), "dump": (32, f32), "DG": (128, f32), "ID": (16, f32), "kc": (64, f32), "nix": (128, f32),
     "d12": (16, f32), "neg": (256, f32),
@@ -41,16 +44,17 @@ SB = {
     "x1": (256, f32), "x2": (128, f32), "x3": (128, f32), "NWc": (64, f32), "SNo": (64, f32),
     "G1": (512, bf), "G2": (512, bf), "sg0": (512, bf), "sg1": (512, bf), "z": (512, bf), "cum": (520, f16), "mm": (512, f16),
     "Ff": (520, bf), "D": (512, bf), "o1": (32, f32), "o2": (32, f32), "pc1": (32, f32), "of": (32, u16),
-    "Y": (320, f32), "vi": (320, i32), "va": (320, i32), "E": (32, u16),
-    "RS": (3 * 320, u16), "RI": (3 * 320, u16), "PS": (3 * 320, u16), "PI": (3 * 320, u16),
+    "Y": (337, f32), "vi": (336, i32), "va": (336, i32), "E": (32, u16), "t3": (128, f32),
+    "RS": (3 * 336, u16), "RI": (3 * 320, u16), "PS": (3 * 320, u16), "PI": (3 * 320, u16),
     "Hg": (5120, bf), "WF": (328, f32), "Ab": (RING * 648, f32),
-    "d": (RING * C, bf), "ct": (RING * C, bf), "r": (RING * C, bf), "cs": (648, f32), "g1": (512, f32), "sc": (520, f32),
-    "key": (64, f32), "mx": (48, f32), "oh": (64, f32), "y": (640, f32), "DB": (648, f32), "dd": (512, bf),
+    "d": (RING * C, bf), "ct": (N * C, bf), "r": (RING * C, bf), "cs": (648, f32), "g1": (512, f32),
+    "key": (64, f32), "mx": (65, f32), "oh": (64, f32), "y": (640, bf), "DB": (648, bf), "dd": (512, bf),
     "en": (32, f32), "eu": (32, u16), "kl": (32, f32), "b1": (32, f32), "b2": (32, f32), "b3": (64, f32), "ow": (32, f32),
     "bi": (24, i32), "bu": (16, u16), "Mk": (128, f32), "Wd": (128, f32), "K": (128, f32),
     "k2": (256, f32), "own": (8, f32), "o256": (8, f32), "fi": (8, f32), "k3": (16, f32), "k4": (16, f32), "ku": (16, u16),
     "YT": (192, f32), "YB": (384, f32), "YW": (48, f32),
 }
+GUEST = {"nw": ("Ab", 656, 512), "m3": ("Ab", 1304, 384), "i2": ("cs", 8, 288), "rn0": ("Ab", 8, 512), "hp": ("Tj", 0, 512)}
 HOME, SCRATCH = {}, {}
 for _k, (_n, _t) in SB.items():
     _h = _k if _n > 600 else "all_" + _t
@@ -64,13 +68,15 @@ for _k in PSUM:
     HOME[_k] = (_k, 0)
 SEMAPHORES = (["v", "s", "p", "g", "sent", "tab"] + ["d%d" % k for k in range(1, 45)]
               + ["%s%d_%d" % (a, r, k) for a in "qa" for r in range(RO) for k in range(SELF)])
-CASES = np.array([[0.9e-3, 0.5e-3, 1.56, 3.8, 0.05, 0.08, 2.7, 0.7, 0.05],
-                  [0.85e-3, 0.43e-3, 1.25, 2.5, 0.04, 0.12, 3.0, 0.9, 0.08],
-                  [1.15e-3, 0.7e-3, 1.85, 5.0, 0.05, 0.06, 2.5, 0.7, 0.05]])
-CY, PE, GA, SC, FIX, HOPS, REM, ISS, ROW = CASES.T
-HOP, DMA, FIRST = 0.08, 2.0, 3.0
-SWEEPS, STEPS, HEAT, SEED = 100, 20000, 0.01, 5
+CASES = np.array([[0.9e-3, 0.55e-3, 1.56, 3.8, 0.05, 0.08, 2.0, 0.7, 0.04, 1.5, 30e3, 0.15],
+                  [0.85e-3, 0.62e-3, 1.2, 2.5, 0.04, 0.12, 1.5, 0.9, 0.02, 1.2, 50e3, 0.3],
+                  [1.15e-3, 0.7e-3, 1.85, 5.0, 0.05, 0.06, 2.7, 0.6, 0.06, 1.8, 16e3, 0.1]])
+CY, PE, GA, SC, FIX, HOPS, REM, ISS, ROW, DMA, RATE, PUT = CASES.T
+HOP, FIRST = 0.08, 3.0
+SIGN_ON_VECTOR, WIN_PE, ZFIRST, QP_V = (4,), 1, 1, 0
+SWEEPS, STEPS, HEAT, SEED = 15, 42000, 0.004, 5
 PLAN = []
+USE, SEEN, TRIES, REACH, PASSES, PARTS = 3, [], 8, 40, 10, 7
 
 
 def rank_program(g, core, T, topo):
@@ -78,9 +84,12 @@ def rank_program(g, core, T, topo):
     if me is None:
         return
     Q = {"v": g.vector, "s": g.scalar, "p": g.tensor, "g": g, "y": g.sync}
-    nodes, recs, nd, chain, last, gate, hush = [], {}, [0], [None], {}, [None], [None]
+    nodes, recs, nd, chain, last, gate, hush, sent = [], {}, [0], [None], {}, [None], [None], [0]
 
     def a(name, lo=0, hi=None, st=1, ps=None):
+        if name in GUEST:
+            host, at, n = GUEST[name]
+            return (host, at + lo, at + (n if hi is None else hi), st, ps)
         return (name, lo, (SB[name][0] if name in SB else 512) if hi is None else hi, st, ps)
 
     def ind(w, o):
@@ -101,7 +110,7 @@ def rank_program(g, core, T, topo):
     def two(x):
         return x[0] in SB and SB[x[0]][1] in (bf, u16, f16)
 
-    def add(q, fn, reads, writes, hold, late=0.0, sem=None, val=None, after=()):
+    def add(q, fn, reads, writes, hold, late=0.0, sem=None, val=None, after=(), eng=0.0):
         use = []
         for x in reads:
             if isinstance(x, tuple):
@@ -130,7 +139,8 @@ def rank_program(g, core, T, topo):
         if gate[0] is not None and q == "v":
             soft = soft | ({gate[0]} - deps)
         nodes.append({"q": q, "fn": fn, "deps": deps | soft, "soft": soft, "holds": hold + 0 * HOPS, "lates": late + 0 * HOPS,
-                      "hold": float((hold + 0 * HOPS)[0]), "late": float((late + 0 * HOPS)[0]), "sem": sem or q, "val": val})
+                      "hold": float((hold + 0 * HOPS)[0]), "late": float((late + eng + 0 * HOPS)[0]), "sem": sem or q, "val": val,
+                      "engs": eng + 0 * HOPS})
         return n
 
     def vec(fn, reads, o, per=1.0):
@@ -182,9 +192,11 @@ def rank_program(g, core, T, topo):
             return ins
         add("p", fn, [x for t in terms for x in t[:2]], [o], sum(max(64, width(t[1])) * (1 if two(t[0]) else 4) * PE for t in terms))
 
-    def dma(q, o, i, reads=(), writes=(), late=DMA):
+    def dma(q, o, i, size, rows=128, reads=(), writes=()):
         nd[0] += 1
-        add(q, lambda: Q[q].dma_start(ap(o), ap(i)), [i] + list(reads), [o] + list(writes), 0.1, late, "d%d" % nd[0], 16)
+        name = "d%d" % nd[0]
+        add(q, lambda: Q[q].dma_start(ap(o), ap(i)), [i] + list(reads), [o] + list(writes), PUT, DMA, name, 16,
+            eng=max(1, rows // 16) * ROW + rows * size / 16 / RATE)
 
     def send(ds, sign, src, dst, sem, read, land, late):
         trs, n = [], 0
@@ -197,8 +209,9 @@ def rank_program(g, core, T, topo):
             rid, pid = topo.addr(peer, core)
             trs.append(RemoteDMATransfer(dst_ids=[DstId(rid=rid, pnc=pid)], dma_engine_mask=sum(1 << e for e in es[k * n:(k + 1) * n]),
                                          remote_sem=T.sem[sem], src=src(dl), dst=dst(dl)))
-        k = add("g", lambda: g.remote_dma_fused(trs, local_sem=T.sem.sent), [read], [], ISS + (FIRST if sem == "tab" else 0.0), 0.0, "sent", n * len(ds))
-        add("r", None, [], [land], late - REM, REM, sem, n * len(ds), [k])
+        add("g", lambda: g.remote_dma_fused(trs, local_sem=T.sem.sent), [read], [land], ISS + (FIRST if sem == "tab" else 0.0), REM, sem,
+            n * len(ds), eng=late)
+        sent[0] += n * len(ds)
 
     def issue():
         n = len(nodes)
@@ -239,57 +252,197 @@ def rank_program(g, core, T, topo):
                 for j in deps[k]:
                     uses[j].append(k)
             qs = [e["q"] for e in nodes]
-            cases = [([float(e["holds"][c]) for e in nodes], [float(e["lates"][c] + HOPS[c]) for e in nodes]) for c in range(len(HOPS))]
+            cases = [([float(e["holds"][c]) for e in nodes], [float(e["lates"][c] + HOPS[c]) for e in nodes],
+                      [float(e["engs"][c]) for e in nodes]) for c in range(len(HOPS))]
+            moves = [bool(e["engs"][0]) for e in nodes]
+            needs = [[j for j in deps[k] if qs[j] + qs[k] != "pp"] for k in range(n)]
+            feeds = [[j for j in uses[k] if qs[j] + qs[k] != "pp"] for k in range(n)]
 
-            def run(turns):
-                total, pairs = 0.0, []
-                for hold, late in cases:
-                    done, why, free = [0.0] * n, [-1] * n, {}
-                    for k in turns:
-                        t, w = free.get(qs[k], (0.0, -1))
-                        for j in deps[k]:
+            def run(turns, first, known, cases, lo=0, hi=n, far=None):
+                total, pairs, state, ends, mover = 0.0, [], [], {}, -1
+                inside = turns[lo:hi]
+                for k in reversed(turns[:first]):
+                    if qs[k] not in ends:
+                        ends[qs[k]] = k
+                    if mover < 0 and moves[k]:
+                        mover = k
+                    if mover >= 0 and len(ends) == len(Q):
+                        break
+                rest = turns[first:hi]
+                for c, ((hold, late, eng), old) in enumerate(zip(cases, known)):
+                    done, why, out, behind = (list(x) for x in old[:4])
+                    free = {q: (out[ends[q]], ends[q]) if q in ends else (0.0, -1) for q in Q}
+                    busy = (done[mover] - late[mover], mover) if mover >= 0 else (0.0, -1)
+                    for k in rest:
+                        t, w = free[qs[k]]
+                        for j in needs[k]:
                             if done[j] > t:
                                 t, w = done[j], j
                         why[k] = w
-                        free[qs[k]] = (t + hold[k], k)
-                        done[k] = t + hold[k] + late[k]
-                    k = max(range(n), key=lambda k: done[k])
-                    total += float(np.log(done[k]))
-                    while why[k] >= 0:
-                        if why[k] not in deps[k]:
-                            pairs.append((why[k], k))
-                        k = why[k]
-                return total, pairs
+                        t += hold[k]
+                        out[k] = t
+                        free[qs[k]] = (t, k)
+                        if moves[k]:
+                            behind[k] = -1
+                            if busy[0] > t:
+                                t, behind[k] = busy
+                            t += eng[k]
+                            busy = (t, k)
+                        done[k] = t + late[k]
+                    landed = True
+                    if far is None:
+                        end = max(done)
+                        k = done.index(end)
+                    else:
+                        beyond, exits = far[c]
+                        end, k = max((done[k] + beyond[k], k) for k in inside)
+                        for q, t in exits.items():
+                            u = busy if q == "e" else free[q]
+                            if u[0] + t > end:
+                                end, k, landed = u[0] + t, u[1], q == "e"
+                    total += math.log(end)
+                    path = set()
+                    state.append((done, why, out, behind, path, end))
+                    while k >= 0 and spot[k] >= lo:
+                        path.add(k)
+                        j = behind[k] if landed and behind[k] >= 0 else why[k]
+                        landed = j in sets[k]
+                        if j >= 0 and not landed and spot[j] >= lo:
+                            pairs.append((j, k))
+                        landed = landed or j == behind[k]
+                        k = j
+                return total, pairs, state
 
-            now, pairs = run(turns)
-            best, keep = now, turns
-            for step in range(STEPS):
-                x, y = pairs[int(rng.integers(len(pairs)))]
-                i, j = turns.index(x), turns.index(y)
-                mid = turns[i:j + 1]
-                if rng.random() < 0.5:
-                    move = {y}
-                    for k in reversed(mid):
-                        if k in move:
-                            move.update(deps[k])
-                    if x in move:
-                        continue
-                    mid = [k for k in mid if k in move] + [k for k in mid if k not in move]
-                else:
-                    move = {x}
+            sets = [set(d) for d in deps]
+            blank = [([0.0] * n, [-1] * n, [0.0] * n, [-1] * n)] * len(cases)
+            every = cases
+            SEEN.append(lambda turns: run(turns, 0, blank, every)[2])
+            cases = cases[:USE]
+
+            def tails(turns, last, known, lo=0):
+                state, ends, mover = [], {}, n
+                for k in turns[last + 1:]:
+                    if qs[k] not in ends:
+                        ends[qs[k]] = k
+                    if mover == n and moves[k]:
+                        mover = k
+                    if mover < n and len(ends) == len(Q):
+                        break
+                head = turns[lo:last + 1][::-1]
+                for (hold, late, eng), old in zip(cases, known):
+                    tail, turn = list(old[0]), list(old[1])
+                    free = {q: tail[ends[q]] if q in ends else 0.0 for q in Q}
+                    busy = turn[mover]
+                    for k in head:
+                        t = 0.0
+                        for j in feeds[k]:
+                            if tail[j] > t:
+                                t = tail[j]
+                        t += late[k]
+                        if moves[k]:
+                            busy = turn[k] = t = max(t, busy) + eng[k]
+                        free[qs[k]] = tail[k] = max(t, free[qs[k]]) + hold[k]
+                    state.append((tail, turn))
+                return state
+
+            def guess(turns, i, j, mid):
+                before, after, mine, total = {}, {}, set(mid), 0.0
+                want = set(qs[k] for k in mid)
+                if any(moves[k] for k in mid):
+                    want.add("e")
+                for side, out in ((turns[i - 1::-1] if i else [], before), (turns[j + 1:], after)):
+                    for k in side:
+                        if qs[k] not in out:
+                            out[qs[k]] = k
+                        if moves[k] and "e" not in out:
+                            out["e"] = k
+                        if want <= out.keys():
+                            break
+                for (hold, late, eng), (done, why, out, behind, path, was), (tail, turn) in zip(cases, known, rear):
+                    free = {q: out[before[q]] if q in before else 0.0 for q in want}
+                    busy = done[before["e"]] - late[before["e"]] if "e" in before else 0.0
+                    new, end = {}, was if path.isdisjoint(mine) else 0.0
                     for k in mid:
-                        if k in move:
-                            move.update(uses[k])
-                    if y in move:
-                        continue
-                    mid = [k for k in mid if k not in move] + [k for k in mid if k in move]
-                other = turns[:i] + mid + turns[j + 1:]
-                total, found = run(other)
-                if total <= now + HEAT * (1.0 - step / STEPS) * rng.random():
-                    turns, now, pairs = other, total, found
+                        t = free[qs[k]]
+                        for u in needs[k]:
+                            u = new[u] if u in new else done[u]
+                            if u > t:
+                                t = u
+                        free[qs[k]] = t = t + hold[k]
+                        if moves[k]:
+                            busy = t = max(t, busy) + eng[k]
+                        new[k] = t = t + late[k]
+                        far = 0.0
+                        for u in feeds[k]:
+                            if tail[u] > far and u not in mine:
+                                far = tail[u]
+                        if t + far > end:
+                            end = t + far
+                    for q in want:
+                        if q in after:
+                            end = max(end, busy + turn[after[q]] if q == "e" else free[q] + tail[after[q]])
+                    total += math.log(end)
+                return total
+
+            best, keep, spot, each = 1e9, turns, {}, STEPS // (PASSES * PARTS)
+            draws = rng.random((STEPS, TRIES, 4)).tolist()
+            for step in range(each * PASSES * PARTS):
+                if step % each == 0:
+                    part = step // each % PARTS
+                    spot.update((k, i) for i, k in enumerate(turns))
+                    now, pairs, known = run(turns, 0, blank, cases)
                     if now < best:
                         best, keep = now, turns
-            return keep
+                    if part == 0:
+                        turns = sorted(turns, key=lambda k: (known[0][2][k] - cases[0][0][k], spot[k]))
+                        spot.update((k, i) for i, k in enumerate(turns))
+                        now, pairs, known = run(turns, 0, blank, cases)
+                    rear = tails(turns, n - 1, [([0.0] * (n + 1), [0.0] * (n + 1))] * len(cases))
+                    lo, hi = n * part // (PARTS + 1), n * (part + 2) // (PARTS + 1)
+                    exits = {}
+                    for k in turns[hi:]:
+                        exits.setdefault(qs[k], k)
+                        if moves[k]:
+                            exits.setdefault("e", k)
+                    far = [({k: max([tail[u] for u in feeds[k] if spot[u] >= hi] + [0.0]) for k in turns[lo:hi]},
+                            {q: (turn if q == "e" else tail)[k] for q, k in exits.items()}) for tail, turn in rear]
+                    now, pairs, known = run(turns, lo, known, cases, lo, hi, far)
+                tried = []
+                for pair, way, reach, tie in draws[step] if pairs else []:
+                    x, y = pairs[int(pair * len(pairs))]
+                    i, j = spot[x], spot[y]
+                    reach = int(reach ** 3 * REACH)
+                    if way < 0.5:
+                        i = max(lo, i - reach)
+                        mid, move = turns[i:j + 1], {y}
+                        for k in reversed(mid):
+                            if k in move:
+                                move.update(deps[k])
+                        if x in move:
+                            continue
+                        mid = [k for k in mid if k in move] + [k for k in mid if k not in move]
+                    else:
+                        j = min(hi - 1, j + reach)
+                        mid, move = turns[i:j + 1], {x}
+                        for k in mid:
+                            if k in move:
+                                move.update(uses[k])
+                        if y in move:
+                            continue
+                        mid = [k for k in mid if k not in move] + [k for k in mid if k in move]
+                    tried.append((guess(turns, i, j, mid), tie, i, j, mid))
+                limit = now + HEAT * (1.0 - step / STEPS) * draws[step][0][3]
+                if not tried or min(tried)[0] > limit:
+                    continue
+                i, j, mid = min(tried)[2:]
+                other = turns[:i] + mid + turns[j + 1:]
+                total, found, state = run(other, i, known, cases, lo, hi, far)
+                if total <= limit:
+                    turns, now, pairs, known = other, total, found, state
+                    rear = tails(turns, j, rear, lo)
+                    for u, k in enumerate(mid):
+                        spot[k] = i + u
+            return turns if run(turns, 0, blank, cases)[0] < best else keep
 
         if not PLAN:
             start, best = place(sorted(range(n), key=lambda k: (-rest[k], k)), False)
@@ -306,22 +459,22 @@ def rank_program(g, core, T, topo):
                 if end <= best:
                     start, best = now, end
             PLAN.append(polish(sorted(range(n), key=lambda k: (start[k], k)), rng))
-        cnt, seen = {}, {q: {} for q in Q}
+        cnt, seen = {"sent": sent[0]}, {q: {} for q in Q}
         for k in PLAN[0]:
             e = nodes[k]
             q, sem = e["q"], e["sem"]
-            if q != "r":
-                need = {}
-                for j in e["deps"] - e["soft"]:
-                    if not (q == "p" and nodes[j]["q"] == "p"):
-                        need[nodes[j]["sem"]] = max(need.get(nodes[j]["sem"], 0), nodes[j]["at"])
-                for s, val in need.items():
-                    if seen[q].get(s, 0) < val:
-                        Q[q].wait_ge(T.sem[s], val)
-                        seen[q][s] = val
-                ins = e["fn"]()
-                if sem != "sent":
-                    ins.then_inc(T.sem[sem], e["val"] or 1)
+            need = {}
+            for j in e["deps"] - e["soft"]:
+                if not (q == "p" and nodes[j]["q"] == "p"):
+                    need[nodes[j]["sem"]] = max(need.get(nodes[j]["sem"], 0), nodes[j]["at"])
+            for s, val in need.items():
+                if seen[q].get(s, 0) < val:
+                    Q[q].wait_ge(T.sem[s], val)
+                    seen[q][s] = val
+            ins = e["fn"]()
+            SEEN.append((k, e, ins))
+            if q != "g" or sem == "g":
+                ins.then_inc(T.sem[sem], e["val"] or 1)
             cnt[sem] = cnt.get(sem, 0) + (e["val"] or 1)
             e["at"] = cnt[sem]
         for s, val in cnt.items():
@@ -347,90 +500,91 @@ def rank_program(g, core, T, topo):
     def col(k):
         return a("col", k, k + 1)
 
-    def zero(name, n):
-        chain[0] = "zero"
-        for lo in range(0, n, 1024):
-            act(a(name, lo, lo + 1024), a("zz"), F.Copy)
-        chain[0] = None
-
     row0 = slice(0, 128, 16)
 
-    dma("y", a("gi", 0, 32), T.gst[:])
-    dma("s", a("gi", 32, 64), T.gln[:])
+    dma("y", a("gi", 0, 64, ps=slice(0, 64)), T.gst[:], 256, 64)
+    dma("s", a("gi", 64, 128, ps=slice(0, 64)), T.gln[:], 256, 64)
     for k in range(2):
-        dma("y", a("sn", 64 * k, 64 * k + 64), T.sens[k::2, :])
-        dma("s", a("rn", 128 * k, 128 * k + 128), T.rel[k::2, :])
-        dma("y", a("nn", 16 * k, 16 * k + 16), T.nxt[:, 256 * k:256 * k + 256])
-    dma("y", a("cn", 0, 1), T.cur[:])
-    dma("s", a("Tj", 0, 512), T.heap[:])
-    dma("y", a("wp", 0, 1536), T.wpos[:, 0:1536], late=6.0)
-    dma("s", a("wp", 1536, V), T.wpos[:, 1536:V], late=6.0)
+        dma("y", a("sn", 64 * k, 64 * k + 64), T.sens[k::2, :], 256)
+        dma("s", a("rn", 128 * k, 128 * k + 128), T.rel[k::2, :], 512)
+        dma("y", a("nn", 16 * k, 16 * k + 16), T.nxt[:, 256 * k:256 * k + 256], 64)
+    dma("y", a("cn", 0, 1), T.cur[:], 4)
+    dma("y", a("hp"), T.heap[:], 2048)
+    for lo in range(0, V, 1024):
+        dma("y", a("wp", lo, min(V, lo + 1024)), T.wpos[:, lo:min(V, lo + 1024)], 4096)
 
     iota(a("pc", 0, 1), [[1, 1]], 0, 1)
-    iota(a("i3"), [[16, 8], [0, 2], [2, 8]], 0, 0)
+    iota(a("i3"), [[8, 8], [64, 2], [1, 8]], 0, -1)
     iota(a("i2", 0, 144), [[1, 144]], -15, 0)
     iota(a("i2", 144, 288), [[1, 144]], -8, 0)
     iota(a("li", 0, 32), [[8, 16], [128, 2]], 0, 0)
     iota(a("li", 32, 64), [[4, 16], [64, 2]], 0, 0)
-    iota(a("li", 64, 68), [[4, 4]], 0, 0)
+    iota(a("li", 64, 68), [[4, 4]], 1, 0)
     iota(a("i4"), [[0, 16], [1, 4]], 0, 0)
-    iota(a("it"), [[0, 64], [1, 8]], 0, 0)
-    iota(a("sli"), [[0, 7], [16, 40]], 0, 0)
-    iota(a("dump"), [[16, 32]], 5120, 0)
+    iota(a("it"), [[1, 8]], 0, 0)
+    iota(a("sli"), [[0, 6], [16, 42]], 0, 0)
+    iota(a("dump"), [[16, 32]], N * BL, 0)
+    for name in ("Ff", "cs", "DB", "Fs", "mx", "WF", "Y"):
+        iota(a(name, 0, 1), [[0, 1]], 0, 0)
+    for k in range(RING):
+        iota(a("Ab", 648 * k, 648 * k + 1), [[0, 1]], 0, 0)
     iota(a("nix"), [[1, 128]], 0, 0)
     iota(a("i16"), [[0, 8], [1, 16]], 0, 0)
     iota(a("R4"), [[0, 32], [1, 4]], 0, 0)
     iota(a("SG"), [[16, 8], [0, 16]], 0, 0)
-    iota(a("cs", 0, 512), [[1, 16], [16, 32]], 0, 0)
+    iota(a("nw"), [[1, 16], [16, 32]], 0, 0)
+    iota(a("one"), [[0, 640]], 1, 0)
     iota(a("d12"), [[16, 16]], 2 * ODD, 0)
     mset(a("zz"), 0.0)
     p0 = a("pc", 0, 1)
     cp(col(0), p0)
-    ts(col(1), p0, -1.0, A.add)
-    ts(a("PM0"), a("i3"), col(0), A.is_equal)
-    ts(a("PM1"), a("i3"), col(1), A.is_equal)
+    ts(a("PM0"), a("i3"), 0.0, A.is_equal)
+    ts(a("PM1"), a("i3"), 64.0, A.is_equal)
     for k, m in ((2, 112), (3, 15), (4, 8), (6, 7), (7, 119), (8, 3), (9, 12)):
         ts(a("pc", k, k + 1), p0, m, A.bitwise_and)
         ts(col(k), a("pc", k, k + 1), {4: 0.125, 9: 0.25}.get(k, 1.0), A.mult)
     ts(col(5), col(4), -1.0, A.mult, 1.0, A.add)
     chain[0] = "zero"
-    for lo in range(0, 5120, 640):
-        iota(a("W0", lo, lo + 640), [[0, 640]], 0, 0)
-    zero("HW", 2 * HP)
+    for lo in range(0, N * BL, BL):
+        iota(a("W0", lo, lo + BL), [[0, BL]], 0, 0)
+    ts(col(16), col(3), 3.0, A.is_equal)
+    ts(col(17), col(3), 2.0, A.is_equal, float(ODD), A.mult)
+    tt(col(17), col(17), col(16), A.add)
+    for lo in range(0, 2 * HP, 1024):
+        act(a("HW", lo, lo + 1024), a("zz"), F.Identity, bias=col(16 + lo // HP))
+    chain[0] = None
 
-    cp(a("gf"), a("gi"))
-    for k in range(4):
-        mm(a("PM", 32 * k, 32 * k + 32), [(a("PM%d" % (k & 1)), a("gf", 32 * (k >> 1), 32 * (k >> 1) + 32))])
-    cp(a("m1"), a("PM", 0, 128))
-    st, ln = a("m1", 0, 64), a("m1", 64, 128)
-    ts(a("m2", 0, 64), st, 127, A.bitwise_and)
-    ts(a("m2", 64, 128), st, 7, A.arith_shift_right)
-    ts(a("m3", 128, 192), ln, 1.0, A.min)
-    ts(a("m3", 192, 256), ln, col(5), A.mult, 2049.0, A.mult)
-    ts(a("m3", 64, 128), a("m2", 64, 128), 2048.0, A.add, col(4), A.mult)
-    ts(a("m3", 0, 64), a("m2", 0, 64), col(5), A.mult)
-    tt(a("m3", 0, 64), a("m3", 0, 64), a("m3", 64, 128), A.add)
-    tt(a("m3", 0, 64), a("m3", 0, 64), a("m3", 128, 192), A.mult)
-    tt(a("m3", 0, 64), a("m3", 0, 64), a("m3", 192, 256), A.add)
-    cp(a("msg"), a("m3", 0, 64))
+    def low(name, k):
+        return a(name, 64 * k, 64 * k + 64, ps=slice(0, 64))
+
+    ts(low("m2", 0), low("gi", 0), 127, A.bitwise_and)
+    ts(low("m3", 2), low("gi", 1), 1.0, A.min)
+    ts(low("m2", 1), low("gi", 0), 7, A.arith_shift_right)
+    ts(low("m3", 3), low("gi", 1), 2049.0, A.mult)
+    tt(low("m3", 4), low("m2", 0), low("m3", 2), A.mult)
+    ts(low("m3", 5), low("m2", 1), 2048.0, A.add)
+    tt(low("m3", 0), low("m3", 4), low("m3", 3), A.add)
+    tt(low("m3", 1), low("m3", 5), low("m3", 2), A.mult)
+    mm(a("PM", 0, 64), [(a("PM%d" % k, ps=slice(0, 64)), low("m3", k)) for k in range(2)])
+    cp(a("msg"), a("PM", 0, 64))
     own = ("DT", SELF, N, 1, None)
-    dma("y", T.DT[SELF], a("msg"), writes=[own])
-    send(list(range(SELF)), -1, lambda dl: T.DT[SELF], lambda dl: T.DT[dl], "tab", own, ("DT", 0, SELF, 1, None), REM + 1.0)
+    dma("y", T.DT[SELF], a("msg"), 128, writes=[own])
+    send(list(range(SELF)), -1, lambda dl: T.DT[SELF], lambda dl: T.DT[dl], "tab", own, ("DT", 0, SELF, 1, None), ROW + 16384 / RATE)
     for dl in range(N):
-        dma("ys"[dl & 1], a("Tc", ps=slice(dl, 128, 8)), T.DT[dl], reads=[("DT", dl, dl + 1, 1, None)])
+        dma("ys"[~dl & 1], a("Tc", ps=slice(dl, 128, 8)), T.DT[dl], 1024, 16, reads=[("DT", dl, dl + 1, 1, None)])
         recs["Tc"], recs["Tc%d" % dl] = [], recs["Tc"]
     recs["Tc"] = [e for dl in range(N) for e in recs["Tc%d" % dl]]
 
     ts(a("lr"), a("li", 0, 32), col(6), A.add)
     ts(a("ls"), a("li", 32, 64), col(8), A.add)
-    ts(a("l4"), a("li", 64, 68), col(9), A.add)
+    ts(a("l4"), a("li", 64, 68), col(9), A.add, 4.0, A.mult)
     colf(128, a("sn"), "s2")
     cp(a("g1"), ind(a("sn"), a("ls")))
     turn(a("SL"), a("g1"))
     ts(a("rn"), a("rn"), float(512 * (SELF - me)), A.add)
     ts(a("rn"), a("rn"), 4095, A.bitwise_and)
-    cp(a("y", 0, 512), ind(a("rn"), a("lr")))
-    turn(a("RL"), a("y", 0, 512))
+    cp(a("rn0"), ind(a("rn"), a("lr")))
+    turn(a("RL"), a("rn0"))
     colf(1, a("cn", 0, 1), "c2")
     cp(a("lc", 0, 1), a("cn", 0, 1))
     act(a("kc"), a("i4"), F.Identity, bias=3.0, scale=-1.0)
@@ -446,10 +600,10 @@ def rank_program(g, core, T, topo):
     squeeze(a("PX1", 32, 64), "t1", 0, 64, 2)
     cp(a("rq"), a("PX1", 32, 64))
 
-    ts(col(10), col(5), 1024.0, A.mult)
-    ts(col(14), col(6), -float(C), A.mult, col(5), A.mult)
+    ts(col(14), col(6), -1.0 / HP, A.mult, col(4), A.mult)
     ts(col(15), col(5), -1.0, A.mult)
-    for name, w in (("Bf", col(5)), ("Bk", col(10)), ("BA", 1.0), ("B2", 2.0), ("Be", 0.5), ("Bh", col(4)), ("Bq", col(14)), ("Bl", col(15))):
+    for name, w in (("Bf", col(5)), ("BA", 1.0), ("B2", 2.0), ("Be", 0.5), ("Bh", col(4)), ("Bq", col(14)), ("Bl", col(15)), ("Bg", col(15)),
+                    ("Bn", -1.0 / BIG)):
         ts(a(name), a("i2", 0, 144), col(2), A.is_equal, w, A.mult)
     ts(a("BK"), a("i2", 144, 288), col(7), A.is_equal)
     ts(a("BP"), a("i2", 144, 288), col(7), A.is_equal, col(5), A.mult)
@@ -458,33 +612,36 @@ def rank_program(g, core, T, topo):
     tt(a("TRI"), a("TRI"), a("SG"), A.mult)
     tt(a("UP"), a("SG"), a("TRI"), A.subtract)
     ts(a("dump"), a("dump"), col(3), A.add)
-    mset(a("c641"), -641.0)
-    mset(a("one"), 1.0)
-    mset(a("cum", 0, 1), -1.0)
-    mset(a("Ff", 0, 1), 0.0)
-    ts(a("R40"), a("sli"), 1.0, A.min)
+    mset(a("c641"), 1023.0 - C)
+    mset(a("cum", 0, 1), 1023.0)
+    ts(a("R40"), a("sli"), BL - 16.0, A.is_lt)
     ts(a("sli"), a("sli"), col(3), A.add)
     ts(col(12), col(4), 1.0 - HP, A.mult, -1.0, A.add)
     ts(col(13), col(4), 127.0, A.mult, 1.0, A.add)
     act(col(11), col(12), F.Copy, scale=-1024.0)
     ts(a("off"), a("it", 0, 8), col(6), A.is_equal)
-    ts(a("Tj", 512, 1024), a("Tj", 0, 512), 4032, A.bitwise_and)
-    cp(a("hb", 0, 512), a("Tj", 512, 1024))
-    act(a("hb", 1024, 1536), a("hb", 0, 512), F.Identity, bias=float(ODD))
-    ts(a("Ti"), a("Tj", 0, 512), 63, A.bitwise_and)
-    ts(a("hb", 512, 1024), a("Ti"), 1.0, A.add)
-    for lo, (p, x) in zip((0, 0, HP, HP), ((0, 0), (1, 512), (0, 1024), (1, 512))):
-        dma("y", a("HW", lo, lo + HP, ps=slice(p, 128, 16)), a("hb", x, x + 512), late=3.0)
+    cp(a("hb", 0, 512), a("hp"))
+    tt(a("hb", 512, 1024), a("hp"), a("hb", 0, 512), A.subtract)
+    for lo, (p, x) in zip((0, 0, HP, HP), ((0, 0), (1, 512), (0, 0), (1, 512))):
+        dma("y", a("HW", lo, lo + HP, ps=slice(p, 128, 16)), a("hb", x, x + 512), 1024)
         if p == 0:
             keep = recs["HW"].pop()
         else:
             recs["HW"].append(keep)
 
-    mset(a("B", 0, 1), -5.0)
-    mset(a("B", V + 1, ODD + 1), -5.0)
-    for lo in range(0, V, 760):
-        ts(a("B", 1 + lo, 761 + lo), a("wp", lo, lo + 760), 4.0, A.mult, -5.0, A.add)
-        act(a("B", ODD + 1 + lo, ODD + 761 + lo), a("B", 1 + lo, 761 + lo), F.Identity, bias=-0.5)
+    gone = -BIG if ABSENT_ON_TENSOR else -5.0
+    mset(a("B", 0, 1), gone)
+    mset(a("B", V + 1, ODD + 1), gone)
+    for lo in range(0, V, 512):
+        hi, bank = min(V, lo + 512), "Z%d" % (lo // 512 & 1)
+        if ABSENT_ON_TENSOR:
+            ts(a(bank, 0, hi - lo), a("wp", lo, hi), 0.5, A.is_lt, -BIG, A.mult)
+            tt(a("B", 1 + lo, 1 + hi), a("wp", lo, hi), a(bank, 0, hi - lo), A.add)
+        else:
+            ts(a("B", 1 + lo, 1 + hi), a("wp", lo, hi), 4.0, A.mult, -5.0, A.add)
+    for lo in range(0, V, 1024):
+        hi = min(V, lo + 1024)
+        act(a("B", ODD + 1 + lo, ODD + 1 + hi), a("B", 1 + lo, 1 + hi), F.Identity, bias=0.5 if ABSENT_ON_TENSOR else -0.5)
 
     cp(a("Ti"), a("Tc"))
     ts(a("Tj", 0, 512), a("Ti"), 2047, A.bitwise_and)
@@ -507,35 +664,43 @@ def rank_program(g, core, T, topo):
             ts(o, x, a("off", q >> 1, (q >> 1) + 1), A.mult)
     chain[0] = None
 
-    mset(a("Ab", 0, RING * 648, 648), 0.0)
-    mset(a("WF", 0, 1), 0.0)
     colf(32, a("nn"), "n2")
     for k in range(2):
         cp(a("ln", k, 32, 2), a("nn", 16 * k, 16 * k + 16))
     cp(a("SN"), ind(a("SL"), a("ln")))
-    act(a("NW"), ind(a("cs", 0, 512), a("ln")), F.Copy)
-    ts(a("OM"), a("it"), col(3), A.is_equal)
-    ts(a("R8"), a("it"), 1.0, A.min)
+    act(a("NW"), ind(a("nw"), a("ln")), F.Copy)
     ts(a("DG"), a("i16"), col(3), A.is_equal)
     ts(a("ID"), a("i16", 0, 16), col(3), A.is_equal)
     ts(a("R16"), a("i16"), 1.0, A.min)
     ts(a("R4"), a("R4"), 1.0, A.min)
-    act(a("S4"), a("SG"), F.Copy, scale=4.0)
-    act(a("S4n"), a("SG"), F.Copy, scale=-4.0)
+    if WIN_PE:
+        ts(a("o4"), a("it", 0, 8), col(3), A.is_equal, 4.0, A.mult)
+        for o in range(N):
+            act(a("SO", 128 * o, 128 * o + 128), a("SG"), F.Copy, scale=a("o4", o, o + 1))
+        scan(a("kq"), a("one", 0, 64), a("kc"), 0.0, A.mult, A.add)
+        act(a("kq"), a("kq"), F.Copy, scale=0.25)
+    else:
+        iota(a("SO", 0, 512), [[0, 64], [1, 8]], 0, 0)
+        ts(a("OM"), a("SO", 0, 512), col(3), A.is_equal)
+        ts(a("R8"), a("SO", 0, 512), 1.0, A.min)
+        act(a("SO", 640, 768), a("SG"), F.Copy, scale=4.0)
+        act(a("SO", 768, 896), a("SG"), F.Copy, scale=-4.0)
     act(a("S256"), a("nix"), F.Copy, scale=1.0 / 4096)
+    act(a("less"), a("nix"), F.Identity, bias=-1.0 / 16, scale=0.0)
     act(a("i3"), a("nix"), F.Identity, bias=1.0, scale=1.0 / 256)
     act(a("d12"), a("d12"), F.Identity, bias=col(3))
-    mset(a("neg"), -5.0)
-    mset(a("c16"), 8.0)
+    mset(a("neg"), gone)
+    ts(a("fi"), a("it", 0, 8), col(3), A.is_equal, 8.0, A.mult)
+    mset(col(18), 8.0)
+    for dl in ABSENT_ON_TENSOR:
+        tt(col(18), col(18), a("fi", dl, dl + 1), A.add)
     for dl in SIGN_ON_VECTOR:
-        ts(a("fi", 0, 1), col(3), float(dl), A.not_equal)
-        ts(a("c16"), a("c16"), a("fi", 0, 1), A.mult)
-    mset(a("cs", 0, 1), 0.0)
-    mset(a("DB", 0, 1), 0.0)
-    mset(a("sc", 0, 8), 0.0)
+        tt(col(18), col(18), a("fi", dl, dl + 1), A.subtract)
+    act(a("c16"), a("zz", 0, 320), F.Identity, bias=col(18))
 
     def forty(name, rd, ds):
-        return a(name, 320 * rd + 40 * ds[0], 320 * rd + 40 * (ds[-1] + 1))
+        w = 42 if name == "RS" else 40
+        return a(name, w * (N * rd + ds[0]), w * (N * rd + ds[-1]) + 40)
 
     def requests(rd):
         W, sg = "W%d" % (rd & 1), "sg%d" % (rd & 1)
@@ -544,16 +709,36 @@ def rank_program(g, core, T, topo):
         if rd:
             cp(a("G1"), ind(a("T1"), a("rq")))
             chain[0] = None
+            if ZFIRST == 1:
+                act(a("z"), ind(a("T1"), a("rq")), F.Relu, bias=1.0)
+            if ZFIRST == 2:
+                act(a(sg), ind(a("T1"), a("rq")), F.Sign)
             act(a("G2"), ind(a("T2"), a("rq")), F.Copy)
-        act(a(sg), a("G1"), F.Sign)
-        scan(a("cum", 1, 513), a("G1"), a("c641"), -1.0, A.add, A.max)
-        act(a("z"), a("G1"), F.Relu, bias=1.0)
-        pick(a("PM", 0, 32), "Bk", sg, 0, 512, True, False)
-        pick(a("PH0", 0, 32), "Bq", sg, 0, 512)
-        tt(a("mm"), a("cum", 0, 512), a(sg), A.mult)
-        pick(a("PM", 0, 32), "Bf", "mm", 0, 512, False, True)
+        if ZFIRST == 0 or (ZFIRST == 2 and not rd):
+            act(a(sg), a("G1"), F.Sign)
+        if ZFIRST != 1 or not rd:
+            act(a("z"), a("G1"), F.Relu, bias=1.0)
+        scan(a("cum", 1, 513), a("G1"), a("c641"), 1023.0, A.add, A.max)
+        if ZFIRST == 1:
+            tt(a("mm"), a("cum", 0, 512), a("z"), A.mult)
+            pick(a("PM", 0, 32), "Bg", "cum", 0, 512, True, False)
+            pick(a("PM", 0, 32), "Bf", "mm", 0, 512, False, True)
+        else:
+            tt(a("mm"), a("cum", 0, 512), a(sg), A.mult)
+            pick(a("PM", 0, 32), "Bf", "mm", 0, 512)
         scan(a("Ff", 1, 513), a("z"), a("G2"), 0.0, A.mult, A.add)
-        act(a("qp"), a("PH0", 0, 32), F.Identity, bias=1023.0)
+        if ZFIRST == 1:
+            act(a(sg), a("z"), F.Identity, bias=-1.0)
+        if QP_V:
+            if rd:
+                cp(a("n2", 0, 32), a("rq"))
+                ts(a("s2", 0, 32), a("n2", 0, 32), 9, A.arith_shift_right)
+            ts(a("qp"), a("s2", 0, 32), float(BL), A.mult, 1023.0, A.add)
+            act(a("qo"), a("qp"), F.Identity, bias=-1023.0 * C / BL, scale=C / BL)
+        else:
+            pick(a("Z1", 128, 160), "Bq", "G1", 0, 512)
+            act(a("qp"), a("Z1", 128, 160), F.Identity, bias=1023.0, scale=float(BL))
+            act(a("qo"), a("Z1", 128, 160), F.Copy, scale=float(C))
         tt(a("D"), a("Ff", 1, 513), a("Ff", 0, 512), A.subtract)
         tt(a("o2"), a("PM", 0, 32), a("qp"), A.add)
         ts(a("o1"), a("PM", 0, 32), C - 1023.5, A.is_gt, 8192.0, A.mult)
@@ -562,25 +747,24 @@ def rank_program(g, core, T, topo):
         cp(a("of"), a("o2"))
         tt(ind(a(W), a("of")), a("D"), a("G1"), A.add)
         for k, ds in enumerate(BATCH):
-            bank, lo, hi = "PX%d" % (k % 3), 40 * ds[0], 40 * (ds[-1] + 1)
-            pick(a(bank, 0, hi - lo), "BA", W, C * ds[0], C * (ds[-1] + 1))
-            scan(a("Y", lo, hi), a("R40", 0, hi - lo), a(bank, 0, hi - lo), 0.0, A.mult, A.add)
-            mm(a(bank, 256, 256 + hi - lo), [(a("TRI"), a("Y", lo, hi))]
-               + [(a("UP"), a("Y", x, x + 39), a(bank, 257 + x - lo, 296 + x - lo)) for x in range(lo, hi, 40)])
+            bank, lo, hi = "PX%d" % (k % 3), 42 * ds[0], 42 * (ds[-1] + 1)
+            pick(a(bank, 0, hi - lo), "BA", W, BL * ds[0], BL * (ds[-1] + 1))
+            scan(a("Y", 1 + lo, 1 + hi), a("R40", 0, hi - lo), a(bank, 0, hi - lo), 0.0, A.mult, A.add)
+            hi -= 2
+            mm(a(bank, 256, 256 + hi - lo), [(a("TRI"), a("Y", 1 + lo, 1 + hi)), (a("UP"), a("Y", lo, hi))])
             tt(a("vi", lo, hi), a(bank, 256, 256 + hi - lo), a("sli", 0, hi - lo), A.add)
             ts(a("va", lo, hi), a("vi", lo, hi), 2 * HP - 1, A.bitwise_and)
             cp(forty("RS", rd, ds), a("va", lo, hi))
             for j, to in enumerate(GROUPS):
                 if to[0] in ds:
                     send(to, 1, lambda dl: ap(forty("RS", rd, [dl])), lambda dl: ap(forty("RI", rd, [dl])), "q%d_%d" % (rd, j),
-                         forty("RS", rd, to), forty("RI", rd, to), REM + 16 * len(to) * ROW)
+                         forty("RS", rd, to), forty("RI", rd, to), 16 * len(to) * ROW)
 
     def ends(rd):
         act(a("pc1"), a("PM", 0, 32), F.Identity, bias=1023.0)
-        act(a("qo"), a("qp"), F.Identity, bias=-1023.0)
         mm(a("PM", 64, 96), [(a("BP", 8, 136), a("cum", 8, 513, 16)), (a("BP", 0, 128), a("cum", 16, 513, 16))])
         pick(a("PM", 96, 128), "Bl", "G1", 0, 512)
-        ts(a("E"), a("PM", 64, 96), -1.0, A.mult, -1.0, A.add)
+        ts(a("E"), a("PM", 64, 96), -1.0, A.mult, 1023.0, A.add)
         tt(a("b3", 0, 32), a("PM", 96, 128), a("pc1"), A.add)
         ts(a("en"), a("b3", 0, 32), float(C), A.min)
         cp(a("eu"), a("en"))
@@ -610,36 +794,48 @@ def rank_program(g, core, T, topo):
             return cp(forty("PI", rd, ds), bank)
         cp(forty("PS", rd, ds), bank)
         send(ds, -1, lambda dl: ap(forty("PS", rd, [dl])), lambda dl: ap(forty("PI", rd, [dl])), "a%d_%d" % (rd, ds[0]),
-             forty("PS", rd, ds), forty("PI", rd, ds), REM + 16 * len(ds) * ROW)
+             forty("PS", rd, ds), forty("PI", rd, ds), 16 * len(ds) * ROW)
 
     def phrases(rd, dl, slot, first, last):
         lo, x0 = C * slot, 648 * slot
         hi, src = lo + C, ind(a("B", 0, ODD + V + 1), forty("PI", rd, [dl]))
-        act(a("Ab", x0 + 1, x0 + 641), src, F.Abs, bias=4.0)
-        tt(a("ct", lo, hi), src, a("Ab", x0, x0 + C), A.is_equal)
+        act(a("Ab", x0 + 1, x0 + 641), src, F.Abs, bias=1.0 if ABSENT_ON_TENSOR else 4.0)
+        ct = a("ct", C * dl, C * dl + C)
+        tt(ct, src, a("Ab", x0, x0 + C), A.is_equal)
         if dl in SIGN_ON_VECTOR:
-            ts(a("d", lo, hi), a("Ab", x0 + 1, x0 + 641), 2.0, A.is_gt, 2.0, A.mult)
-        else:
+            ts(a("d", lo, hi), a("Ab", x0 + 1, x0 + 641), *((float(2 ** 30), A.is_lt) if ABSENT_ON_TENSOR else (2.0, A.is_gt)), 2.0, A.mult)
+        elif not ABSENT_ON_TENSOR:
             act(a("d", lo, hi), a("Ab", x0 + 1, x0 + 641), F.Sign, bias=-2.0)
-        scan(a("r", lo, hi), a("ct", lo, hi), a("ct", lo, hi), 0.0, A.mult, A.add)
+        elif dl not in ABSENT_ON_TENSOR:
+            act(a("d", lo, hi), a("Ab", x0 + 1, x0 + 641), F.Sign, bias=float(2 ** 30), scale=-1.0)
+        scan(a("r", lo, hi), ct, ct, 0.0, A.mult, A.add)
         for k in range(2):
-            x, y = lo + 320 * k, lo + 320 * k + 320
-            mm(a("Z%d" % k, 0, 320), [(band("BA", 8 + dl), a("ct", x, y)), (band("Be", dl), a("d", x, y))], first, False)
+            if dl in ABSENT_ON_TENSOR:
+                x = x0 + 1 + 320 * k
+                mm(a("Z%d" % k, 0, 320), [(band("Bn", dl), a("Ab", x, x + 320))], first, False)
+            else:
+                mm(a("Z%d" % k, 0, 320), [(band("Be", dl), a("d", lo + 320 * k, lo + 320 * k + 320))], first, False)
         for k in range(2):
             mm(a("Z%d" % k, 0, 320), [(band("B2", dl), a("r", lo + 320 * k, lo + 320 * k + 320))], False, last)
 
     def winner(rd):
+        if WIN_PE:
+            mm(a("PM", 128, 192), [(a("SO", 0, 128), a("kq"))], True, False)
         scan(a("cs", 1, 321), a("c16"), a("Z0", 0, 320), 0.0, A.add, A.add)
         scan(a("cs", 321, 641), a("c16"), a("Z1", 0, 320), a("cs", 320, 321), A.add, A.add)
-        for k in range(2):
-            act(a("y", 320 * k, 320 * k + 320), a("Z%d" % k, 0, 320), F.Relu, bias=9216.0, scale=-1024.0)
-        tt(a("g1"), ind(a("cs", 0, 641), a("E")), a("OM"), A.mult)
-        scan(a("sc", 8, 520), a("R8"), a("g1"), 0.0, A.mult, A.add)
-        mm(a("PM", 128, 192), [(a("S4"), a("sc", 15, 520, 8)), (a("S4n"), a("sc", 7, 512, 8))])
-        tt(a("key"), a("PM", 128, 192), a("kc"), A.add)
-        tt(a("mx", 16, 48), a("key", 0, 64, 2), a("key", 1, 64, 2), A.max)
-        tt(a("mx", 0, 16), a("mx", 16, 48, 2), a("mx", 17, 48, 2), A.max)
-        tt(a("oh"), ind(a("mx", 0, 16), a("l4")), a("key"), A.is_equal)
+        if WIN_PE:
+            cp(a("g1", 0, 256), ind(a("cs", 0, 641), a("E", 0, 16)))
+            act(a("g1", 256, 512), ind(a("cs", 0, 641), a("E", 16, 32)), F.Copy)
+            mm(a("PM", 128, 192), [(a("SO", 128 * o, 128 * o + 128), a("g1", o, 512, 8)) for o in range(N)], False, True)
+            cp(a("Fs", 1, 65), a("PM", 128, 192))
+            tt(a("key"), a("PM", 128, 192), a("Fs", 0, 64), A.subtract)
+        else:
+            tt(a("g1"), ind(a("cs", 0, 641), a("E")), a("OM"), A.mult)
+            scan(a("SO", 8, 520), a("R8"), a("g1"), 0.0, A.mult, A.add)
+            mm(a("PM", 128, 192), [(a("SO", 640, 768), a("SO", 15, 520, 8)), (a("SO", 768, 896), a("SO", 7, 512, 8))])
+            tt(a("key"), a("PM", 128, 192), a("kc"), A.add)
+        scan(a("mx", 1, 65), a("R4", 0, 64), a("key"), 0.0, A.mult, A.max)
+        tt(a("oh"), ind(a("mx"), a("l4")), a("key"), A.is_equal)
         if rd + 1 < RO:
             for k in range(2):
                 tt(a("u2", 64 * k, 64 * k + 64), a("PX0", 64 * k, 64 * k + 64), a("oh"), A.mult)
@@ -649,26 +845,34 @@ def rank_program(g, core, T, topo):
 
     def results(rd):
         shown(rd)
-        act(a("YT", 64 * rd, 64 * rd + 64), a("PM", 128, 192), F.Copy, scale=0.25)
+        for k in range(4):
+            act(a("YT", 64 * rd + k, 64 * rd + 64, 4), a("key", k, 64, 4), F.Identity, bias=(k - 3) / 4, scale=0.25)
+        w = 128 if rd + 1 < RO else 64
         tt(a("t2", 0, 64), a("NWc"), a("oh"), A.mult)
-        mm(a("PX1", 64, 80), [(a("SG"), a("t2", k, 64, 4)) for k in range(4)])
-        act(a("YW", 16 * rd, 16 * rd + 16), a("PX1", 64, 80), F.Copy, scale=1.0 / 16)
         if rd + 1 < RO:
             tt(a("t2", 64, 128), a("SNo"), a("oh"), A.mult)
-            squeeze(a("PX1", 96, 100), "t2", 64, 128, 4, 4, 4)
+        scan(a("t3", 0, w), a("R4", 0, w), a("t2", 0, w), 0.0, A.mult, A.add)
+        act(a("YW", 16 * rd, 16 * rd + 16), a("t3", 3, 64, 4), F.Copy)
+        if rd + 1 < RO:
+            squeeze(a("PX1", 96, 100), "t3", 67, 128, 4, 4)
             cp(a("sl"), a("PX1", 96, 100))
 
     def distances(rd):
+        for dl in [SELF] + list(range(SELF)):
+            for k in range(2):
+                mm(a("PH%d" % k, 0, 320), [(band("BA", 8 + dl), a("ct", C * dl + 320 * k, C * dl + 320 * k + 320))], dl == SELF, dl == SELF - 1)
+        for k in range(2):
+            act(a("y", 320 * k, 320 * k + 320), a("PH%d" % k, 0, 320), F.Relu, bias=9216.0, scale=-1024.0)
         scan(a("DB", 1, 641), a("one"), a("y"), 0.0, A.add, A.min)
         tt(a("dd"), ind(a("DB", 0, 641), a("eu")), a("sg%d" % (rd & 1)), A.mult)
 
     def barrier_words(rd):
         pick(a("Z0", 0, 32), "Bh", "dd", 0, 512)
-        squeeze(a("Z0", 64, 96), "oh", 0, 64, 2)
+        squeeze(a("Z1", 64, 96), "oh", 0, 64, 2)
         tt(a("b1"), a("Z0", 0, 32), a("kl"), A.is_gt)
         tt(a("b2"), a("Z0", 0, 32), a("en"), A.add)
-        tt(a("b1"), a("b1"), a("Z0", 64, 96), A.mult)
-        tt(a("b2"), a("b2"), a("b1"), A.mult)
+        tt(a("b1"), a("b1"), a("b2"), A.mult)
+        tt(a("b2"), a("b1"), a("Z1", 64, 96), A.mult)
         cp(a("WF", 1, 321), forty("PI", rd, [0, SELF]))
         mm(a("Z1", 32, 40), [(a("BK", 8 - 8 * (k >> 1), 136 - 8 * (k >> 1)), a("b2", k, 32, 4)) for k in range(4)])
         ts(a("bi", 0, 8), a("Z1", 32, 40), 15.0, A.add)
@@ -677,15 +881,14 @@ def rank_program(g, core, T, topo):
         cp(a("bu"), a("bi", 8, 24))
         act(a("Mk"), ind(a("ID"), a("bu", 0, 8)), F.Copy)
         tt(a("Wd"), ind(a("WF", 0, 321), a("bu", 8, 16)), a("Mk"), A.mult)
-        mm(a("Z1", 256, 384), [(a("SG"), a("S256"))] * (rd + 1 < RO) + [(a("SG"), a("Wd"))])
-        ts(a("x2"), a("Z1", 256, 384), ODD + 0.75, A.is_gt, -float(ODD), A.mult)
-        tt(a("K"), a("Z1", 256, 384), a("x2"), A.add)
+        mm(a("Z0", 256, 384), [(a("SG"), a("S256" if rd + 1 < RO else "less"))], True, False)
+        mm(a("Z0", 256, 384), [(a("SG"), a("Wd"))], False, True)
+        ts(a("x2"), a("Z0", 256, 384), ODD - 0.25, A.is_gt, -float(ODD), A.mult)
+        tt(a("K") if rd + 1 < RO else a("YB", 128 * rd, 128 * rd + 128), a("Z0", 256, 384), a("x2"), A.add)
 
     def shown(rd):
         if rd + 1 < RO:
             tt(a("YB", 128 * rd, 128 * rd + 128), a("K"), a("i3"), A.subtract)
-        else:
-            act(a("YB", 128 * rd, 128 * rd + 128), a("K"), F.Identity, bias=-1.0)
 
     def barriers():
         tt(a("k2", 0, 128), a("K"), a("DG"), A.mult)
@@ -713,8 +916,8 @@ def rank_program(g, core, T, topo):
     slot = 0
     for rd in range(RO):
         if rd + 1 < RO:
-            for lo in range(0, 5120, 1024):
-                dma("y", a("W%d" % (~rd & 1), lo, lo + 1024), a("zz"), reads=[a("cs" if rd else "Tb")], late=4.0)
+            for lo in range(0, N * BL, 896):
+                dma("y", a("W%d" % (~rd & 1), lo, lo + 896), a("zz", 0, 896), 1792, reads=[a("cs", 1) if rd else a("Tb")])
         requests(rd)
         if rd:
             barrier_words(rd - 1)
@@ -742,7 +945,7 @@ def rank_program(g, core, T, topo):
     chain[0] = None
     barrier_words(RO - 1)
     results(RO - 1)
-    dma("y", T.yb[:], a("YB", ps=row0))
-    dma("s", T.yt[:], a("YT", ps=row0))
-    dma("y", T.yw[:], a("YW", ps=row0))
+    dma("y", T.yb[:], a("YB", ps=row0), 1536, 8)
+    dma("s", T.yt[:], a("YT", ps=row0), 768, 8)
+    dma("y", T.yw[:], a("YW", ps=row0), 192, 8)
     issue()

@@ -7,9 +7,9 @@ N, V, HP, C, RO = 8, 3040, 8192, 640, 3
 BIG = float(2 ** 60)
 SELF = N - 1
 GROUPS = [[0, 1], [2, 3], [4, 5], [6]]
-BATCH = [[0, 1], [2, 3, 4, 5], [6, 7]]
+BATCH = [[0, 1], [2, 3], [4, 5], [6, 7]]
 ANSWERS = [[0, 1], [7], [2, 3], [4, 5], [6]]
-HEAP_ON_VECTOR = (0, 2, 4)
+HEAP_ON_VECTOR = (0, 2, 4, 6)
 ABSENT_ON_TENSOR = ()
 EARLY = [1]
 GATE = 3
@@ -21,7 +21,7 @@ RING = 3
 BL = 672
 f32, bf, i32, u16, f16 = "float32", "bfloat16", "int32", "uint16", "float16"
 SB = {
-    "wp": (V, i32), "B": (2 * ODD + 256, f32), "hb": (1024, bf), "HW": (2 * HP, bf), "sli": (252, f32), "R40": (252, f32),
+    "wp": (V, i32), "B": (2 * ODD + 256, f32), "hb": (1024, bf), "HW": (2 * HP, bf), "sli": (252, f32), "R40": (252, bf),
     "DQ": (512, f32), "DH": (256, f32), "acc": (8, f32), "S256": (128, f32), "nb": (8, f32),
     "W0": (N * BL + 512, bf), "W1": (N * BL + 512, bf), "gi": (128, i32), "m2": (128, i32),
     "msg": (64, u16), "Tc": (512, u16), "Ti": (512, i32), "Tj": (512, i32), "Tl": (512, f16),
@@ -31,12 +31,11 @@ SB = {
     "SN": (512, f32), "NW": (512, f32), "lr": (32, u16), "ls": (32, u16), "ln": (32, u16), "lc": (2, u16),
     "l4": (4, u16), "li": (72, f32), "zz": (1024, bf),
     "pc": (16, i32), "col": (32, f32), "it": (8, f32), "i3": (128, f32), "i4": (64, f32),
-    "BA": (144, bf), "B2": (144, bf), "Be": (144, bf), "Bg": (144, f16), "Bh": (144, bf), "Bf": (144, f16),
-    "Bq": (144, bf), "Bl": (144, bf),
-    "BK": (144, f32), "BP": (144, f16), "SG": (128, f32), "TRI": (128, f32), "UP": (128, f32),
-    "PM0": (128, f32), "PM1": (128, f32), "R4": (128, f32), "Bn": (144, f32), "SO": (1024, f32),
-    "o4": (8, f32), "kq": (64, f32), "less": (128, f32), "Fs": (72, f32),
-    "R16": (128, f32), "i16": (128, f32), "c641": (512, f16), "one": (640, bf),
+    "BA": (144, bf), "B4": (144, bf), "Bh": (144, bf), "Bf": (144, f16), "Bl": (144, bf),
+    "BK": (144, f16), "BP": (144, f16), "SG": (128, f32), "TRI": (128, f32), "UP": (128, f32),
+    "PM0": (128, f32), "PM1": (128, f32), "R4": (256, bf), "SO": (640, f32), "OM": (256, bf), "BQ": (144, f16), "g2": (256, f32),
+    "du": (512, bf), "kq": (64, f32), "less": (128, f32), "Fs": (72, f32),
+    "R16": (128, bf), "i16": (128, f32), "c641": (512, f16), "one": (640, bf),
     "c16": (320, bf), "dump": (32, f32), "DG": (128, f32), "ID": (16, f32), "kc": (64, f32), "nix": (128, f32),
     "d12": (16, f32), "neg": (256, f32),
     "sl": (4, u16), "sq": (16, u16), "rq": (32, u16), "qo": (32, f32), "qp": (32, f32),
@@ -50,11 +49,12 @@ SB = {
     "d": (RING * C, bf), "ct": (N * C, bf), "r": (RING * C, bf), "cs": (648, f32), "g1": (512, f32),
     "key": (64, f32), "mx": (65, f32), "oh": (64, f32), "y": (640, bf), "DB": (648, bf), "dd": (512, bf),
     "en": (32, f32), "eu": (32, u16), "kl": (32, f32), "b1": (32, f32), "b2": (32, f32), "b3": (64, f32), "ow": (32, f32),
-    "bi": (24, i32), "bu": (16, u16), "Mk": (128, f32), "Wd": (128, f32), "K": (128, f32),
+    "bi": (96, i32), "bh": (64, f16), "two": (128, f32), "bu": (16, u16), "Mk": (128, f32), "Wd": (128, f32), "K": (128, f32),
     "k2": (256, f32), "own": (8, f32), "o256": (8, f32), "fi": (8, f32), "k3": (16, f32), "k4": (16, f32), "ku": (16, u16),
     "YT": (192, f32), "YB": (384, f32), "YW": (48, f32),
 }
-GUEST = {"nw": ("Ab", 656, 512), "m3": ("Ab", 1304, 384), "i2": ("cs", 8, 288), "rn0": ("Ab", 8, 512), "hp": ("Tj", 0, 512)}
+GUEST = {"nw": ("Ab", 656, 512), "m3": ("Ab", 1304, 384), "i2": ("cs", 8, 288), "rn0": ("Ab", 8, 512), "hp": ("Tj", 0, 512),
+         "o4": ("cs", 304, 256)}
 HOME, SCRATCH = {}, {}
 for _k, (_n, _t) in SB.items():
     _h = _k if _n > 600 else "all_" + _t
@@ -66,17 +66,18 @@ PSUM = ["Z0", "Z1", "PX0", "PX1", "PX2", "PH0", "PH1", "PM"]
 for _k in PSUM:
     SCRATCH[_k] = ("psum", [128, 512], f32)
     HOME[_k] = (_k, 0)
-SEMAPHORES = (["v", "s", "p", "g", "sent", "tab"] + ["d%d" % k for k in range(1, 45)]
-              + ["%s%d_%d" % (a, r, k) for a in "qa" for r in range(RO) for k in range(SELF)])
+SEMAPHORES = (["v", "s", "p", "g", "sent", "tab"] + ["d%d" % k for k in range(1, 70)]
+              + ["%s%d_%d" % (a, r, k) for a in "qa" for r in range(RO) for k in range(N)])
 CASES = np.array([[0.9e-3, 0.55e-3, 1.56, 3.8, 0.05, 0.08, 2.0, 0.7, 0.04, 1.5, 30e3, 0.15],
                   [0.85e-3, 0.62e-3, 1.2, 2.5, 0.04, 0.12, 1.5, 0.9, 0.02, 1.2, 50e3, 0.3],
                   [1.15e-3, 0.7e-3, 1.85, 5.0, 0.05, 0.06, 2.7, 0.6, 0.06, 1.8, 16e3, 0.1]])
 CY, PE, GA, SC, FIX, HOPS, REM, ISS, ROW, DMA, RATE, PUT = CASES.T
 HOP, FIRST = 0.08, 3.0
-SIGN_ON_VECTOR, WIN_PE, ZFIRST, QP_V = (4,), 1, 1, 0
-SWEEPS, STEPS, HEAT, SEED = 15, 42000, 0.004, 5
+SIGN_ON_VECTOR, ZFIRST, QP_V, MARK_ON_SCALAR, DD_S, WHOLE = (), 1, 1, 0, 0, 1.5 * 2 ** 23
+IN_HALVES, W0_BY_COPY, HW_BY_COPY = (6,), 0, (3, 3)
+SWEEPS, STEPS, HEAT, SEED = 15, 59400, 0.02, 5
 PLAN = []
-USE, SEEN, TRIES, REACH, PASSES, PARTS = 3, [], 8, 40, 10, 7
+USE, SEEN, TRIES, REACH, PASSES, PARTS = 3, [], 4, 40, 20, 11
 
 
 def rank_program(g, core, T, topo):
@@ -185,6 +186,9 @@ def rank_program(g, core, T, topo):
         kw = {} if SB[o[0]][1] == i32 else {"allow_small_or_imprecise_dtypes": True}
         add("g", lambda: g.iota(ap(o), pat, base, ch, **kw), [], [o], 0.15 + 2 * width(o) * CY)
 
+    def keep_where(o, i, pat, f, base, ch):
+        add("g", lambda: g.affine_select(ap(o), ap(i), pat, f, 0.0, base, ch), [i], [o], 0.19 + 2 * width(o) * CY)
+
     def mm(o, terms, start=True, stop=True):
         def fn():
             for k, t in enumerate(terms):
@@ -201,7 +205,7 @@ def rank_program(g, core, T, topo):
     def send(ds, sign, src, dst, sem, read, land, late):
         trs, n = [], 0
         for k, dl in enumerate(ds):
-            peer = T.cores[(me + sign * (dl + 1)) % N]
+            peer = T.cores[(me + sign * (dl - SELF)) % N]
             es = topo.engines(core, peer)
             n = 1
             while 2 * n * len(ds) <= len(es):
@@ -530,11 +534,24 @@ def rank_program(g, core, T, topo):
         iota(a("Ab", 648 * k, 648 * k + 1), [[0, 1]], 0, 0)
     iota(a("nix"), [[1, 128]], 0, 0)
     iota(a("i16"), [[0, 8], [1, 16]], 0, 0)
-    iota(a("R4"), [[0, 32], [1, 4]], 0, 0)
     iota(a("SG"), [[16, 8], [0, 16]], 0, 0)
     iota(a("nw"), [[1, 16], [16, 32]], 0, 0)
     iota(a("one"), [[0, 640]], 1, 0)
     iota(a("d12"), [[16, 16]], 2 * ODD, 0)
+    iota(a("two"), [[0, 128]], 2, 0)
+    iota(a("neg"), [[0, 256]], -1, 0)
+    if MARK_ON_SCALAR:
+        add("s", lambda: g.scalar.activation(ap(a("neg")), ap(a("neg")), F.Tanh), [a("neg")], [a("neg")], 1.3 + 256 * CY + FIX)
+    else:
+        act(a("neg"), a("neg"), F.Copy, scale=0.625)
+    iota(a("o4"), [[0, 64], [1, 4]], 0, 0)
+    iota(a("B", 0, 1), [[0, 1]], -5, 0)
+    iota(a("B", V + 1, ODD + 1), [[0, ODD - V]], -5, 0)
+    keep_where(a("R4"), a("one", 0, 256), [[0, 64], [1, 4]], A.is_gt, 0, 0)
+    keep_where(a("R16"), a("one", 0, 128), [[0, 8], [1, 16]], A.is_gt, 0, 0)
+    keep_where(a("R40"), a("one", 0, 252), [[0, 6], [-1, 42]], A.is_gt, 41, 0)
+    for o in range(4):
+        keep_where(a("SO", 128 * o, 128 * o + 128), a("two"), [[-16, 8], [0, 16]], A.is_equal, -4 - o, 1)
     mset(a("zz"), 0.0)
     p0 = a("pc", 0, 1)
     cp(col(0), p0)
@@ -546,12 +563,18 @@ def rank_program(g, core, T, topo):
     ts(col(5), col(4), -1.0, A.mult, 1.0, A.add)
     chain[0] = "zero"
     for lo in range(0, N * BL, BL):
-        iota(a("W0", lo, lo + BL), [[0, BL]], 0, 0)
+        if lo // BL < W0_BY_COPY:
+            dma("y", a("W0", lo, lo + BL), a("zz", 0, BL), 2 * BL)
+        else:
+            iota(a("W0", lo, lo + BL), [[0, BL]], 0, 0)
     ts(col(16), col(3), 3.0, A.is_equal)
     ts(col(17), col(3), 2.0, A.is_equal, float(ODD), A.mult)
     tt(col(17), col(17), col(16), A.add)
     for lo in range(0, 2 * HP, 1024):
-        act(a("HW", lo, lo + 1024), a("zz"), F.Identity, bias=col(16 + lo // HP))
+        if lo % HP >= HP - 1024 * HW_BY_COPY[lo // HP]:
+            dma("y", a("HW", lo, lo + 1024), a("HW", lo - lo % HP, lo - lo % HP + 1024), 2048)
+        else:
+            act(a("HW", lo, lo + 1024), a("zz"), F.Identity, bias=col(16 + lo // HP))
     chain[0] = None
 
     def low(name, k):
@@ -567,11 +590,11 @@ def rank_program(g, core, T, topo):
     tt(low("m3", 1), low("m3", 5), low("m3", 2), A.mult)
     mm(a("PM", 0, 64), [(a("PM%d" % k, ps=slice(0, 64)), low("m3", k)) for k in range(2)])
     cp(a("msg"), a("PM", 0, 64))
-    own = ("DT", SELF, N, 1, None)
+    own, peers = ("DT", N, N + 1, 1, None), [dl for dl in range(N) if dl != SELF]
     dma("y", T.DT[SELF], a("msg"), 128, writes=[own])
-    send(list(range(SELF)), -1, lambda dl: T.DT[SELF], lambda dl: T.DT[dl], "tab", own, ("DT", 0, SELF, 1, None), ROW + 16384 / RATE)
+    send(peers, -1, lambda dl: T.DT[SELF], lambda dl: T.DT[dl], "tab", own, ("DT", 0, N, 1, None), ROW + 16384 / RATE)
     for dl in range(N):
-        dma("ys"[~dl & 1], a("Tc", ps=slice(dl, 128, 8)), T.DT[dl], 1024, 16, reads=[("DT", dl, dl + 1, 1, None)])
+        dma("ys"[~dl & 1], a("Tc", ps=slice(dl, 128, 8)), T.DT[dl], 1024, 16, reads=[own if dl == SELF else ("DT", 0, N, 1, None)])
         recs["Tc"], recs["Tc%d" % dl] = [], recs["Tc"]
     recs["Tc"] = [e for dl in range(N) for e in recs["Tc%d" % dl]]
 
@@ -581,13 +604,13 @@ def rank_program(g, core, T, topo):
     colf(128, a("sn"), "s2")
     cp(a("g1"), ind(a("sn"), a("ls")))
     turn(a("SL"), a("g1"))
-    ts(a("rn"), a("rn"), float(512 * (SELF - me)), A.add)
+    ts(a("rn"), a("rn"), float(512 * (N + SELF - me)), A.add)
     ts(a("rn"), a("rn"), 4095, A.bitwise_and)
     cp(a("rn0"), ind(a("rn"), a("lr")))
     turn(a("RL"), a("rn0"))
     colf(1, a("cn", 0, 1), "c2")
     cp(a("lc", 0, 1), a("cn", 0, 1))
-    act(a("kc"), a("i4"), F.Identity, bias=3.0, scale=-1.0)
+    act(a("kc"), a("i4"), F.Identity, bias=1.5, scale=-0.5)
     ts(a("i4", 0, 4), a("i4", 0, 4), col(9), A.is_equal)
     for d in range(4):
         ts(a("DQ", 128 * d, 128 * d + 128), a("nix"), col(0), A.is_equal, a("i4", d, d + 1), A.mult)
@@ -600,21 +623,21 @@ def rank_program(g, core, T, topo):
     squeeze(a("PX1", 32, 64), "t1", 0, 64, 2)
     cp(a("rq"), a("PX1", 32, 64))
 
-    ts(col(14), col(6), -1.0 / HP, A.mult, col(4), A.mult)
-    ts(col(15), col(5), -1.0, A.mult)
-    for name, w in (("Bf", col(5)), ("BA", 1.0), ("B2", 2.0), ("Be", 0.5), ("Bh", col(4)), ("Bq", col(14)), ("Bl", col(15)), ("Bg", col(15)),
-                    ("Bn", -1.0 / BIG)):
+    ts(col(15), col(4), -1.0, A.add)
+    for name, w in (("Bf", col(5)), ("BA", 1.0), ("B4", 4.0), ("Bh", col(4)), ("Bl", col(15))):
         ts(a(name), a("i2", 0, 144), col(2), A.is_equal, w, A.mult)
     ts(a("BK"), a("i2", 144, 288), col(7), A.is_equal)
-    ts(a("BP"), a("i2", 144, 288), col(7), A.is_equal, col(5), A.mult)
+    ts(col(1), col(0), 4.0, A.add)
+    ts(a("BP"), a("i2", 144, 288), col(1), A.is_equal, a("i4", 0, 1), A.mult)
+    ts(a("BQ"), a("i2", 144, 288), col(0), A.is_equal, a("i4", 1, 2), A.mult)
+    ts(a("OM"), a("o4"), col(3), A.is_equal)
     ts(a("SG"), a("SG"), col(2), A.is_equal)
-    ts(a("TRI"), a("nix"), col(0), A.is_ge)
-    tt(a("TRI"), a("TRI"), a("SG"), A.mult)
-    tt(a("UP"), a("SG"), a("TRI"), A.subtract)
+    act(a("SO", 512, 640), a("SG"), F.Copy, scale=2.0)
+    keep_where(a("TRI"), a("SG"), [[1, 128]], A.is_ge, 0, -1)
+    keep_where(a("UP"), a("SG"), [[-1, 128]], A.is_gt, 0, 1)
     ts(a("dump"), a("dump"), col(3), A.add)
     mset(a("c641"), 1023.0 - C)
     mset(a("cum", 0, 1), 1023.0)
-    ts(a("R40"), a("sli"), BL - 16.0, A.is_lt)
     ts(a("sli"), a("sli"), col(3), A.add)
     ts(col(12), col(4), 1.0 - HP, A.mult, -1.0, A.add)
     ts(col(13), col(4), 127.0, A.mult, 1.0, A.add)
@@ -629,19 +652,10 @@ def rank_program(g, core, T, topo):
         else:
             recs["HW"].append(keep)
 
-    gone = -BIG if ABSENT_ON_TENSOR else -5.0
-    mset(a("B", 0, 1), gone)
-    mset(a("B", V + 1, ODD + 1), gone)
     for lo in range(0, V, 512):
-        hi, bank = min(V, lo + 512), "Z%d" % (lo // 512 & 1)
-        if ABSENT_ON_TENSOR:
-            ts(a(bank, 0, hi - lo), a("wp", lo, hi), 0.5, A.is_lt, -BIG, A.mult)
-            tt(a("B", 1 + lo, 1 + hi), a("wp", lo, hi), a(bank, 0, hi - lo), A.add)
-        else:
-            ts(a("B", 1 + lo, 1 + hi), a("wp", lo, hi), 4.0, A.mult, -5.0, A.add)
-    for lo in range(0, V, 1024):
-        hi = min(V, lo + 1024)
-        act(a("B", ODD + 1 + lo, ODD + 1 + hi), a("B", 1 + lo, 1 + hi), F.Identity, bias=0.5 if ABSENT_ON_TENSOR else -0.5)
+        hi = min(V, lo + 512)
+        ts(a("B", 1 + lo, 1 + hi), a("wp", lo, hi), 0.5, A.mult, -0.625, A.add)
+        act(a("B", ODD + 1 + lo, ODD + 1 + hi), a("B", 1 + lo, 1 + hi), F.Identity, bias=-0.0625)
 
     cp(a("Ti"), a("Tc"))
     ts(a("Tj", 0, 512), a("Ti"), 2047, A.bitwise_and)
@@ -670,32 +684,12 @@ def rank_program(g, core, T, topo):
     cp(a("SN"), ind(a("SL"), a("ln")))
     act(a("NW"), ind(a("nw"), a("ln")), F.Copy)
     ts(a("DG"), a("i16"), col(3), A.is_equal)
-    ts(a("ID"), a("i16", 0, 16), col(3), A.is_equal)
-    ts(a("R16"), a("i16"), 1.0, A.min)
-    ts(a("R4"), a("R4"), 1.0, A.min)
-    if WIN_PE:
-        ts(a("o4"), a("it", 0, 8), col(3), A.is_equal, 4.0, A.mult)
-        for o in range(N):
-            act(a("SO", 128 * o, 128 * o + 128), a("SG"), F.Copy, scale=a("o4", o, o + 1))
-        scan(a("kq"), a("one", 0, 64), a("kc"), 0.0, A.mult, A.add)
-        act(a("kq"), a("kq"), F.Copy, scale=0.25)
-    else:
-        iota(a("SO", 0, 512), [[0, 64], [1, 8]], 0, 0)
-        ts(a("OM"), a("SO", 0, 512), col(3), A.is_equal)
-        ts(a("R8"), a("SO", 0, 512), 1.0, A.min)
-        act(a("SO", 640, 768), a("SG"), F.Copy, scale=4.0)
-        act(a("SO", 768, 896), a("SG"), F.Copy, scale=-4.0)
+    scan(a("kq"), a("one", 0, 64), a("kc"), 0.0, A.mult, A.add)
     act(a("S256"), a("nix"), F.Copy, scale=1.0 / 4096)
     act(a("less"), a("nix"), F.Identity, bias=-1.0 / 16, scale=0.0)
-    act(a("i3"), a("nix"), F.Identity, bias=1.0, scale=1.0 / 256)
     act(a("d12"), a("d12"), F.Identity, bias=col(3))
-    mset(a("neg"), gone)
-    ts(a("fi"), a("it", 0, 8), col(3), A.is_equal, 8.0, A.mult)
-    mset(col(18), 8.0)
-    for dl in ABSENT_ON_TENSOR:
-        tt(col(18), col(18), a("fi", dl, dl + 1), A.add)
-    for dl in SIGN_ON_VECTOR:
-        tt(col(18), col(18), a("fi", dl, dl + 1), A.subtract)
+    for k, dl in enumerate(SIGN_ON_VECTOR or (16,)):
+        ts(col(18), col(3), float(dl), A.not_equal, col(18) if k else 16.0, A.mult)
     act(a("c16"), a("zz", 0, 320), F.Identity, bias=col(18))
 
     def forty(name, rd, ds):
@@ -721,7 +715,7 @@ def rank_program(g, core, T, topo):
         scan(a("cum", 1, 513), a("G1"), a("c641"), 1023.0, A.add, A.max)
         if ZFIRST == 1:
             tt(a("mm"), a("cum", 0, 512), a("z"), A.mult)
-            pick(a("PM", 0, 32), "Bg", "cum", 0, 512, True, False)
+            pick(a("PM", 0, 32), "Bl", "cum", 0, 512, True, False)
             pick(a("PM", 0, 32), "Bf", "mm", 0, 512, False, True)
         else:
             tt(a("mm"), a("cum", 0, 512), a(sg), A.mult)
@@ -734,7 +728,7 @@ def rank_program(g, core, T, topo):
                 cp(a("n2", 0, 32), a("rq"))
                 ts(a("s2", 0, 32), a("n2", 0, 32), 9, A.arith_shift_right)
             ts(a("qp"), a("s2", 0, 32), float(BL), A.mult, 1023.0, A.add)
-            act(a("qo"), a("qp"), F.Identity, bias=-1023.0 * C / BL, scale=C / BL)
+            act(a("qo"), a("qp"), F.Identity, bias=15.0 - 1023.0 * C / BL, scale=C / BL)
         else:
             pick(a("Z1", 128, 160), "Bq", "G1", 0, 512)
             act(a("qp"), a("Z1", 128, 160), F.Identity, bias=1023.0, scale=float(BL))
@@ -762,7 +756,8 @@ def rank_program(g, core, T, topo):
 
     def ends(rd):
         act(a("pc1"), a("PM", 0, 32), F.Identity, bias=1023.0)
-        mm(a("PM", 64, 96), [(a("BP", 8, 136), a("cum", 8, 513, 16)), (a("BP", 0, 128), a("cum", 16, 513, 16))])
+        for k in range(2):
+            mm(a("PM", 64 + 16 * k, 80 + 16 * k), [(a("BQ" if k else "BP", 12 - 4 * q, 140 - 4 * q), a("cum", 8 + 8 * q, 513, 32)) for q in range(4)])
         pick(a("PM", 96, 128), "Bl", "G1", 0, 512)
         ts(a("E"), a("PM", 64, 96), -1.0, A.mult, 1023.0, A.add)
         tt(a("b3", 0, 32), a("PM", 96, 128), a("pc1"), A.add)
@@ -797,50 +792,41 @@ def rank_program(g, core, T, topo):
              forty("PS", rd, ds), forty("PI", rd, ds), 16 * len(ds) * ROW)
 
     def phrases(rd, dl, slot, first, last):
-        lo, x0 = C * slot, 648 * slot
-        hi, src = lo + C, ind(a("B", 0, ODD + V + 1), forty("PI", rd, [dl]))
-        act(a("Ab", x0 + 1, x0 + 641), src, F.Abs, bias=1.0 if ABSENT_ON_TENSOR else 4.0)
-        ct = a("ct", C * dl, C * dl + C)
-        tt(ct, src, a("Ab", x0, x0 + C), A.is_equal)
-        if dl in SIGN_ON_VECTOR:
-            ts(a("d", lo, hi), a("Ab", x0 + 1, x0 + 641), *((float(2 ** 30), A.is_lt) if ABSENT_ON_TENSOR else (2.0, A.is_gt)), 2.0, A.mult)
-        elif not ABSENT_ON_TENSOR:
-            act(a("d", lo, hi), a("Ab", x0 + 1, x0 + 641), F.Sign, bias=-2.0)
-        elif dl not in ABSENT_ON_TENSOR:
-            act(a("d", lo, hi), a("Ab", x0 + 1, x0 + 641), F.Sign, bias=float(2 ** 30), scale=-1.0)
-        scan(a("r", lo, hi), ct, ct, 0.0, A.mult, A.add)
-        for k in range(2):
-            if dl in ABSENT_ON_TENSOR:
-                x = x0 + 1 + 320 * k
-                mm(a("Z%d" % k, 0, 320), [(band("Bn", dl), a("Ab", x, x + 320))], first, False)
+        w = 320 if dl in IN_HALVES else C
+        for u in range(0, C, w):
+            lo, x0, at = C * slot + u, 648 * slot + u, forty("PI", rd, [dl])[1] + u // 16
+            src = ind(a("B", 0, ODD + V + 1), a("PI", at, at + w // 16))
+            act(a("Ab", x0 + 1, x0 + 1 + w), src, F.Abs, bias=0.5)
+            ct = a("ct", C * dl + u, C * dl + u + w)
+            tt(ct, src, a("Ab", x0, x0 + w), A.is_equal)
+            if dl in SIGN_ON_VECTOR:
+                ts(a("d", lo, lo + w), a("Ab", x0 + 1, x0 + 1 + w), 0.25, A.is_gt, 2.0, A.mult)
             else:
-                mm(a("Z%d" % k, 0, 320), [(band("Be", dl), a("d", lo + 320 * k, lo + 320 * k + 320))], first, False)
+                act(a("d", lo, lo + w), a("Ab", x0 + 1, x0 + 1 + w), F.Sign, bias=-0.25)
+            scan(a("r", lo, lo + w), ct, ct, a("r", lo - 1, lo) if u else 0.0, A.mult, A.add)
+        lo = C * slot
         for k in range(2):
-            mm(a("Z%d" % k, 0, 320), [(band("B2", dl), a("r", lo + 320 * k, lo + 320 * k + 320))], False, last)
+            mm(a("Z%d" % k, 0, 320), [(band("BA", dl), a("d", lo + 320 * k, lo + 320 * k + 320))], first, False)
+        for k in range(2):
+            mm(a("Z%d" % k, 0, 320), [(band("B4", dl), a("r", lo + 320 * k, lo + 320 * k + 320))], False, last)
 
     def winner(rd):
-        if WIN_PE:
-            mm(a("PM", 128, 192), [(a("SO", 0, 128), a("kq"))], True, False)
+        mm(a("PM", 128, 192), [(a("SO", 0, 128), a("kq"))], True, False)
         scan(a("cs", 1, 321), a("c16"), a("Z0", 0, 320), 0.0, A.add, A.add)
         scan(a("cs", 321, 641), a("c16"), a("Z1", 0, 320), a("cs", 320, 321), A.add, A.add)
-        if WIN_PE:
-            cp(a("g1", 0, 256), ind(a("cs", 0, 641), a("E", 0, 16)))
-            act(a("g1", 256, 512), ind(a("cs", 0, 641), a("E", 16, 32)), F.Copy)
-            mm(a("PM", 128, 192), [(a("SO", 128 * o, 128 * o + 128), a("g1", o, 512, 8)) for o in range(N)], False, True)
-            cp(a("Fs", 1, 65), a("PM", 128, 192))
-            tt(a("key"), a("PM", 128, 192), a("Fs", 0, 64), A.subtract)
-        else:
-            tt(a("g1"), ind(a("cs", 0, 641), a("E")), a("OM"), A.mult)
-            scan(a("SO", 8, 520), a("R8"), a("g1"), 0.0, A.mult, A.add)
-            mm(a("PM", 128, 192), [(a("SO", 640, 768), a("SO", 15, 520, 8)), (a("SO", 768, 896), a("SO", 7, 512, 8))])
-            tt(a("key"), a("PM", 128, 192), a("kc"), A.add)
+        tt(a("g1", 0, 256), ind(a("cs", 0, 641), a("E", 0, 16)), a("OM"), A.mult)
+        act(a("g1", 256, 512), ind(a("cs", 0, 641), a("E", 16, 32)), F.Copy)
+        scan(a("g2"), a("R4"), a("g1", 0, 256), 0.0, A.mult, A.add)
+        mm(a("PM", 128, 192), [(a("SO", 128 * o, 128 * o + 128), a("g1", 256 + o, 512, 4)) for o in range(4)], False, False)
+        mm(a("PM", 128, 192), [(a("SO", 512, 640), a("g2", 3, 256, 4))], False, True)
+        cp(a("Fs", 1, 65), a("PM", 128, 192))
+        tt(a("key"), a("PM", 128, 192), a("Fs", 0, 64), A.subtract)
         scan(a("mx", 1, 65), a("R4", 0, 64), a("key"), 0.0, A.mult, A.max)
         tt(a("oh"), ind(a("mx"), a("l4")), a("key"), A.is_equal)
         if rd + 1 < RO:
             for k in range(2):
                 tt(a("u2", 64 * k, 64 * k + 64), a("PX0", 64 * k, 64 * k + 64), a("oh"), A.mult)
-            scan(a("u3"), a("R4"), a("u2"), 0.0, A.mult, A.add)
-            for k in range(2):
+                scan(a("u3", 64 * k, 64 * k + 64), a("R4", 0, 64, 1), a("u2", 64 * k, 64 * k + 64), 0.0, A.mult, A.add)
                 cp(a("rq", k, 32, 2), a("u3", 64 * k + 3, 64 * k + 64, 4))
 
     def results(rd):
@@ -858,28 +844,32 @@ def rank_program(g, core, T, topo):
             cp(a("sl"), a("PX1", 96, 100))
 
     def distances(rd):
-        for dl in [SELF] + list(range(SELF)):
+        for dl in [SELF] + peers:
             for k in range(2):
-                mm(a("PH%d" % k, 0, 320), [(band("BA", 8 + dl), a("ct", C * dl + 320 * k, C * dl + 320 * k + 320))], dl == SELF, dl == SELF - 1)
+                mm(a("PH%d" % k, 0, 320), [(band("BA", 8 + dl), a("ct", C * dl + 320 * k, C * dl + 320 * k + 320))], dl == SELF, dl == peers[-1])
         for k in range(2):
             act(a("y", 320 * k, 320 * k + 320), a("PH%d" % k, 0, 320), F.Relu, bias=9216.0, scale=-1024.0)
         scan(a("DB", 1, 641), a("one"), a("y"), 0.0, A.add, A.min)
-        tt(a("dd"), ind(a("DB", 0, 641), a("eu")), a("sg%d" % (rd & 1)), A.mult)
+        if DD_S:
+            act(a("du"), ind(a("DB", 0, 641), a("eu")), F.Copy)
+            tt(a("dd"), a("du"), a("sg%d" % (rd & 1)), A.mult)
+        else:
+            tt(a("dd"), ind(a("DB", 0, 641), a("eu")), a("sg%d" % (rd & 1)), A.mult)
 
     def barrier_words(rd):
         pick(a("Z0", 0, 32), "Bh", "dd", 0, 512)
         squeeze(a("Z1", 64, 96), "oh", 0, 64, 2)
         tt(a("b1"), a("Z0", 0, 32), a("kl"), A.is_gt)
         tt(a("b2"), a("Z0", 0, 32), a("en"), A.add)
-        tt(a("b1"), a("b1"), a("b2"), A.mult)
-        tt(a("b2"), a("b1"), a("Z1", 64, 96), A.mult)
-        cp(a("WF", 1, 321), forty("PI", rd, [0, SELF]))
-        mm(a("Z1", 32, 40), [(a("BK", 8 - 8 * (k >> 1), 136 - 8 * (k >> 1)), a("b2", k, 32, 4)) for k in range(4)])
-        ts(a("bi", 0, 8), a("Z1", 32, 40), 15.0, A.add)
-        ts(a("bi", 8, 16), a("bi", 0, 8), 15, A.bitwise_and)
-        ts(a("bi", 16, 24), a("bi", 0, 8), 4, A.arith_shift_right)
-        cp(a("bu"), a("bi", 8, 24))
-        act(a("Mk"), ind(a("ID"), a("bu", 0, 8)), F.Copy)
+        tt(a("bi", 0, 32), a("b1"), a("b2"), A.mult)
+        ts(a("bi", 32, 64), a("bi", 0, 32), 15, A.bitwise_and)
+        ts(a("bi", 64, 96), a("bi", 0, 32), 4, A.arith_shift_right)
+        for k in range(2):
+            tt(a("bh", 32 * k, 32 * k + 32), a("bi", 32 * k + 32, 32 * k + 64), a("Z1", 64, 96), A.mult)
+        cp(a("WF", 1, 321), forty("PI", rd, [0, N - 1]))
+        mm(a("Z1", 32, 48), [(a("BK", 8 - 8 * (k >> 1), 136 - 8 * (k >> 1)), a("bh", k, 64, 4)) for k in range(4)])
+        cp(a("bu"), a("Z1", 32, 48))
+        act(a("Mk"), ind(a("DG", 0, 16), a("bu", 0, 8)), F.Copy)
         tt(a("Wd"), ind(a("WF", 0, 321), a("bu", 8, 16)), a("Mk"), A.mult)
         mm(a("Z0", 256, 384), [(a("SG"), a("S256" if rd + 1 < RO else "less"))], True, False)
         mm(a("Z0", 256, 384), [(a("SG"), a("Wd"))], False, True)
@@ -888,7 +878,8 @@ def rank_program(g, core, T, topo):
 
     def shown(rd):
         if rd + 1 < RO:
-            tt(a("YB", 128 * rd, 128 * rd + 128), a("K"), a("i3"), A.subtract)
+            act(a("x3"), a("K"), F.Identity, bias=WHOLE - 1.0)
+            act(a("YB", 128 * rd, 128 * rd + 128), a("x3"), F.Identity, bias=-WHOLE)
 
     def barriers():
         tt(a("k2", 0, 128), a("K"), a("DG"), A.mult)
@@ -911,7 +902,10 @@ def rank_program(g, core, T, topo):
         tt(a("k3", 8, 16), a("acc"), a("own"), A.add)
         tt(a("k4"), a("k3"), a("d12"), A.min)
         cp(a("ku"), a("k4"))
-        cp(ind(a("B"), a("ku")), a("neg"))
+        if MARK_ON_SCALAR:
+            add("s", lambda: g.scalar.activation(ap(ind(a("B"), a("ku"))), ap(a("neg")), F.Tanh), [a("neg")], [ind(a("B"), a("ku"))], 256 * SC * CY + FIX)
+        else:
+            cp(ind(a("B"), a("ku")), a("neg"))
 
     slot = 0
     for rd in range(RO):
@@ -935,8 +929,8 @@ def rank_program(g, core, T, topo):
         ends(rd)
         ahead(rd)
         chain[0], gate[0] = "phrases", None
-        for dl in [SELF] + list(range(SELF)):
-            phrases(rd, dl, slot % RING, dl == SELF, dl == SELF - 1)
+        for dl in [SELF] + peers:
+            phrases(rd, dl, slot % RING, dl == SELF, dl == peers[-1])
             slot += 1
         chain[0] = None
         winner(rd)

import math
import numpy as np
from concourse.bass import DstId, RemoteDMATransfer
from concourse.mybir import AluOpType as A, AxisListType, ActivationFunctionType as F

N, V, HP, C, RO = 8, 3040, 8192, 640, 3
BIG = float(2 ** 60)
SELF = N - 1
GROUPS = [[0, 1], [2, 3], [4, 5], [6]]
BATCH = [[0, 1], [2, 3], [4, 5], [6, 7]]
ANSWERS = [[0, 1], [7], [2, 3], [4, 5], [6]]
HEAP_ON_VECTOR = (0, 2, 4, 6)
ABSENT_ON_TENSOR = ()
EARLY = [1]
GATE = 3
HUSH = 2
REPEATS_ON_VECTOR = 0
T2_ON_SCALAR = 16
ODD = 3072
RING = 3
BL = 672
f32, bf, i32, u16, f16 = "float32", "bfloat16", "int32", "uint16", "float16"
SB = {
    "wp": (V, i32), "B": (2 * ODD + 256, f32), "hb": (1024, bf), "HW": (2 * HP, bf), "sli": (252, f32), "R40": (252, bf),
    "DQ": (512, f32), "DH": (256, f32), "acc": (8, f32), "S256": (128, f32), "nb": (8, f32),
    "W0": (N * BL + 512, bf), "W1": (N * BL + 512, bf), "gi": (128, i32), "m2": (128, i32),
    "msg": (64, u16), "Tc": (512, u16), "Ti": (512, i32), "Tj": (512, i32), "Tl": (512, f16),
    "off": (8, f32), "Ta": (512, bf), "qt": (64, u16),
    "Tb": (512, bf), "T1": (4096, bf), "T2": (4096, bf), "rn": (256, i32), "sn": (128, i32), "s2": (256, i32),
    "nn": (32, i32), "n2": (64, i32), "cn": (4, i32), "c2": (8, i32), "RL": (512, f32), "SL": (512, f32),
    "SN": (512, f32), "NW": (512, f32), "lr": (32, u16), "ls": (32, u16), "ln": (32, u16), "lc": (2, u16),
    "l4": (4, u16), "li": (72, f32), "zz": (1024, bf),
    "pc": (16, i32), "col": (32, f32), "it": (8, f32), "i3": (128, f32), "i4": (64, f32),
    "BA": (144, bf), "B4": (144, bf), "Bh": (144, bf), "Bf": (144, f16), "Bl": (144, bf),
    "BK": (144, f16), "BP": (144, f16), "SG": (128, f32), "TRI": (128, f32), "UP": (128, f32),
    "PM0": (128, f32), "PM1": (128, f32), "R4": (256, bf), "SO": (640, f32), "OM": (256, bf), "BQ": (144, f16), "g2": (256, f32),
    "du": (512, bf), "kq": (64, f32), "less": (128, f32), "Fs": (72, f32),
    "R16": (128, bf), "i16": (128, f32), "c641": (512, f16), "one": (640, bf),
    "c16": (320, bf), "dump": (32, f32), "DG": (128, f32), "ID": (16, f32), "kc": (64, f32), "nix": (128, f32),
    "d12": (16, f32), "neg": (256, f32),
    "sl": (4, u16), "sq": (16, u16), "rq": (32, u16), "qo": (32, f32), "qp": (32, f32),
    "t1": (256, f32), "t2": (128, f32), "u2": (128, f32), "u3": (128, f32),
    "x1": (256, f32), "x2": (128, f32), "x3": (128, f32), "NWc": (64, f32), "SNo": (64, f32),
    "G1": (512, bf), "G2": (512, bf), "sg0": (512, bf), "sg1": (512, bf), "z": (512, bf), "cum": (520, f16), "mm": (512, f16),
    "Ff": (520, bf), "D": (512, bf), "o1": (32, f32), "o2": (32, f32), "pc1": (32, f32), "of": (32, u16),
    "Y": (337, f32), "vi": (336, i32), "va": (336, i32), "E": (32, u16), "t3": (128, f32),
    "RS": (3 * 336, u16), "RI": (3 * 320, u16), "PS": (3 * 320, u16), "PI": (3 * 320, u16),
    "Hg": (5120, bf), "WF": (328, f32), "Ab": (RING * 648, f32),
    "d": (RING * C, bf), "ct": (N * C, bf), "r": (RING * C, bf), "cs": (648, f32), "g1": (512, f32),
    "key": (64, f32), "mx": (65, f32), "oh": (64, f32), "y": (640, bf), "DB": (648, bf), "dd": (512, bf),
    "en": (32, f32), "eu": (32, u16), "kl": (32, f32), "b1": (32, f32), "b2": (32, f32), "b3": (64, f32), "ow": (32, f32),
    "bi": (96, i32), "bh": (64, f16), "two": (128, f32), "bu": (16, u16), "Mk": (128, f32), "Wd": (128, f32), "K": (128, f32),
    "k2": (256, f32), "own": (8, f32), "o256": (8, f32), "fi": (8, f32), "k3": (16, f32), "k4": (16, f32), "ku": (16, u16),
    "YT": (192, f32), "YB": (384, f32), "YW": (48, f32),
}
GUEST = {"nw": ("Ab", 656, 512), "m3": ("Ab", 1304, 384), "i2": ("cs", 8, 288), "rn0": ("Ab", 8, 512), "hp": ("Tj", 0, 512),
         "o4": ("cs", 304, 256)}
HOME, SCRATCH = {}, {}
for _k, (_n, _t) in SB.items():
    _h = _k if _n > 600 else "all_" + _t
    _at = SCRATCH[_h][1][1] if _h in SCRATCH else 0
    HOME[_k] = (_h, _at)
    SCRATCH[_h] = ("sbuf", [128, _at + (_n + 15) // 16 * 16], _t)
SCRATCH["DT"] = ("dram", [N, 128, 64], u16)
PSUM = ["Z0", "Z1", "PX0", "PX1", "PX2", "PH0", "PH1", "PM"]
for _k in PSUM:
    SCRATCH[_k] = ("psum", [128, 512], f32)
    HOME[_k] = (_k, 0)
SEMAPHORES = (["v", "s", "p", "g", "sent", "tab"] + ["d%d" % k for k in range(1, 70)]
              + ["%s%d_%d" % (a, r, k) for a in "qa" for r in range(RO) for k in range(N)])
CASES = np.array([[0.9e-3, 0.55e-3, 1.56, 3.8, 0.05, 0.08, 2.0, 0.7, 0.04, 1.5, 30e3, 0.15],
                  [0.85e-3, 0.62e-3, 1.2, 2.5, 0.04, 0.12, 1.5, 0.9, 0.02, 1.2, 50e3, 0.3],
                  [1.15e-3, 0.7e-3, 1.85, 5.0, 0.05, 0.06, 2.7, 0.6, 0.06, 1.8, 16e3, 0.1]])
CY, PE, GA, SC, FIX, HOPS, REM, ISS, ROW, DMA, RATE, PUT = CASES.T
HOP, FIRST = 0.08, 3.0
SIGN_ON_VECTOR, ZFIRST, QP_V, MARK_ON_SCALAR, DD_S, WHOLE = (), 1, 1, 0, 0, 1.5 * 2 ** 23
IN_HALVES, W0_BY_COPY, HW_BY_COPY = (6,), 0, (3, 3)
SWEEPS, STEPS, HEAT, SEED = 15, 59400, 0.02, 5
PLAN = []
USE, SEEN, TRIES, REACH, PASSES, PARTS = 3, [], 4, 40, 20, 11


def rank_program(g, core, T, topo):
    me = T.rank_of(core)
    if me is None:
        return
    Q = {"v": g.vector, "s": g.scalar, "p": g.tensor, "g": g, "y": g.sync}
    nodes, recs, nd, chain, last, gate, hush, sent = [], {}, [0], [None], {}, [None], [None], [0]

    def a(name, lo=0, hi=None, st=1, ps=None):
        if name in GUEST:
            host, at, n = GUEST[name]
            return (host, at + lo, at + (n if hi is None else hi), st, ps)
        return (name, lo, (SB[name][0] if name in SB else 512) if hi is None else hi, st, ps)

    def ind(w, o):
        return ("@", w, o)

    def ap(x):
        if not isinstance(x, tuple):
            return x
        if x[0] == "@":
            return ap(x[1]).indirect(ap(x[2]))
        ps = slice(0, 128) if x[4] is None else x[4]
        h, at = HOME[x[0]]
        return T[h][ps, at + x[1]:at + x[2]:x[3]] if x[3] > 1 else T[h][ps, at + x[1]:at + x[2]]

    def width(x):
        return 16 * width(x[2]) if x[0] == "@" else (x[2] - x[1] + x[3] - 1) // x[3]

    def two(x):
        return x[0] in SB and SB[x[0]][1] in (bf, u16, f16)

    def add(q, fn, reads, writes, hold, late=0.0, sem=None, val=None, after=(), eng=0.0):
        use = []
        for x in reads:
            if isinstance(x, tuple):
                use += [(x[1], 0), (x[2], 0)] if x[0] == "@" else [(x, 0)]
        for x in writes:
            if isinstance(x, tuple):
                use += [(x[1], 1), (x[2], 0)] if x[0] == "@" else [(x, 1)]
        deps, n = set(after), len(nodes)
        for x, w in use:
            for lo, hi, w0, q0, k in recs.get(x[0], []):
                if (q0 != q or w or w0) if x[0] in PSUM else ((w or w0) and lo < x[2] and x[1] < hi):
                    deps.add(k)
        for x, w in use:
            old = recs.get(x[0], [])
            if w and x[0] in PSUM:
                old = []
            elif w and x[3] == 1 and x[4] is None:
                old = [e for e in old if not (x[1] <= e[0] and e[1] <= x[2])]
            recs[x[0]] = old + [(x[1], x[2], w, q, n)]
        soft = set()
        if chain[0]:
            soft = {last[q, chain[0]]} - deps if (q, chain[0]) in last else set()
            last[q, chain[0]] = n
        if hush[0] is not None and q == "s":
            soft = soft | ({hush[0]} - deps)
        if gate[0] is not None and q == "v":
            soft = soft | ({gate[0]} - deps)
        nodes.append({"q": q, "fn": fn, "deps": deps | soft, "soft": soft, "holds": hold + 0 * HOPS, "lates": late + 0 * HOPS,
                      "hold": float((hold + 0 * HOPS)[0]), "late": float((late + eng + 0 * HOPS)[0]), "sem": sem or q, "val": val,
                      "engs": eng + 0 * HOPS})
        return n

    def vec(fn, reads, o, per=1.0):
        big = [x for x in reads if isinstance(x, tuple) and width(x) > 1] + [o]
        if o[0] == "@":
            per = SC
        elif any(x[0] == "@" for x in big):
            per = GA
        elif all(two(x) for x in big):
            per *= 0.5
        add("v", fn, reads, [o], np.maximum(64, per * max(width(x) for x in big)) * CY + FIX)

    def cp(o, i):
        vec(lambda: g.vector.tensor_copy(ap(o), ap(i)), [i], o)

    def tt(o, x, y, f):
        vec(lambda: g.vector.tensor_tensor(ap(o), ap(x), ap(y), f), [x, y], o, 1.0 if x[0] in PSUM or y[0] in PSUM else 2.0)

    def ts(o, x, s1, f1, s2=None, f2=None):
        if f2 is None:
            vec(lambda: g.vector.tensor_scalar(ap(o), ap(x), ap(s1), None, f1), [x, s1], o)
        else:
            vec(lambda: g.vector.tensor_scalar(ap(o), ap(x), ap(s1), ap(s2), f1, f2), [x, s1, s2], o)

    def scan(o, d0, d1, init, f0, f1):
        vec(lambda: g.vector.tensor_tensor_scan(ap(o), ap(d0), ap(d1), ap(init), f0, f1), [d0, d1, init], o)

    def mset(o, c):
        vec(lambda: g.vector.memset(ap(o), c), [], o)

    def turn(o, i):
        vec(lambda: g.vector.transpose(ap(o), ap(i)), [i], o)

    def least(o, x):
        vec(lambda: g.vector.tensor_reduce(ap(o), ap(x), AxisListType.X, A.min, apply_absolute_value=True), [x], o)

    def act(o, i, f, bias=0.0, scale=1.0, total=None):
        add("s", lambda: g.scalar.activation(ap(o), ap(i), f, bias=ap(bias), scale=ap(scale), accum_out=ap(total)),
            [i, bias, scale], [o, total], np.maximum(64, width(o) * (GA if i[0] == "@" else 1.0)) * CY + FIX)

    def iota(o, pat, base, ch):
        kw = {} if SB[o[0]][1] == i32 else {"allow_small_or_imprecise_dtypes": True}
        add("g", lambda: g.iota(ap(o), pat, base, ch, **kw), [], [o], 0.15 + 2 * width(o) * CY)

    def keep_where(o, i, pat, f, base, ch):
        add("g", lambda: g.affine_select(ap(o), ap(i), pat, f, 0.0, base, ch), [i], [o], 0.19 + 2 * width(o) * CY)

    def mm(o, terms, start=True, stop=True):
        def fn():
            for k, t in enumerate(terms):
                ins = g.tensor.matmul(ap(t[2] if len(t) > 2 else o), ap(t[0]), ap(t[1]), start and k == 0, stop and k == len(terms) - 1)
            return ins
        add("p", fn, [x for t in terms for x in t[:2]], [o], sum(max(64, width(t[1])) * (1 if two(t[0]) else 4) * PE for t in terms))

    def dma(q, o, i, size, rows=128, reads=(), writes=()):
        nd[0] += 1
        name = "d%d" % nd[0]
        add(q, lambda: Q[q].dma_start(ap(o), ap(i)), [i] + list(reads), [o] + list(writes), PUT, DMA, name, 16,
            eng=max(1, rows // 16) * ROW + rows * size / 16 / RATE)

    def send(ds, sign, src, dst, sem, read, land, late):
        trs, n = [], 0
        for k, dl in enumerate(ds):
            peer = T.cores[(me + sign * (dl - SELF)) % N]
            es = topo.engines(core, peer)
            n = 1
            while 2 * n * len(ds) <= len(es):
                n *= 2
            rid, pid = topo.addr(peer, core)
            trs.append(RemoteDMATransfer(dst_ids=[DstId(rid=rid, pnc=pid)], dma_engine_mask=sum(1 << e for e in es[k * n:(k + 1) * n]),
                                         remote_sem=T.sem[sem], src=src(dl), dst=dst(dl)))
        add("g", lambda: g.remote_dma_fused(trs, local_sem=T.sem.sent), [read], [land], ISS + (FIRST if sem == "tab" else 0.0), REM, sem,
            n * len(ds), eng=late)
        sent[0] += n * len(ds)

    def issue():
        n = len(nodes)
        rest = [0.0] * n
        for k in range(n - 1, -1, -1):
            rest[k] += nodes[k]["hold"] + nodes[k]["late"] + HOP
            for j in nodes[k]["deps"]:
                rest[j] = max(rest[j], rest[k])
        users = [[] for k in range(n)]
        for k in range(n):
            for j in nodes[k]["deps"]:
                users[j].append(k)

        def place(turns, back):
            at, used = [0.0] * n, {q: [] for q in "vspgyr"}
            for k in turns:
                e = nodes[k]
                if back:
                    t = max([at[j] + nodes[j]["hold"] for j in users[k]] + [0.0]) + e["late"] + HOP
                else:
                    t = max([at[j] + nodes[j]["hold"] + nodes[j]["late"] + HOP for j in e["deps"]] + [0.0])
                if e["q"] in used:
                    spans = used[e["q"]]
                    i = len(spans)
                    while i and spans[i - 1][1] > t:
                        i -= 1
                    while i < len(spans) and spans[i][0] < t + e["hold"]:
                        t = max(t, spans[i][1])
                        i += 1
                    spans.insert(i, (t, t + e["hold"]))
                at[k] = t
            return at, max(at[k] + nodes[k]["hold"] + (0.0 if back else nodes[k]["late"]) for k in range(n))

        def polish(turns, rng):
            deps = [sorted(e["deps"] - e["soft"]) for e in nodes]
            uses = [[] for k in range(n)]
            for k in range(n):
                for j in deps[k]:
                    uses[j].append(k)
            qs = [e["q"] for e in nodes]
            cases = [([float(e["holds"][c]) for e in nodes], [float(e["lates"][c] + HOPS[c]) for e in nodes],
                      [float(e["engs"][c]) for e in nodes]) for c in range(len(HOPS))]
            moves = [bool(e["engs"][0]) for e in nodes]
            needs = [[j for j in deps[k] if qs[j] + qs[k] != "pp"] for k in range(n)]
            feeds = [[j for j in uses[k] if qs[j] + qs[k] != "pp"] for k in range(n)]

            def run(turns, first, known, cases, lo=0, hi=n, far=None):
                total, pairs, state, ends, mover = 0.0, [], [], {}, -1
                inside = turns[lo:hi]
                for k in reversed(turns[:first]):
                    if qs[k] not in ends:
                        ends[qs[k]] = k
                    if mover < 0 and moves[k]:
                        mover = k
                    if mover >= 0 and len(ends) == len(Q):
                        break
                rest = turns[first:hi]
                for c, ((hold, late, eng), old) in enumerate(zip(cases, known)):
                    done, why, out, behind = (list(x) for x in old[:4])
                    free = {q: (out[ends[q]], ends[q]) if q in ends else (0.0, -1) for q in Q}
                    busy = (done[mover] - late[mover], mover) if mover >= 0 else (0.0, -1)
                    for k in rest:
                        t, w = free[qs[k]]
                        for j in needs[k]:
                            if done[j] > t:
                                t, w = done[j], j
                        why[k] = w
                        t += hold[k]
                        out[k] = t
                        free[qs[k]] = (t, k)
                        if moves[k]:
                            behind[k] = -1
                            if busy[0] > t:
                                t, behind[k] = busy
                            t += eng[k]
                            busy = (t, k)
                        done[k] = t + late[k]
                    landed = True
                    if far is None:
                        end = max(done)
                        k = done.index(end)
                    else:
                        beyond, exits = far[c]
                        end, k = max((done[k] + beyond[k], k) for k in inside)
                        for q, t in exits.items():
                            u = busy if q == "e" else free[q]
                            if u[0] + t > end:
                                end, k, landed = u[0] + t, u[1], q == "e"
                    total += math.log(end)
                    path = set()
                    state.append((done, why, out, behind, path, end))
                    while k >= 0 and spot[k] >= lo:
                        path.add(k)
                        j = behind[k] if landed and behind[k] >= 0 else why[k]
                        landed = j in sets[k]
                        if j >= 0 and not landed and spot[j] >= lo:
                            pairs.append((j, k))
                        landed = landed or j == behind[k]
                        k = j
                return total, pairs, state

            sets = [set(d) for d in deps]
            blank = [([0.0] * n, [-1] * n, [0.0] * n, [-1] * n)] * len(cases)
            every = cases
            SEEN.append(lambda turns: run(turns, 0, blank, every)[2])
            cases = cases[:USE]

            def tails(turns, last, known, lo=0):
                state, ends, mover = [], {}, n
                for k in turns[last + 1:]:
                    if qs[k] not in ends:
                        ends[qs[k]] = k
                    if mover == n and moves[k]:
                        mover = k
                    if mover < n and len(ends) == len(Q):
                        break
                head = turns[lo:last + 1][::-1]
                for (hold, late, eng), old in zip(cases, known):
                    tail, turn = list(old[0]), list(old[1])
                    free = {q: tail[ends[q]] if q in ends else 0.0 for q in Q}
                    busy = turn[mover]
                    for k in head:
                        t = 0.0
                        for j in feeds[k]:
                            if tail[j] > t:
                                t = tail[j]
                        t += late[k]
                        if moves[k]:
                            busy = turn[k] = t = max(t, busy) + eng[k]
                        free[qs[k]] = tail[k] = max(t, free[qs[k]]) + hold[k]
                    state.append((tail, turn))
                return state

            def guess(turns, i, j, mid):
                before, after, mine, total = {}, {}, set(mid), 0.0
                want = set(qs[k] for k in mid)
                if any(moves[k] for k in mid):
                    want.add("e")
                for side, out in ((turns[i - 1::-1] if i else [], before), (turns[j + 1:], after)):
                    for k in side:
                        if qs[k] not in out:
                            out[qs[k]] = k
                        if moves[k] and "e" not in out:
                            out["e"] = k
                        if want <= out.keys():
                            break
                for (hold, late, eng), (done, why, out, behind, path, was), (tail, turn) in zip(cases, known, rear):
                    free = {q: out[before[q]] if q in before else 0.0 for q in want}
                    busy = done[before["e"]] - late[before["e"]] if "e" in before else 0.0
                    new, end = {}, was if path.isdisjoint(mine) else 0.0
                    for k in mid:
                        t = free[qs[k]]
                        for u in needs[k]:
                            u = new[u] if u in new else done[u]
                            if u > t:
                                t = u
                        free[qs[k]] = t = t + hold[k]
                        if moves[k]:
                            busy = t = max(t, busy) + eng[k]
                        new[k] = t = t + late[k]
                        far = 0.0
                        for u in feeds[k]:
                            if tail[u] > far and u not in mine:
                                far = tail[u]
                        if t + far > end:
                            end = t + far
                    for q in want:
                        if q in after:
                            end = max(end, busy + turn[after[q]] if q == "e" else free[q] + tail[after[q]])
                    total += math.log(end)
                return total

            best, keep, spot, each = 1e9, turns, {}, STEPS // (PASSES * PARTS)
            draws = rng.random((STEPS, TRIES, 4)).tolist()
            for step in range(each * PASSES * PARTS):
                if step % each == 0:
                    part = step // each % PARTS
                    spot.update((k, i) for i, k in enumerate(turns))
                    now, pairs, known = run(turns, 0, blank, cases)
                    if now < best:
                        best, keep = now, turns
                    if part == 0:
                        turns = sorted(turns, key=lambda k: (known[0][2][k] - cases[0][0][k], spot[k]))
                        spot.update((k, i) for i, k in enumerate(turns))
                        now, pairs, known = run(turns, 0, blank, cases)
                    rear = tails(turns, n - 1, [([0.0] * (n + 1), [0.0] * (n + 1))] * len(cases))
                    lo, hi = n * part // (PARTS + 1), n * (part + 2) // (PARTS + 1)
                    exits = {}
                    for k in turns[hi:]:
                        exits.setdefault(qs[k], k)
                        if moves[k]:
                            exits.setdefault("e", k)
                    far = [({k: max([tail[u] for u in feeds[k] if spot[u] >= hi] + [0.0]) for k in turns[lo:hi]},
                            {q: (turn if q == "e" else tail)[k] for q, k in exits.items()}) for tail, turn in rear]
                    now, pairs, known = run(turns, lo, known, cases, lo, hi, far)
                tried = []
                for pair, way, reach, tie in draws[step] if pairs else []:
                    x, y = pairs[int(pair * len(pairs))]
                    i, j = spot[x], spot[y]
                    reach = int(reach ** 3 * REACH)
                    if way < 0.5:
                        i = max(lo, i - reach)
                        mid, move = turns[i:j + 1], {y}
                        for k in reversed(mid):
                            if k in move:
                                move.update(deps[k])
                        if x in move:
                            continue
                        mid = [k for k in mid if k in move] + [k for k in mid if k not in move]
                    else:
                        j = min(hi - 1, j + reach)
                        mid, move = turns[i:j + 1], {x}
                        for k in mid:
                            if k in move:
                                move.update(uses[k])
                        if y in move:
                            continue
                        mid = [k for k in mid if k not in move] + [k for k in mid if k in move]
                    tried.append((guess(turns, i, j, mid), tie, i, j, mid))
                limit = now + HEAT * (1.0 - step / STEPS) * draws[step][0][3]
                if not tried or min(tried)[0] > limit:
                    continue
                i, j, mid = min(tried)[2:]
                other = turns[:i] + mid + turns[j + 1:]
                total, found, state = run(other, i, known, cases, lo, hi, far)
                if total <= limit:
                    turns, now, pairs, known = other, total, found, state
                    rear = tails(turns, j, rear, lo)
                    for u, k in enumerate(mid):
                        spot[k] = i + u
            return turns if run(turns, 0, blank, cases)[0] < best else keep

        if not PLAN:
            start, best = place(sorted(range(n), key=lambda k: (-rest[k], k)), False)
            rng = np.random.default_rng(SEED)
            for sweep in range(SWEEPS):
                key = np.array(start) + rng.normal(0.0, (0.3, 1.0, 3.0)[sweep % 3], n) * (rng.random(n) < 0.3)
                for k in range(n):
                    for j in nodes[k]["deps"]:
                        key[k] = max(key[k], key[j])
                now, end = place(sorted(range(n), key=lambda k: (key[k], k)), False)
                if sweep % 4 == 0:
                    late = place(sorted(range(n), key=lambda k: (-now[k] - nodes[k]["hold"] - nodes[k]["late"], -k)), True)[0]
                    now, end = place(sorted(range(n), key=lambda k: (-late[k] - nodes[k]["hold"], k)), False)
                if end <= best:
                    start, best = now, end
            PLAN.append(polish(sorted(range(n), key=lambda k: (start[k], k)), rng))
        cnt, seen = {"sent": sent[0]}, {q: {} for q in Q}
        for k in PLAN[0]:
            e = nodes[k]
            q, sem = e["q"], e["sem"]
            need = {}
            for j in e["deps"] - e["soft"]:
                if not (q == "p" and nodes[j]["q"] == "p"):
                    need[nodes[j]["sem"]] = max(need.get(nodes[j]["sem"], 0), nodes[j]["at"])
            for s, val in need.items():
                if seen[q].get(s, 0) < val:
                    Q[q].wait_ge(T.sem[s], val)
                    seen[q][s] = val
            ins = e["fn"]()
            SEEN.append((k, e, ins))
            if q != "g" or sem == "g":
                ins.then_inc(T.sem[sem], e["val"] or 1)
            cnt[sem] = cnt.get(sem, 0) + (e["val"] or 1)
            e["at"] = cnt[sem]
        for s, val in cnt.items():
            if max(seen[q].get(s, 0) for q in Q) < val:
                g.sync.wait_ge(T.sem[s], val)

    def band(name, i):
        return a(name, 15 - i, 143 - i)

    def pick(o, name, src, lo, hi, start=True, stop=True):
        mm(o, [(band(name, i), a(src, lo + i, hi, 16)) for i in range(16)], start, stop)

    def squeeze(o, name, lo, hi, f, st=1, sums=1):
        mm(o, [(a("DQ" if f == 4 else "DH", 128 * d, 128 * d + 128), a(name, lo + st * d + k, hi, st * f))
               for d in range(f) for k in range(sums)])

    def colf(w, x, tmp):
        ts(a(tmp, 0, w), x, 15, A.bitwise_and)
        ts(a(tmp, w, 2 * w), x, 4, A.arith_shift_right)
        ts(a(tmp, 0, w), a(tmp, 0, w), 32.0, A.mult)
        tt(x, a(tmp, 0, w), a(tmp, w, 2 * w), A.add)

    def col(k):
        return a("col", k, k + 1)

    row0 = slice(0, 128, 16)

    dma("y", a("gi", 0, 64, ps=slice(0, 64)), T.gst[:], 256, 64)
    dma("s", a("gi", 64, 128, ps=slice(0, 64)), T.gln[:], 256, 64)
    for k in range(2):
        dma("y", a("sn", 64 * k, 64 * k + 64), T.sens[k::2, :], 256)
        dma("s", a("rn", 128 * k, 128 * k + 128), T.rel[k::2, :], 512)
        dma("y", a("nn", 16 * k, 16 * k + 16), T.nxt[:, 256 * k:256 * k + 256], 64)
    dma("y", a("cn", 0, 1), T.cur[:], 4)
    dma("y", a("hp"), T.heap[:], 2048)
    for lo in range(0, V, 1024):
        dma("y", a("wp", lo, min(V, lo + 1024)), T.wpos[:, lo:min(V, lo + 1024)], 4096)

    iota(a("pc", 0, 1), [[1, 1]], 0, 1)
    iota(a("i3"), [[8, 8], [64, 2], [1, 8]], 0, -1)
    iota(a("i2", 0, 144), [[1, 144]], -15, 0)
    iota(a("i2", 144, 288), [[1, 144]], -8, 0)
    iota(a("li", 0, 32), [[8, 16], [128, 2]], 0, 0)
    iota(a("li", 32, 64), [[4, 16], [64, 2]], 0, 0)
    iota(a("li", 64, 68), [[4, 4]], 1, 0)
    iota(a("i4"), [[0, 16], [1, 4]], 0, 0)
    iota(a("it"), [[1, 8]], 0, 0)
    iota(a("sli"), [[0, 6], [16, 42]], 0, 0)
    iota(a("dump"), [[16, 32]], N * BL, 0)
    for name in ("Ff", "cs", "DB", "Fs", "mx", "WF", "Y"):
        iota(a(name, 0, 1), [[0, 1]], 0, 0)
    for k in range(RING):
        iota(a("Ab", 648 * k, 648 * k + 1), [[0, 1]], 0, 0)
    iota(a("nix"), [[1, 128]], 0, 0)
    iota(a("i16"), [[0, 8], [1, 16]], 0, 0)
    iota(a("SG"), [[16, 8], [0, 16]], 0, 0)
    iota(a("nw"), [[1, 16], [16, 32]], 0, 0)
    iota(a("one"), [[0, 640]], 1, 0)
    iota(a("d12"), [[16, 16]], 2 * ODD, 0)
    iota(a("two"), [[0, 128]], 2, 0)
    iota(a("neg"), [[0, 256]], -1, 0)
    if MARK_ON_SCALAR:
        add("s", lambda: g.scalar.activation(ap(a("neg")), ap(a("neg")), F.Tanh), [a("neg")], [a("neg")], 1.3 + 256 * CY + FIX)
    else:
        act(a("neg"), a("neg"), F.Copy, scale=0.625)
    iota(a("o4"), [[0, 64], [1, 4]], 0, 0)
    iota(a("B", 0, 1), [[0, 1]], -5, 0)
    iota(a("B", V + 1, ODD + 1), [[0, ODD - V]], -5, 0)
    keep_where(a("R4"), a("one", 0, 256), [[0, 64], [1, 4]], A.is_gt, 0, 0)
    keep_where(a("R16"), a("one", 0, 128), [[0, 8], [1, 16]], A.is_gt, 0, 0)
    keep_where(a("R40"), a("one", 0, 252), [[0, 6], [-1, 42]], A.is_gt, 41, 0)
    for o in range(4):
        keep_where(a("SO", 128 * o, 128 * o + 128), a("two"), [[-16, 8], [0, 16]], A.is_equal, -4 - o, 1)
    mset(a("zz"), 0.0)
    p0 = a("pc", 0, 1)
    cp(col(0), p0)
    ts(a("PM0"), a("i3"), 0.0, A.is_equal)
    ts(a("PM1"), a("i3"), 64.0, A.is_equal)
    for k, m in ((2, 112), (3, 15), (4, 8), (6, 7), (7, 119), (8, 3), (9, 12)):
        ts(a("pc", k, k + 1), p0, m, A.bitwise_and)
        ts(col(k), a("pc", k, k + 1), {4: 0.125, 9: 0.25}.get(k, 1.0), A.mult)
    ts(col(5), col(4), -1.0, A.mult, 1.0, A.add)
    chain[0] = "zero"
    for lo in range(0, N * BL, BL):
        if lo // BL < W0_BY_COPY:
            dma("y", a("W0", lo, lo + BL), a("zz", 0, BL), 2 * BL)
        else:
            iota(a("W0", lo, lo + BL), [[0, BL]], 0, 0)
    ts(col(16), col(3), 3.0, A.is_equal)
    ts(col(17), col(3), 2.0, A.is_equal, float(ODD), A.mult)
    tt(col(17), col(17), col(16), A.add)
    for lo in range(0, 2 * HP, 1024):
        if lo % HP >= HP - 1024 * HW_BY_COPY[lo // HP]:
            dma("y", a("HW", lo, lo + 1024), a("HW", lo - lo % HP, lo - lo % HP + 1024), 2048)
        else:
            act(a("HW", lo, lo + 1024), a("zz"), F.Identity, bias=col(16 + lo // HP))
    chain[0] = None

    def low(name, k):
        return a(name, 64 * k, 64 * k + 64, ps=slice(0, 64))

    ts(low("m2", 0), low("gi", 0), 127, A.bitwise_and)
    ts(low("m3", 2), low("gi", 1), 1.0, A.min)
    ts(low("m2", 1), low("gi", 0), 7, A.arith_shift_right)
    ts(low("m3", 3), low("gi", 1), 2049.0, A.mult)
    tt(low("m3", 4), low("m2", 0), low("m3", 2), A.mult)
    ts(low("m3", 5), low("m2", 1), 2048.0, A.add)
    tt(low("m3", 0), low("m3", 4), low("m3", 3), A.add)
    tt(low("m3", 1), low("m3", 5), low("m3", 2), A.mult)
    mm(a("PM", 0, 64), [(a("PM%d" % k, ps=slice(0, 64)), low("m3", k)) for k in range(2)])
    cp(a("msg"), a("PM", 0, 64))
    own, peers = ("DT", N, N + 1, 1, None), [dl for dl in range(N) if dl != SELF]
    dma("y", T.DT[SELF], a("msg"), 128, writes=[own])
    send(peers, -1, lambda dl: T.DT[SELF], lambda dl: T.DT[dl], "tab", own, ("DT", 0, N, 1, None), ROW + 16384 / RATE)
    for dl in range(N):
        dma("ys"[~dl & 1], a("Tc", ps=slice(dl, 128, 8)), T.DT[dl], 1024, 16, reads=[own if dl == SELF else ("DT", 0, N, 1, None)])
        recs["Tc"], recs["Tc%d" % dl] = [], recs["Tc"]
    recs["Tc"] = [e for dl in range(N) for e in recs["Tc%d" % dl]]

    ts(a("lr"), a("li", 0, 32), col(6), A.add)
    ts(a("ls"), a("li", 32, 64), col(8), A.add)
    ts(a("l4"), a("li", 64, 68), col(9), A.add, 4.0, A.mult)
    colf(128, a("sn"), "s2")
    cp(a("g1"), ind(a("sn"), a("ls")))
    turn(a("SL"), a("g1"))
    ts(a("rn"), a("rn"), float(512 * (N + SELF - me)), A.add)
    ts(a("rn"), a("rn"), 4095, A.bitwise_and)
    cp(a("rn0"), ind(a("rn"), a("lr")))
    turn(a("RL"), a("rn0"))
    colf(1, a("cn", 0, 1), "c2")
    cp(a("lc", 0, 1), a("cn", 0, 1))
    act(a("kc"), a("i4"), F.Identity, bias=1.5, scale=-0.5)
    ts(a("i4", 0, 4), a("i4", 0, 4), col(9), A.is_equal)
    for d in range(4):
        ts(a("DQ", 128 * d, 128 * d + 128), a("nix"), col(0), A.is_equal, a("i4", d, d + 1), A.mult)
    for d in range(2):
        ts(a("DH", 128 * d, 128 * d + 128), a("nix"), col(0), A.is_equal, col(5 - d), A.mult)
    act(a("SNo", 0, 16), ind(a("SL"), a("lc", 0, 1)), F.Copy)
    squeeze(a("PX1", 0, 4), "SNo", 0, 16, 4)
    cp(a("sl"), a("PX1", 0, 4))
    act(a("t1", 0, 64), ind(a("RL"), a("sl")), F.Copy)
    squeeze(a("PX1", 32, 64), "t1", 0, 64, 2)
    cp(a("rq"), a("PX1", 32, 64))

    ts(col(15), col(4), -1.0, A.add)
    for name, w in (("Bf", col(5)), ("BA", 1.0), ("B4", 4.0), ("Bh", col(4)), ("Bl", col(15))):
        ts(a(name), a("i2", 0, 144), col(2), A.is_equal, w, A.mult)
    ts(a("BK"), a("i2", 144, 288), col(7), A.is_equal)
    ts(col(1), col(0), 4.0, A.add)
    ts(a("BP"), a("i2", 144, 288), col(1), A.is_equal, a("i4", 0, 1), A.mult)
    ts(a("BQ"), a("i2", 144, 288), col(0), A.is_equal, a("i4", 1, 2), A.mult)
    ts(a("OM"), a("o4"), col(3), A.is_equal)
    ts(a("SG"), a("SG"), col(2), A.is_equal)
    act(a("SO", 512, 640), a("SG"), F.Copy, scale=2.0)
    keep_where(a("TRI"), a("SG"), [[1, 128]], A.is_ge, 0, -1)
    keep_where(a("UP"), a("SG"), [[-1, 128]], A.is_gt, 0, 1)
    ts(a("dump"), a("dump"), col(3), A.add)
    mset(a("c641"), 1023.0 - C)
    mset(a("cum", 0, 1), 1023.0)
    ts(a("sli"), a("sli"), col(3), A.add)
    ts(col(12), col(4), 1.0 - HP, A.mult, -1.0, A.add)
    ts(col(13), col(4), 127.0, A.mult, 1.0, A.add)
    act(col(11), col(12), F.Copy, scale=-1024.0)
    ts(a("off"), a("it", 0, 8), col(6), A.is_equal)
    cp(a("hb", 0, 512), a("hp"))
    tt(a("hb", 512, 1024), a("hp"), a("hb", 0, 512), A.subtract)
    for lo, (p, x) in zip((0, 0, HP, HP), ((0, 0), (1, 512), (0, 0), (1, 512))):
        dma("y", a("HW", lo, lo + HP, ps=slice(p, 128, 16)), a("hb", x, x + 512), 1024)
        if p == 0:
            keep = recs["HW"].pop()
        else:
            recs["HW"].append(keep)

    for lo in range(0, V, 512):
        hi = min(V, lo + 512)
        ts(a("B", 1 + lo, 1 + hi), a("wp", lo, hi), 0.5, A.mult, -0.625, A.add)
        act(a("B", ODD + 1 + lo, ODD + 1 + hi), a("B", 1 + lo, 1 + hi), F.Identity, bias=-0.0625)

    cp(a("Ti"), a("Tc"))
    ts(a("Tj", 0, 512), a("Ti"), 2047, A.bitwise_and)
    ts(a("Tb"), a("Tj", 0, 512), col(13), A.mult)
    ts(a("Tl"), a("Tc"), 1.0 / 2048, A.mult, 1024.0, A.add)
    ts(a("Ta"), a("Tl"), col(12), A.mult, col(11), A.add)
    cp(a("n2", 0, 32), a("rq"))
    ts(a("s2", 0, 32), a("n2", 0, 32), 9, A.arith_shift_right)
    ts(a("s2", 32, 64), a("n2", 0, 32), 511, A.bitwise_and)
    cp(a("qt"), a("s2", 0, 64))
    act(a("dd"), ind(a("off"), a("qt", 0, 32)), F.Copy)
    tt(a("G1"), ind(a("Ta"), a("qt", 32, 64)), a("dd"), A.mult)
    tt(a("G2"), ind(a("Tb"), a("qt", 32, 64)), a("dd"), A.mult)
    chain[0] = "tables"
    for q in range(2 * N):
        o, x = a("T%d" % (1 + (q & 1)), 512 * (q >> 1), 512 * (q >> 1) + 512), a("Tb" if q & 1 else "Ta")
        if q < T2_ON_SCALAR:
            act(o, x, F.Copy, scale=a("off", q >> 1, (q >> 1) + 1))
        else:
            ts(o, x, a("off", q >> 1, (q >> 1) + 1), A.mult)
    chain[0] = None

    colf(32, a("nn"), "n2")
    for k in range(2):
        cp(a("ln", k, 32, 2), a("nn", 16 * k, 16 * k + 16))
    cp(a("SN"), ind(a("SL"), a("ln")))
    act(a("NW"), ind(a("nw"), a("ln")), F.Copy)
    ts(a("DG"), a("i16"), col(3), A.is_equal)
    scan(a("kq"), a("one", 0, 64), a("kc"), 0.0, A.mult, A.add)
    act(a("S256"), a("nix"), F.Copy, scale=1.0 / 4096)
    act(a("less"), a("nix"), F.Identity, bias=-1.0 / 16, scale=0.0)
    act(a("d12"), a("d12"), F.Identity, bias=col(3))
    for k, dl in enumerate(SIGN_ON_VECTOR or (16,)):
        ts(col(18), col(3), float(dl), A.not_equal, col(18) if k else 16.0, A.mult)
    act(a("c16"), a("zz", 0, 320), F.Identity, bias=col(18))

    def forty(name, rd, ds):
        w = 42 if name == "RS" else 40
        return a(name, w * (N * rd + ds[0]), w * (N * rd + ds[-1]) + 40)

    def requests(rd):
        W, sg = "W%d" % (rd & 1), "sg%d" % (rd & 1)
        for k in range(len(EARLY)):
            chain[0] = chain[0] if EARLY[k] else None
        if rd:
            cp(a("G1"), ind(a("T1"), a("rq")))
            chain[0] = None
            if ZFIRST == 1:
                act(a("z"), ind(a("T1"), a("rq")), F.Relu, bias=1.0)
            if ZFIRST == 2:
                act(a(sg), ind(a("T1"), a("rq")), F.Sign)
            act(a("G2"), ind(a("T2"), a("rq")), F.Copy)
        if ZFIRST == 0 or (ZFIRST == 2 and not rd):
            act(a(sg), a("G1"), F.Sign)
        if ZFIRST != 1 or not rd:
            act(a("z"), a("G1"), F.Relu, bias=1.0)
        scan(a("cum", 1, 513), a("G1"), a("c641"), 1023.0, A.add, A.max)
        if ZFIRST == 1:
            tt(a("mm"), a("cum", 0, 512), a("z"), A.mult)
            pick(a("PM", 0, 32), "Bl", "cum", 0, 512, True, False)
            pick(a("PM", 0, 32), "Bf", "mm", 0, 512, False, True)
        else:
            tt(a("mm"), a("cum", 0, 512), a(sg), A.mult)
            pick(a("PM", 0, 32), "Bf", "mm", 0, 512)
        scan(a("Ff", 1, 513), a("z"), a("G2"), 0.0, A.mult, A.add)
        if ZFIRST == 1:
            act(a(sg), a("z"), F.Identity, bias=-1.0)
        if QP_V:
            if rd:
                cp(a("n2", 0, 32), a("rq"))
                ts(a("s2", 0, 32), a("n2", 0, 32), 9, A.arith_shift_right)
            ts(a("qp"), a("s2", 0, 32), float(BL), A.mult, 1023.0, A.add)
            act(a("qo"), a("qp"), F.Identity, bias=15.0 - 1023.0 * C / BL, scale=C / BL)
        else:
            pick(a("Z1", 128, 160), "Bq", "G1", 0, 512)
            act(a("qp"), a("Z1", 128, 160), F.Identity, bias=1023.0, scale=float(BL))
            act(a("qo"), a("Z1", 128, 160), F.Copy, scale=float(C))
        tt(a("D"), a("Ff", 1, 513), a("Ff", 0, 512), A.subtract)
        tt(a("o2"), a("PM", 0, 32), a("qp"), A.add)
        ts(a("o1"), a("PM", 0, 32), C - 1023.5, A.is_gt, 8192.0, A.mult)
        tt(a("o1"), a("o1"), a("o2"), A.add)
        tt(a("o2"), a("o1"), a("dump"), A.min)
        cp(a("of"), a("o2"))
        tt(ind(a(W), a("of")), a("D"), a("G1"), A.add)
        for k, ds in enumerate(BATCH):
            bank, lo, hi = "PX%d" % (k % 3), 42 * ds[0], 42 * (ds[-1] + 1)
            pick(a(bank, 0, hi - lo), "BA", W, BL * ds[0], BL * (ds[-1] + 1))
            scan(a("Y", 1 + lo, 1 + hi), a("R40", 0, hi - lo), a(bank, 0, hi - lo), 0.0, A.mult, A.add)
            hi -= 2
            mm(a(bank, 256, 256 + hi - lo), [(a("TRI"), a("Y", 1 + lo, 1 + hi)), (a("UP"), a("Y", lo, hi))])
            tt(a("vi", lo, hi), a(bank, 256, 256 + hi - lo), a("sli", 0, hi - lo), A.add)
            ts(a("va", lo, hi), a("vi", lo, hi), 2 * HP - 1, A.bitwise_and)
            cp(forty("RS", rd, ds), a("va", lo, hi))
            for j, to in enumerate(GROUPS):
                if to[0] in ds:
                    send(to, 1, lambda dl: ap(forty("RS", rd, [dl])), lambda dl: ap(forty("RI", rd, [dl])), "q%d_%d" % (rd, j),
                         forty("RS", rd, to), forty("RI", rd, to), 16 * len(to) * ROW)

    def ends(rd):
        act(a("pc1"), a("PM", 0, 32), F.Identity, bias=1023.0)
        for k in range(2):
            mm(a("PM", 64 + 16 * k, 80 + 16 * k), [(a("BQ" if k else "BP", 12 - 4 * q, 140 - 4 * q), a("cum", 8 + 8 * q, 513, 32)) for q in range(4)])
        pick(a("PM", 96, 128), "Bl", "G1", 0, 512)
        ts(a("E"), a("PM", 64, 96), -1.0, A.mult, 1023.0, A.add)
        tt(a("b3", 0, 32), a("PM", 96, 128), a("pc1"), A.add)
        ts(a("en"), a("b3", 0, 32), float(C), A.min)
        cp(a("eu"), a("en"))
        tt(a("kl"), a("pc1"), a("en"), A.subtract)
        tt(a("en"), a("en"), a("qo"), A.add)

    def ahead(rd):
        act(a("NWc"), ind(a("NW"), a("sl")), F.Copy)
        if rd + 1 < RO:
            act(a("SNo"), ind(a("SN"), a("sl")), F.Copy)
            squeeze(a("PX1", 0, 16), "SNo", 0, 64, 4)
            cp(a("sq"), a("PX1", 0, 16))
            act(a("t1"), ind(a("RL"), a("sq")), F.Copy)
            for k in range(2):
                mm(a("PX0", 64 * k, 64 * k + 64), [(a("DH", 128 * d, 128 * d + 128), a("t1", 2 * k + d, 256, 4)) for d in range(2)])

    def answer(rd, ds):
        for dl in ds:
            src = ind(a("HW"), forty("RS" if dl == SELF else "RI", rd, [dl]))
            if dl in HEAP_ON_VECTOR:
                cp(a("Hg", C * dl, C * dl + C), src)
            else:
                act(a("Hg", C * dl, C * dl + C), src, F.Copy)
        bank = a("PH%d" % (ANSWERS.index(ds) & 1), 0, 40 * len(ds))
        pick(bank, "BA", "Hg", C * ds[0], C * (ds[-1] + 1))
        if ds == [SELF]:
            return cp(forty("PI", rd, ds), bank)
        cp(forty("PS", rd, ds), bank)
        send(ds, -1, lambda dl: ap(forty("PS", rd, [dl])), lambda dl: ap(forty("PI", rd, [dl])), "a%d_%d" % (rd, ds[0]),
             forty("PS", rd, ds), forty("PI", rd, ds), 16 * len(ds) * ROW)

    def phrases(rd, dl, slot, first, last):
        w = 320 if dl in IN_HALVES else C
        for u in range(0, C, w):
            lo, x0, at = C * slot + u, 648 * slot + u, forty("PI", rd, [dl])[1] + u // 16
            src = ind(a("B", 0, ODD + V + 1), a("PI", at, at + w // 16))
            act(a("Ab", x0 + 1, x0 + 1 + w), src, F.Abs, bias=0.5)
            ct = a("ct", C * dl + u, C * dl + u + w)
            tt(ct, src, a("Ab", x0, x0 + w), A.is_equal)
            if dl in SIGN_ON_VECTOR:
                ts(a("d", lo, lo + w), a("Ab", x0 + 1, x0 + 1 + w), 0.25, A.is_gt, 2.0, A.mult)
            else:
                act(a("d", lo, lo + w), a("Ab", x0 + 1, x0 + 1 + w), F.Sign, bias=-0.25)
            scan(a("r", lo, lo + w), ct, ct, a("r", lo - 1, lo) if u else 0.0, A.mult, A.add)
        lo = C * slot
        for k in range(2):
            mm(a("Z%d" % k, 0, 320), [(band("BA", dl), a("d", lo + 320 * k, lo + 320 * k + 320))], first, False)
        for k in range(2):
            mm(a("Z%d" % k, 0, 320), [(band("B4", dl), a("r", lo + 320 * k, lo + 320 * k + 320))], False, last)

    def winner(rd):
        mm(a("PM", 128, 192), [(a("SO", 0, 128), a("kq"))], True, False)
        scan(a("cs", 1, 321), a("c16"), a("Z0", 0, 320), 0.0, A.add, A.add)
        scan(a("cs", 321, 641), a("c16"), a("Z1", 0, 320), a("cs", 320, 321), A.add, A.add)
        tt(a("g1", 0, 256), ind(a("cs", 0, 641), a("E", 0, 16)), a("OM"), A.mult)
        act(a("g1", 256, 512), ind(a("cs", 0, 641), a("E", 16, 32)), F.Copy)
        scan(a("g2"), a("R4"), a("g1", 0, 256), 0.0, A.mult, A.add)
        mm(a("PM", 128, 192), [(a("SO", 128 * o, 128 * o + 128), a("g1", 256 + o, 512, 4)) for o in range(4)], False, False)
        mm(a("PM", 128, 192), [(a("SO", 512, 640), a("g2", 3, 256, 4))], False, True)
        cp(a("Fs", 1, 65), a("PM", 128, 192))
        tt(a("key"), a("PM", 128, 192), a("Fs", 0, 64), A.subtract)
        scan(a("mx", 1, 65), a("R4", 0, 64), a("key"), 0.0, A.mult, A.max)
        tt(a("oh"), ind(a("mx"), a("l4")), a("key"), A.is_equal)
        if rd + 1 < RO:
            for k in range(2):
                tt(a("u2", 64 * k, 64 * k + 64), a("PX0", 64 * k, 64 * k + 64), a("oh"), A.mult)
                scan(a("u3", 64 * k, 64 * k + 64), a("R4", 0, 64, 1), a("u2", 64 * k, 64 * k + 64), 0.0, A.mult, A.add)
                cp(a("rq", k, 32, 2), a("u3", 64 * k + 3, 64 * k + 64, 4))

    def results(rd):
        shown(rd)
        for k in range(4):
            act(a("YT", 64 * rd + k, 64 * rd + 64, 4), a("key", k, 64, 4), F.Identity, bias=(k - 3) / 4, scale=0.25)
        w = 128 if rd + 1 < RO else 64
        tt(a("t2", 0, 64), a("NWc"), a("oh"), A.mult)
        if rd + 1 < RO:
            tt(a("t2", 64, 128), a("SNo"), a("oh"), A.mult)
        scan(a("t3", 0, w), a("R4", 0, w), a("t2", 0, w), 0.0, A.mult, A.add)
        act(a("YW", 16 * rd, 16 * rd + 16), a("t3", 3, 64, 4), F.Copy)
        if rd + 1 < RO:
            squeeze(a("PX1", 96, 100), "t3", 67, 128, 4, 4)
            cp(a("sl"), a("PX1", 96, 100))

    def distances(rd):
        for dl in [SELF] + peers:
            for k in range(2):
                mm(a("PH%d" % k, 0, 320), [(band("BA", 8 + dl), a("ct", C * dl + 320 * k, C * dl + 320 * k + 320))], dl == SELF, dl == peers[-1])
        for k in range(2):
            act(a("y", 320 * k, 320 * k + 320), a("PH%d" % k, 0, 320), F.Relu, bias=9216.0, scale=-1024.0)
        scan(a("DB", 1, 641), a("one"), a("y"), 0.0, A.add, A.min)
        if DD_S:
            act(a("du"), ind(a("DB", 0, 641), a("eu")), F.Copy)
            tt(a("dd"), a("du"), a("sg%d" % (rd & 1)), A.mult)
        else:
            tt(a("dd"), ind(a("DB", 0, 641), a("eu")), a("sg%d" % (rd & 1)), A.mult)

    def barrier_words(rd):
        pick(a("Z0", 0, 32), "Bh", "dd", 0, 512)
        squeeze(a("Z1", 64, 96), "oh", 0, 64, 2)
        tt(a("b1"), a("Z0", 0, 32), a("kl"), A.is_gt)
        tt(a("b2"), a("Z0", 0, 32), a("en"), A.add)
        tt(a("bi", 0, 32), a("b1"), a("b2"), A.mult)
        ts(a("bi", 32, 64), a("bi", 0, 32), 15, A.bitwise_and)
        ts(a("bi", 64, 96), a("bi", 0, 32), 4, A.arith_shift_right)
        for k in range(2):
            tt(a("bh", 32 * k, 32 * k + 32), a("bi", 32 * k + 32, 32 * k + 64), a("Z1", 64, 96), A.mult)
        cp(a("WF", 1, 321), forty("PI", rd, [0, N - 1]))
        mm(a("Z1", 32, 48), [(a("BK", 8 - 8 * (k >> 1), 136 - 8 * (k >> 1)), a("bh", k, 64, 4)) for k in range(4)])
        cp(a("bu"), a("Z1", 32, 48))
        act(a("Mk"), ind(a("DG", 0, 16), a("bu", 0, 8)), F.Copy)
        tt(a("Wd"), ind(a("WF", 0, 321), a("bu", 8, 16)), a("Mk"), A.mult)
        mm(a("Z0", 256, 384), [(a("SG"), a("S256" if rd + 1 < RO else "less"))], True, False)
        mm(a("Z0", 256, 384), [(a("SG"), a("Wd"))], False, True)
        ts(a("x2"), a("Z0", 256, 384), ODD - 0.25, A.is_gt, -float(ODD), A.mult)
        tt(a("K") if rd + 1 < RO else a("YB", 128 * rd, 128 * rd + 128), a("Z0", 256, 384), a("x2"), A.add)

    def shown(rd):
        if rd + 1 < RO:
            act(a("x3"), a("K"), F.Identity, bias=WHOLE - 1.0)
            act(a("YB", 128 * rd, 128 * rd + 128), a("x3"), F.Identity, bias=-WHOLE)

    def barriers():
        tt(a("k2", 0, 128), a("K"), a("DG"), A.mult)
        scan(a("k2", 128, 256), a("R16"), a("k2", 0, 128), 0.0, A.mult, A.add)
        act(a("nb"), a("k2", 143, 256, 16), F.Identity, bias=64.0, scale=-256.0)
        for c in range(8):
            if c < REPEATS_ON_VECTOR:
                x = a("x3", 64 * (c & 1), 64 * (c & 1) + 16 * c + 16)
                ts(x, a("K", 0, 16 * c + 16), a("k2", 143 + 16 * c, 144 + 16 * c), A.subtract, 0.25, A.add)
                least(a("fi", c, c + 1), x)
                continue
            x = a("x1", 128 * (c & 1), 128 * (c & 1) + 16 * c + 16)
            act(x, a("K", 0, 16 * c + 16), F.Abs, bias=a("nb", c, c + 1), scale=256.0)
            act(x, x, F.Relu, bias=64.0 * 8192, scale=-8192.0, total=a("acc", c, c + 1))
        if REPEATS_ON_VECTOR:
            ts(a("acc", 0, REPEATS_ON_VECTOR), a("fi", 0, REPEATS_ON_VECTOR), 0.25, A.is_lt, 8192.0, A.mult)
        act(a("own"), a("k2", 143, 256, 16), F.Identity, bias=float(ODD))
        last["repeats"] = len(nodes) - 2 - (REPEATS_ON_VECTOR > 0)
        tt(a("k3", 0, 8), a("acc"), a("k2", 143, 256, 16), A.add)
        tt(a("k3", 8, 16), a("acc"), a("own"), A.add)
        tt(a("k4"), a("k3"), a("d12"), A.min)
        cp(a("ku"), a("k4"))
        if MARK_ON_SCALAR:
            add("s", lambda: g.scalar.activation(ap(ind(a("B"), a("ku"))), ap(a("neg")), F.Tanh), [a("neg")], [ind(a("B"), a("ku"))], 256 * SC * CY + FIX)
        else:
            cp(ind(a("B"), a("ku")), a("neg"))

    slot = 0
    for rd in range(RO):
        if rd + 1 < RO:
            for lo in range(0, N * BL, 896):
                dma("y", a("W%d" % (~rd & 1), lo, lo + 896), a("zz", 0, 896), 1792, reads=[a("cs", 1) if rd else a("Tb")])
        requests(rd)
        if rd:
            barrier_words(rd - 1)
            barriers()
        chain[0] = "answer"
        for k, ds in enumerate(ANSWERS):
            hush[0] = last["repeats"] if rd and k >= HUSH else None
            answer(rd, ds)
            hush[0] = None
            if k == GATE:
                wait_for = last["v", "answer"]
        chain[0], gate[0] = None, wait_for
        if rd:
            results(rd - 1)
        ends(rd)
        ahead(rd)
        chain[0], gate[0] = "phrases", None
        for dl in [SELF] + peers:
            phrases(rd, dl, slot % RING, dl == SELF, dl == peers[-1])
            slot += 1
        chain[0] = None
        winner(rd)
        chain[0] = "first%d" % rd
        distances(rd)
    chain[0] = None
    barrier_words(RO - 1)
    results(RO - 1)
    dma("y", T.yb[:], a("YB", ps=row0), 1536, 8)
    dma("s", T.yt[:], a("YT", ps=row0), 768, 8)
    dma("y", T.yw[:], a("YW", ps=row0), 192, 8)
    issue()
